import numpy as np
import ml_dtypes


def mxq(x, axis, fmt="e4m3"):
    dtype, down = {"e4m3": (ml_dtypes.float8_e4m3fn, 7), "e5m2": (ml_dtypes.float8_e5m2, 14)}[fmt]
    v = np.moveaxis(np.asarray(x, np.float32).astype(ml_dtypes.bfloat16).astype(np.float64), axis, -1)
    blocks = v.reshape(v.shape[:-1] + (-1, 32))
    amax = np.abs(blocks).max(-1, keepdims=True)
    byte = np.maximum(np.where(amax > 0, np.frexp(amax)[1] - 1 + 127, 0) - down, 1)
    scale = np.exp2(byte - 127.0)
    codes = (blocks / scale).astype(np.float32).astype(dtype).astype(np.float64)
    return np.moveaxis((codes * scale).reshape(v.shape), -1, axis)


WIDE = False


def mx_kscale(k):
    if not WIDE:
        return np.ones(k)
    levels = np.array([10, -10, 5, -5, 0])
    if k % 512:
        return np.exp2(np.random.permutation(np.resize(levels, k // 32))).repeat(32)
    a = np.empty((k // 512, 16))
    for p in range(k // 512):
        a[p, :8] = np.random.permutation(np.resize(levels, 8))
        for g in range(8):
            far = levels[np.abs(levels - a[p, g]) >= 10]
            a[p, g + 8] = far[np.random.randint(len(far))]
    return np.exp2(a.ravel()).repeat(32)


def f64(x):
    return np.asarray(x).astype(np.float64)


def striped(idx):
    return np.tile(idx.reshape(-1, 16).T, (8, 1)).astype(np.uint16)


def unstriped(offs):
    return offs[:16].T.reshape(-1).astype(np.int64)


E2M1 = np.array([0.0, 0.5, 1.0, 1.5, 2.0, 3.0, 4.0, 6.0, -0.0, -0.5, -1.0, -1.5, -2.0, -3.0, -4.0, -6.0])


def pack_weight(w, fmt):
    k, n = w.shape
    w = f64(np.asarray(w, np.float32).astype(ml_dtypes.bfloat16)).reshape(k // 32, 32, n)
    amax = np.abs(w).max(1)
    if fmt == "e4m3":
        byte = np.frexp(amax)[1] - 1 + 127 - 7
    else:
        mant, ex = np.frexp(amax / 6.0)
        byte = np.where(mant > 0.5, ex, ex - 1) + 127
    byte = np.clip(np.where(amax > 0, byte, 1), 1, 254)
    scaled = (w * np.exp2(127.0 - byte)[:, None, :]).reshape(k, n).astype(np.float32)
    by_word = np.ascontiguousarray(scaled.reshape(k // 512, 128, 4, n).transpose(0, 1, 3, 2))
    if fmt == "e4m3":
        words = by_word.astype(ml_dtypes.float8_e4m3fn).view(np.uint8)
    else:
        c = by_word.astype(ml_dtypes.float4_e2m1fn).view(np.uint8) & 0xF
        words = (c[..., 0::2] | (c[..., 1::2] << 4)).reshape(k // 512, 128, 2 * n)
    return np.ascontiguousarray(words), np.ascontiguousarray(byte.astype(np.uint8).reshape(k // 512, 16, n))


def unpack_weight(words, scales, fmt):
    g, _, n = scales.shape
    words = np.ascontiguousarray(words).reshape(g, 128, n, -1)
    if fmt == "e4m3":
        vals = words.view(ml_dtypes.float8_e4m3fn).astype(np.float64)
    else:
        nib = np.empty((g, 128, n, 4), np.uint8)
        nib[..., 0::2] = words & 0xF
        nib[..., 1::2] = words >> 4
        vals = E2M1[nib]
    vals = vals * np.repeat(np.exp2(scales.astype(np.float64) - 127.0), 8, axis=1)[..., None]
    return vals.transpose(0, 1, 3, 2).reshape(g * 512, n)


def sigmoid(v):
    return 1.0 / (1.0 + np.exp(-np.maximum(v, -700.0)))


K, T, E, C, H, N = 1024, 640, 5, 256, 512, 384


def by_expert(wq, xq):
    return np.concatenate([wq[e].T @ xq[:, e * C:(e + 1) * C] for e in range(E)], axis=1)


def setup_inputs():
    n = np.random.standard_normal
    s = mx_kscale(K)[:, None]
    u = mx_kscale(H)
    first = np.random.permutation(np.repeat(np.arange(E), T // E))
    second = (first + 1 + np.random.permutation(np.repeat(np.arange(E - 1), -(-T // (E - 1)))[:T])) % E
    while np.bincount(second, minlength=E).max() != T // E:
        load = np.bincount(second, minlength=E); hi, lo = int(load.argmax()), int(load.argmin())
        t = np.flatnonzero((second == hi) & (first != lo))[0]; second[t] = lo
    slot_token = np.empty(E * C, np.int64); pos = np.empty((2, T), np.int64); fill = np.zeros(E, np.int64)
    place = np.stack([np.random.permutation(C) for _ in range(E)])
    for r, deal in enumerate((first, second)):
        for t in np.random.permutation(T):
            e = deal[t]; j = e * C + place[e, fill[e]]; fill[e] += 1; slot_token[j] = t; pos[r, t] = j
    g = np.random.uniform(0.2, 0.8, T)
    x = pack_weight(n((K, T)) * s, "e4m3")
    return {
        "x_words": x[0],
        "x_scales": x[1],
        "w1": (n((E, K, H)) / np.sqrt(K) / s[None]).astype(np.float32),
        "w3": (n((E, K, H)) / np.sqrt(K) / s[None] * u[None, None, :]).astype(np.float32),
        "w2": (n((E, H, N)) / np.sqrt(H) / u[None, :, None]).astype(np.float32),
        "gate": np.stack([np.tile(g, (N, 1)), np.tile(1.0 - g, (N, 1))]).astype(np.float32),
        "offs": striped(slot_token),
        "pos1": striped(pos[0]),
        "pos2": striped(pos[1]),
    }


def reference(x_words, x_scales, w1, w3, w2, gate, offs, pos1, pos2):
    idx = unstriped(offs)
    xq = unpack_weight(x_words, x_scales, "e4m3")[:, idx]
    h = sigmoid(by_expert(mxq(f64(w1), 1, "e4m3"), xq))
    h = h * by_expert(mxq(f64(w3), 1, "e4m3"), xq)
    y = by_expert(mxq(f64(w2), 1, "e4m3"), mxq(h, 0, "e4m3"))
    return f64(gate[0]) * y[:, unstriped(pos1)] + f64(gate[1]) * y[:, unstriped(pos2)]

@@ -1,0 +1,238 @@
+from contextlib import ExitStack
+
+import concourse.mybir as mybir
+
+K, T, E, C, H, N = 1024, 640, 5, 256, 512, 384
+S = E * C
+FLOPS = 2 * S * (2 * K * H + H * N)
+
+F32 = mybir.dt.float32
+BF16 = mybir.dt.bfloat16
+I32 = mybir.dt.int32
+U32 = mybir.dt.uint32
+U16 = mybir.dt.uint16
+U8 = mybir.dt.uint8
+FP8X4 = mybir.dt.float8_e4m3fn_x4
+MULT = mybir.AluOpType.mult
+ADD = mybir.AluOpType.add
+SIGMOID = mybir.ActivationFunctionType.Sigmoid
+
+P = 128
+PACK = 4
+K_PASS = P * PACK
+PASSES = K // K_PASS
+HALF = 128
+N_TILES = N // P
+STREAM_BUFS = 13
+GROUPED_BUFS = 12
+EXPERT_GROUPS = ((0, E - 1), (E - 1, E))
+M_VECTOR = 48
+M_VECTOR_LAST = 84
+
+
+def tile_moe_pkd_glu_sigmoid_kernel(
+    tc, x_words, x_scales, w1, w3, w2, gate, offs, pos1, pos2, out
+):
+    nc = tc.nc
+    with ExitStack() as ctx:
+        keep = ctx.enter_context(tc.tile_pool(name="keep", bufs=1))
+        rings = ctx.enter_context(tc.tile_pool(name="rings", bufs=1))
+        psum = ctx.enter_context(tc.psum_pool(name="psum", bufs=1))
+        turns = {}
+
+        def ring_tile(pool, ring, depth, shape, dtype):
+            turn = turns.get(ring, 0)
+            turns[ring] = turn + 1
+            tag = "%s%d" % (ring, turn % depth)
+            if ring == "bank":
+                return pool.tile(shape, dtype, name=ring, tag=tag)
+            return pool.tile(shape, dtype, name=ring, tag=tag, align_bytes=64)
+
+        def stream_tile(shape):
+            return ring_tile(rings, "stream", STREAM_BUFS, shape, F32)
+
+        def bank_tile():
+            return ring_tile(psum, "bank", 8, [P, 512], F32)
+
+        slot_list = keep.tile([P, S // 16], U16, name="slot_list")
+        nc.sync.dma_start(slot_list[:], offs)
+        token_scales = keep.tile([P, T // 4], I32, name="token_scales", align_bytes=64)
+        nc.vector.memset(token_scales[:], 0)
+        token_words = []
+        for a in range(PASSES):
+            words = keep.tile([P, T], I32, name="token_words%d" % a, align_bytes=64)
+            nc.sync.dma_start(words[:], x_words[a].rearrange("p t r -> p (t r)").bitcast(I32))
+            token_words.append(words)
+        for q in range(4):
+            nc.scalar.dma_start(
+                token_scales[32 * q : 32 * q + 4 * PASSES, :], x_scales[:, 4 * q : 4 * q + 4, :].bitcast(I32)
+            )
+
+        def gather_next(tag):
+            e, part = waiting[0]
+            waiting.remove((e, part))
+            offsets = slot_list[:, e * C // 16 : (e + 1) * C // 16]
+            if part < PASSES:
+                window, dtype = token_words[part][:].bitcast(U32), U32
+            else:
+                window, dtype = token_scales[:].bitcast(U8), U8
+            gathered = rings.tile([P, C], dtype, name="gathered", tag=tag, align_bytes=64)
+            nc.vector.tensor_copy(gathered[:], window.indirect(offsets))
+            tokens[e].append(gathered)
+
+        tokens = [[] for e in range(E)]
+        waiting = [(e, part) for e in range(E) for part in range(PASSES + 1)]
+        for part in range(PASSES + 1):
+            gather_next("first_tokens%d" % part)
+
+        def quantise_first_layer_pass(w, e, a, m_vector):
+            raw = stream_tile([P, PACK, H])
+            rows = w[e, a * K_PASS : (a + 1) * K_PASS, :]
+            nc.sync.dma_start(raw[:], rows.rearrange("(p j) c -> p j c", j=PACK))
+            grouped = ring_tile(rings, "grouped", GROUPED_BUFS, [P, PACK * H], BF16)
+            src = raw[:].rearrange("p j (m t) -> p m j t", t=PACK)
+            dst = grouped[:].rearrange("p (t m j) -> p m j t", t=PACK, j=PACK)
+            nc.vector.tensor_copy(dst[:, :m_vector], src[:, :m_vector])
+            nc.scalar.copy(dst[:, m_vector:], src[:, m_vector:])
+            w_codes = ring_tile(rings, "w_codes", 8, [P, H], U32)
+            w_scales = ring_tile(rings, "w_scales", 8, [P, H], U8)
+            nc.vector.quantize_mx(out=w_codes[:].bitcast(FP8X4), scales=w_scales[:], in_=grouped[:])
+            chunk = turns["grouped"] - 1
+            if waiting and (chunk == 0 or chunk % 4 != 0):
+                gather_next("grouped%d" % (chunk % GROUPED_BUFS))
+            return w_codes, w_scales, raw, grouped
+
+        def first_layer_product(weights, e, half):
+            words, slot_scales = tokens[e][:PASSES], tokens[e][PASSES]
+            slots = slice(half * HALF, (half + 1) * HALF)
+            bank = bank_tile()
+            for t in range(PACK):
+                cols = slice(t * P, (t + 1) * P)
+                for a in range(PASSES):
+                    nc.tensor.matmul_mx(
+                        out=bank[:, t * HALF : (t + 1) * HALF],
+                        lhsT=weights[a][0][:, cols].bitcast(FP8X4),
+                        lhsT_scale=weights[a][1][:, cols],
+                        rhs=words[a][:, slots].bitcast(FP8X4),
+                        rhs_scale=slot_scales[4 * a :, slots],
+                        start=(a == 0),
+                        stop=(a == PASSES - 1),
+                    )
+            return bank[:].rearrange("p (t s) -> p s t", t=PACK)
+
+        halves = range(C // HALF)
+        hidden = []
+
+        def finish_hidden(lin, sig, h_bf):
+            e = len(hidden)
+            h_codes = keep.tile([P, C], U32, name="h_codes%d" % e, align_bytes=64)
+            h_scales = keep.tile([P, C], U8, name="h_scales%d" % e, align_bytes=64)
+            width = HALF * PACK
+            for half in halves:
+                h_half = h_bf[:, half * width : (half + 1) * width].rearrange("p (s t) -> p s t", t=PACK)
+                nc.vector.tensor_tensor(h_half, lin[half], sig[half], MULT)
+            for half in halves:
+                slots = slice(half * HALF, (half + 1) * HALF)
+                nc.vector.quantize_mx(
+                    out=h_codes[:, slots].bitcast(FP8X4),
+                    scales=h_scales[:, slots],
+                    in_=h_bf[:, half * width : (half + 1) * width],
+                )
+            hidden.append((h_codes, h_scales))
+
+        pending = None
+        for e in range(E):
+            last = e == E - 1
+            q1 = [quantise_first_layer_pass(w1, e, 0, M_VECTOR)]
+            if pending is not None:
+                finish_hidden(pending[0], pending[1], q1[0][3])
+            q1.append(quantise_first_layer_pass(w1, e, 1, M_VECTOR))
+            pre = [first_layer_product(q1, e, half) for half in halves]
+            q3 = [quantise_first_layer_pass(w3, e, 0, M_VECTOR)]
+            q3.append(quantise_first_layer_pass(w3, e, 1, M_VECTOR_LAST if last else M_VECTOR))
+            sig = []
+            for half in halves:
+                spent = q3[half if last else PASSES - 1][2]
+                sig.append(spent[:, half].rearrange("p (s t) -> p s t", t=PACK))
+                nc.scalar.activation(sig[half], pre[half], SIGMOID)
+            lin = [first_layer_product(q3, e, half) for half in halves]
+            pending = (lin, sig)
+        first_list = keep.tile([P, T // 16], U16, name="first_list")
+        second_list = keep.tile([P, T // 16], U16, name="second_list")
+        nc.sync.dma_start(first_list[:], pos1)
+        nc.sync.dma_start(second_list[:], pos2)
+        h_last = ring_tile(rings, "h_last", 1, [P, C * PACK], BF16)
+        finish_hidden(pending[0], pending[1], h_last)
+
+        def load_w2(n):
+            most = stream_tile([P, E - 1, PACK * P])
+            rest = stream_tile([P, T])
+            raw = [most[:, e] for e in range(E - 1)] + [rest[:, : PACK * P]]
+            for e in range(E):
+                rows = w2[e, :, n * P : (n + 1) * P]
+                nc.sync.dma_start(
+                    raw[e].rearrange("p (j c) -> p j c", j=PACK), rows.rearrange("(p j) c -> p j c", j=PACK)
+                )
+            return raw, rest
+
+        def load_gate(r, n):
+            weights = stream_tile([P, T])
+            nc.sync.dma_start(weights[:], gate[r, n * P : (n + 1) * P, :])
+            return weights
+
+        def second_layer(n, raw):
+            grouped = ring_tile(rings, "grouped2", 2, [P, E, P * PACK], BF16)
+            for e in range(E):
+                dst = grouped[:, e].rearrange("p (c i j) -> p c j i", i=4, j=PACK)
+                src = raw[e].rearrange("p (j c i) -> p c j i", i=4, j=PACK)
+                if n == 0 and e < 2:
+                    nc.vector.tensor_copy(dst, src)
+                else:
+                    nc.scalar.copy(dst, src)
+            w_codes = ring_tile(rings, "w2_codes", 2, [P, E * P], U32)
+            w_scales = ring_tile(rings, "w2_scales", 2, [P, E * P], U8)
+            for e0, e1 in EXPERT_GROUPS:
+                nc.vector.quantize_mx(
+                    out=w_codes[:, e0 * P : e1 * P].bitcast(FP8X4),
+                    scales=w_scales[:, e0 * P : e1 * P],
+                    in_=grouped[:, e0:e1].rearrange("p e x -> p (e x)"),
+                )
+            y = keep.tile([P, S], F32, name="y%d" % n)
+            for e0 in range(0, E, 2):
+                pair = range(e0, min(e0 + 2, E))
+                bank = bank_tile()
+                for e in pair:
+                    nc.tensor.matmul_mx(
+                        out=bank[:, (e - e0) * C : (e - e0 + 1) * C],
+                        lhsT=w_codes[:, e * P : (e + 1) * P].bitcast(FP8X4),
+                        lhsT_scale=w_scales[:, e * P : (e + 1) * P],
+                        rhs=hidden[e][0][:].bitcast(FP8X4),
+                        rhs_scale=hidden[e][1][:],
+                        start=True,
+                        stop=True,
+                    )
+                width = len(pair) * C
+                nc.scalar.copy(y[:, e0 * C : e0 * C + width], bank[:, :width])
+            return y
+
+        w2_raw = [load_w2(0)]
+        gates = {}
+        for n in range(N_TILES):
+            gates[0, n] = load_gate(0, n)
+            if n + 1 < N_TILES:
+                w2_raw.append(load_w2(n + 1))
+            gates[1, n] = load_gate(1, n)
+        y = second_layer(0, w2_raw[0][0])
+        for n in range(N_TILES):
+            first = ring_tile(rings, "first", 2, [P, T], F32)
+            nc.vector.tensor_tensor(first[:], y[:].indirect(first_list[:]), gates[0, n][:], MULT)
+            if n + 1 < N_TILES:
+                y_next = second_layer(n + 1, w2_raw[n + 1][0])
+                second = w2_raw[n + 1][1]
+            else:
+                second = ring_tile(rings, "second", 1, [P, T], F32)
+            nc.vector.tensor_tensor(second[:], y[:].indirect(second_list[:]), gates[1, n][:], MULT)
+            total = ring_tile(rings, "total", 2, [P, T], F32)
+            nc.vector.tensor_tensor(total[:], first[:], second[:], ADD)
+            nc.sync.dma_start(out[n * P : (n + 1) * P, :], total[:])
+            y = y_next

@@ -23,11 +23,28 @@ K_PASS = P * PACK
 PASSES = K // K_PASS
 HALF = 128
 N_TILES = N // P
+UPFRONT = 6
+GATHER_AFTER = (2, 5, 6, 7, 9, 10, 13, 14, 15)
+V_HALVES = (1, 2, 0, 0, 1, 2, 0, 0, 1, 2, 0, 0, 1, 2, 0, 0, 2, 1, 0, 1)
+SIG_AFTER = (3, 3)
+SIG_AFTER_LAST = (3, 3)
+MULT_AFTER = 0
+QH_SPLIT = (2, 2, 1, 2, 2)
+W2_ON_V = ((0, 1), (0, 3), (1, 1), (1, 2), (1, 4), (2, 4))
+WARM = True
+A_COUNT = (2, 4, 3)
+Y_TIE = (False, True)
+Q_GROUPS = (((0, 2), (2, 3), (3, 4), (4, 5)), ((0, 2), (2, 3), (3, 4), (4, 5)), ((0, 1), (1, 2), (2, 3), (3, 4), (4, 5)))
+COPY_GROUPS = (((0, 2), (2, 4), (4, 5)),) * 3
+LAST_Y_HALVES = True
+SPLIT_LAST = False
+FINAL_PARTS = 2
+EARLY_Y0 = True
+GATE_ORDER = 1
+SECOND_TIE = (False, False)
 STREAM_BUFS = 13
 GROUPED_BUFS = 12
 EXPERT_GROUPS = ((0, E - 1), (E - 1, E))
-M_VECTOR = 48
-M_VECTOR_LAST = 84
 
 
 def tile_moe_pkd_glu_sigmoid_kernel(
@@ -82,23 +99,36 @@ def tile_moe_pkd_glu_sigmoid_kernel(
 
         tokens = [[] for e in range(E)]
         waiting = [(e, part) for e in range(E) for part in range(PASSES + 1)]
-        for part in range(PASSES + 1):
+        for part in range(UPFRONT):
             gather_next("first_tokens%d" % part)
+        if WARM:
+            warm = keep.tile([P, 8], F32, name="warm")
+            nc.vector.memset(warm[:], 0.0)
+            nc.scalar.activation(warm[:], warm[:], SIGMOID)
 
-        def quantise_first_layer_pass(w, e, a, m_vector):
+        def quantise_first_layer_pass(w, e, a):
             raw = stream_tile([P, PACK, H])
             rows = w[e, a * K_PASS : (a + 1) * K_PASS, :]
-            nc.sync.dma_start(raw[:], rows.rearrange("(p j) c -> p j c", j=PACK))
             grouped = ring_tile(rings, "grouped", GROUPED_BUFS, [P, PACK * H], BF16)
+            parts = 2 if SPLIT_LAST and turns["grouped"] == 4 * E else 1
+            for part in range(parts):
+                cols = slice(part * H // parts, (part + 1) * H // parts)
+                nc.sync.dma_start(raw[:, :, cols], rows.rearrange("(p j) c -> p j c", j=PACK)[:, :, cols])
             src = raw[:].rearrange("p j (m t) -> p m j t", t=PACK)
             dst = grouped[:].rearrange("p (t m j) -> p m j t", t=PACK, j=PACK)
-            nc.vector.tensor_copy(dst[:, :m_vector], src[:, :m_vector])
-            nc.scalar.copy(dst[:, m_vector:], src[:, m_vector:])
+            chunk = turns["grouped"] - 1
+            for part in range(parts):
+                ms = slice(part * P // parts, (part + 1) * P // parts)
+                for pair in range(2):
+                    planes = slice(2 * pair, 2 * pair + 2)
+                    if pair < V_HALVES[chunk]:
+                        nc.vector.tensor_copy(dst[:, ms, :, planes], src[:, ms, :, planes])
+                    else:
+                        nc.scalar.copy(dst[:, ms, :, planes], src[:, ms, :, planes])
             w_codes = ring_tile(rings, "w_codes", 8, [P, H], U32)
             w_scales = ring_tile(rings, "w_scales", 8, [P, H], U8)
             nc.vector.quantize_mx(out=w_codes[:].bitcast(FP8X4), scales=w_scales[:], in_=grouped[:])
-            chunk = turns["grouped"] - 1
-            if waiting and (chunk == 0 or chunk % 4 != 0):
+            if chunk in GATHER_AFTER:
                 gather_next("grouped%d" % (chunk % GROUPED_BUFS))
             return w_codes, w_scales, raw, grouped
 
@@ -131,108 +161,157 @@ def tile_moe_pkd_glu_sigmoid_kernel(
             for half in halves:
                 h_half = h_bf[:, half * width : (half + 1) * width].rearrange("p (s t) -> p s t", t=PACK)
                 nc.vector.tensor_tensor(h_half, lin[half], sig[half], MULT)
-            for half in halves:
-                slots = slice(half * HALF, (half + 1) * HALF)
+            step = C // QH_SPLIT[e]
+            for s0 in range(0, C, step):
                 nc.vector.quantize_mx(
-                    out=h_codes[:, slots].bitcast(FP8X4),
-                    scales=h_scales[:, slots],
-                    in_=h_bf[:, half * width : (half + 1) * width],
+                    out=h_codes[:, s0 : s0 + step].bitcast(FP8X4),
+                    scales=h_scales[:, s0 : s0 + step],
+                    in_=h_bf[:, s0 * PACK : (s0 + step) * PACK],
                 )
             hidden.append((h_codes, h_scales))
 
-        pending = None
-        for e in range(E):
-            last = e == E - 1
-            q1 = [quantise_first_layer_pass(w1, e, 0, M_VECTOR)]
-            if pending is not None:
-                finish_hidden(pending[0], pending[1], q1[0][3])
-            q1.append(quantise_first_layer_pass(w1, e, 1, M_VECTOR))
-            pre = [first_layer_product(q1, e, half) for half in halves]
-            q3 = [quantise_first_layer_pass(w3, e, 0, M_VECTOR)]
-            q3.append(quantise_first_layer_pass(w3, e, 1, M_VECTOR_LAST if last else M_VECTOR))
-            sig = []
-            for half in halves:
-                spent = q3[half if last else PASSES - 1][2]
-                sig.append(spent[:, half].rearrange("p (s t) -> p s t", t=PACK))
-                nc.scalar.activation(sig[half], pre[half], SIGMOID)
-            lin = [first_layer_product(q3, e, half) for half in halves]
-            pending = (lin, sig)
         first_list = keep.tile([P, T // 16], U16, name="first_list")
         second_list = keep.tile([P, T // 16], U16, name="second_list")
-        nc.sync.dma_start(first_list[:], pos1)
-        nc.sync.dma_start(second_list[:], pos2)
-        h_last = ring_tile(rings, "h_last", 1, [P, C * PACK], BF16)
-        finish_hidden(pending[0], pending[1], h_last)
+        pending = None
+        for e in range(E):
+            chunks = []
+            sig = [None, None]
+            for c in range(4):
+                chunks.append(quantise_first_layer_pass(w1 if c < 2 else w3, e, c % 2))
+                if pending is not None and c == MULT_AFTER:
+                    finish_hidden(pending[0], pending[1], chunks[c][3])
+                if c == 1 and e == 0:
+                    nc.sync.dma_start(first_list[:], pos1)
+                    nc.sync.dma_start(second_list[:], pos2)
+                if c == 1:
+                    pre = [first_layer_product(chunks[:2], e, half) for half in halves]
+                for half in halves:
+                    if c == (SIG_AFTER_LAST if e == E - 1 else SIG_AFTER)[half]:
+                        sig[half] = chunks[c][2][:, half].rearrange("p (s t) -> p s t", t=PACK)
+                        nc.scalar.activation(sig[half], pre[half], SIGMOID)
+            lin = [first_layer_product(chunks[2:], e, half) for half in halves]
+            pending = (lin, sig)
+
+        w2_raw, spent_tag, spent_rest, gates = {}, {}, {}, {}
 
         def load_w2(n):
-            most = stream_tile([P, E - 1, PACK * P])
-            rest = stream_tile([P, T])
-            raw = [most[:, e] for e in range(E - 1)] + [rest[:, : PACK * P]]
+            count = A_COUNT[n]
+            spent_tag[n] = "stream%d" % (turns["stream"] % STREAM_BUFS)
+            most = stream_tile([P, count * PACK * P])
+            width = max((E - count) * PACK * P, T)
+            rest = stream_tile([P, width])
+            spent_rest[n] = rest[:, width - T :]
             for e in range(E):
+                if e < count:
+                    piece = most[:, e * PACK * P : (e + 1) * PACK * P]
+                else:
+                    piece = rest[:, width - (E - e) * PACK * P : width - (E - e - 1) * PACK * P]
                 rows = w2[e, :, n * P : (n + 1) * P]
                 nc.sync.dma_start(
-                    raw[e].rearrange("p (j c) -> p j c", j=PACK), rows.rearrange("(p j) c -> p j c", j=PACK)
+                    piece.rearrange("p (j c) -> p j c", j=PACK), rows.rearrange("(p j) c -> p j c", j=PACK)
                 )
-            return raw, rest
+                w2_raw[n, e] = piece
 
         def load_gate(r, n):
-            weights = stream_tile([P, T])
-            nc.sync.dma_start(weights[:], gate[r, n * P : (n + 1) * P, :])
-            return weights
+            gates[r, n] = stream_tile([P, T])
+            nc.sync.dma_start(gates[r, n][:], gate[r, n * P : (n + 1) * P, :])
 
-        def second_layer(n, raw):
-            grouped = ring_tile(rings, "grouped2", 2, [P, E, P * PACK], BF16)
-            for e in range(E):
+        orders = (
+            ("w0", "00", "w1", "10", "01", "w2", "11", "02", "12"),
+            ("w0", "w1", "00", "10", "w2", "01", "11", "02", "12"),
+            ("w0", "00", "w1", "10", "w2", "01", "11", "02", "12"),
+            ("w0", "w1", "00", "10", "01", "w2", "11", "02", "12"),
+            ("w0", "00", "10", "w1", "01", "11", "w2", "02", "12"),
+            ("w0", "w1", "00", "w2", "10", "01", "11", "02", "12"),
+        )
+        for item in orders[GATE_ORDER]:
+            if item[0] == "w":
+                load_w2(int(item[1]))
+            else:
+                load_gate(int(item[0]), int(item[1]))
+
+        w2_q, banks, ys = {}, {}, {}
+
+        def cast_w2(n, experts):
+            if n not in w2_q:
+                w2_q[n] = (
+                    ring_tile(rings, "grouped2", 2, [P, E, P * PACK], BF16),
+                    ring_tile(rings, "w2_codes", 2, [P, E * P], U32),
+                    ring_tile(rings, "w2_scales", 2, [P, E * P], U8),
+                )
+            grouped, w_codes, w_scales = w2_q[n]
+            for e in experts:
                 dst = grouped[:, e].rearrange("p (c i j) -> p c j i", i=4, j=PACK)
-                src = raw[e].rearrange("p (j c i) -> p c j i", i=4, j=PACK)
-                if n == 0 and e < 2:
+                src = w2_raw[n, e].rearrange("p (j c i) -> p c j i", i=4, j=PACK)
+                if (n, e) in W2_ON_V:
                     nc.vector.tensor_copy(dst, src)
                 else:
                     nc.scalar.copy(dst, src)
-            w_codes = ring_tile(rings, "w2_codes", 2, [P, E * P], U32)
-            w_scales = ring_tile(rings, "w2_scales", 2, [P, E * P], U8)
-            for e0, e1 in EXPERT_GROUPS:
-                nc.vector.quantize_mx(
-                    out=w_codes[:, e0 * P : e1 * P].bitcast(FP8X4),
-                    scales=w_scales[:, e0 * P : e1 * P],
-                    in_=grouped[:, e0:e1].rearrange("p e x -> p (e x)"),
-                )
-            y = keep.tile([P, S], F32, name="y%d" % n)
-            for e0 in range(0, E, 2):
-                pair = range(e0, min(e0 + 2, E))
-                bank = bank_tile()
-                for e in pair:
-                    nc.tensor.matmul_mx(
-                        out=bank[:, (e - e0) * C : (e - e0 + 1) * C],
-                        lhsT=w_codes[:, e * P : (e + 1) * P].bitcast(FP8X4),
-                        lhsT_scale=w_scales[:, e * P : (e + 1) * P],
-                        rhs=hidden[e][0][:].bitcast(FP8X4),
-                        rhs_scale=hidden[e][1][:],
-                        start=True,
-                        stop=True,
-                    )
-                width = len(pair) * C
-                nc.scalar.copy(y[:, e0 * C : e0 * C + width], bank[:, :width])
-            return y
+                for e0, e1 in Q_GROUPS[n]:
+                    if e == e1 - 1:
+                        nc.vector.quantize_mx(
+                            out=w_codes[:, e0 * P : e1 * P].bitcast(FP8X4),
+                            scales=w_scales[:, e0 * P : e1 * P],
+                            in_=grouped[:, e0:e1].rearrange("p e x -> p (e x)"),
+                        )
 
-        w2_raw = [load_w2(0)]
-        gates = {}
+        def slot_results(n, groups):
+            grouped, w_codes, w_scales = w2_q[n]
+            if n not in ys:
+                tag = spent_tag[n + 1] if n + 1 < N_TILES and Y_TIE[n] else "y%d" % n
+                ys[n] = rings.tile([P, S], F32, name="y", tag=tag, align_bytes=64)
+            for e0, e1 in groups:
+                parts = 2 if LAST_Y_HALVES and n == 0 and e0 == E - 1 else 1
+                for part in range(parts):
+                    bank = bank_tile()
+                    width = C // parts
+                    for e in range(e0, e1):
+                        slots = slice(part * width, (part + 1) * width)
+                        nc.tensor.matmul_mx(
+                            out=bank[:, (e - e0) * C : (e - e0) * C + width],
+                            lhsT=w_codes[:, e * P : (e + 1) * P].bitcast(FP8X4),
+                            lhsT_scale=w_scales[:, e * P : (e + 1) * P],
+                            rhs=hidden[e][0][:, slots].bitcast(FP8X4),
+                            rhs_scale=hidden[e][1][:, slots],
+                            start=True,
+                            stop=True,
+                        )
+                    total_width = (e1 - e0) * width
+                    first_slot = e0 * C + part * width
+                    nc.scalar.copy(ys[n][:, first_slot : first_slot + total_width], bank[:, :total_width])
+
+        h_last = ring_tile(rings, "h_last", 1, [P, C * PACK], BF16)
+        if EARLY_Y0:
+            cast_w2(0, range(E))
+            if Y_TIE[0]:
+                cast_w2(1, range(A_COUNT[1]))
+            slot_results(0, COPY_GROUPS[0][:-1])
+            finish_hidden(pending[0], pending[1], h_last)
+            slot_results(0, COPY_GROUPS[0][-1:])
+        else:
+            finish_hidden(pending[0], pending[1], h_last)
+            cast_w2(0, range(E))
+            if Y_TIE[0]:
+                cast_w2(1, range(A_COUNT[1]))
+            slot_results(0, COPY_GROUPS[0])
         for n in range(N_TILES):
-            gates[0, n] = load_gate(0, n)
-            if n + 1 < N_TILES:
-                w2_raw.append(load_w2(n + 1))
-            gates[1, n] = load_gate(1, n)
-        y = second_layer(0, w2_raw[0][0])
-        for n in range(N_TILES):
+            parts = FINAL_PARTS if n == N_TILES - 1 else 1
+            y = ys[n]
             first = ring_tile(rings, "first", 2, [P, T], F32)
-            nc.vector.tensor_tensor(first[:], y[:].indirect(first_list[:]), gates[0, n][:], MULT)
-            if n + 1 < N_TILES:
-                y_next = second_layer(n + 1, w2_raw[n + 1][0])
-                second = w2_raw[n + 1][1]
-            else:
-                second = ring_tile(rings, "second", 1, [P, T], F32)
-            nc.vector.tensor_tensor(second[:], y[:].indirect(second_list[:]), gates[1, n][:], MULT)
             total = ring_tile(rings, "total", 2, [P, T], F32)
-            nc.vector.tensor_tensor(total[:], first[:], second[:], ADD)
-            nc.sync.dma_start(out[n * P : (n + 1) * P, :], total[:])
-            y = y_next
+            for part in range(parts):
+                cols = slice(part * T // parts, (part + 1) * T // parts)
+                entries = slice(part * T // parts // 16, (part + 1) * T // parts // 16)
+                nc.vector.tensor_tensor(first[:, cols], y[:].indirect(first_list[:, entries]), gates[0, n][:, cols], MULT)
+                if n + 1 < N_TILES:
+                    cast_w2(n + 1, range(A_COUNT[n + 1] if Y_TIE[n] else 0, E))
+                    if n + 2 < N_TILES and Y_TIE[n + 1]:
+                        cast_w2(n + 2, range(A_COUNT[n + 2]))
+                    slot_results(n + 1, COPY_GROUPS[n + 1])
+                if n + 1 < N_TILES and SECOND_TIE[n]:
+                    second = spent_rest[n + 1]
+                elif part == 0:
+                    second = ring_tile(rings, "second", 1, [P, T], F32)[:]
+                nc.vector.tensor_tensor(second[:, cols], y[:].indirect(second_list[:, entries]), gates[1, n][:, cols], MULT)
+                nc.vector.tensor_tensor(total[:, cols], first[:, cols], second[:, cols], ADD)
+                nc.sync.dma_start(out[n * P : (n + 1) * P, cols], total[:, cols])

@@ -1,6 +1,7 @@
 from contextlib import ExitStack
 
 import concourse.mybir as mybir
+from concourse.masks import make_identity
 
 K, T, E, C, H, N = 1024, 640, 5, 256, 512, 384
 S = E * C
@@ -21,30 +22,35 @@ P = 128
 PACK = 4
 K_PASS = P * PACK
 PASSES = K // K_PASS
+CHUNKS = 2 * PASSES
 HALF = 128
+BANK = 512
 N_TILES = N // P
-UPFRONT = 6
-GATHER_AFTER = (2, 5, 6, 7, 9, 10, 13, 14, 15)
-V_HALVES = (1, 2, 0, 0, 1, 2, 0, 0, 1, 2, 0, 0, 1, 2, 0, 0, 2, 1, 0, 1)
-SIG_AFTER = (3, 3)
-SIG_AFTER_LAST = (3, 3)
-MULT_AFTER = 0
-QH_SPLIT = (2, 2, 1, 2, 2)
-W2_ON_V = ((0, 1), (0, 3), (1, 1), (1, 2), (1, 4), (2, 4))
-WARM = True
-A_COUNT = (2, 4, 3)
-Y_TIE = (False, True)
-Q_GROUPS = (((0, 2), (2, 3), (3, 4), (4, 5)), ((0, 2), (2, 3), (3, 4), (4, 5)), ((0, 1), (1, 2), (2, 3), (3, 4), (4, 5)))
-COPY_GROUPS = (((0, 2), (2, 4), (4, 5)),) * 3
-LAST_Y_HALVES = True
-SPLIT_LAST = False
+PIECE = PACK * P
+STREAM_BUFS = 10
+GROUPED_BUFS = 6
+CODE_BUFS = 8
+LEAD = 2
+VP0 = (0, 0, 0, 0)
+MULTC = (0, 0)
+QH_PARTS = 1
+WORDS_AFTER = {2: 0, 3: 1, 4: 2}
+ON_V = (0, 1, 6, 7)
+SIG_PIECE = 2
+W2_AFTER = 1
+N0_EARLY = 0
+TIE0 = True
+LAST_PARTS = 2
+H_TIE = (None, None)
+PE_ADD = ()
+SIG0 = 3
+SUM_TAGS = ("w2_codes2", "w2_scales2")
+GROUPS0 = ((0, 2), (2, 4), (4, 5))
+EARLY_EXPERTS = 2
+RAW = PACK * H
+SIG = PACK * HALF
 FINAL_PARTS = 2
-EARLY_Y0 = True
-GATE_ORDER = 1
-SECOND_TIE = (False, False)
-STREAM_BUFS = 13
-GROUPED_BUFS = 12
-EXPERT_GROUPS = ((0, E - 1), (E - 1, E))
+EXPERT_GROUPS = ((0, 2), (2, 4), (4, 5))
 
 
 def tile_moe_pkd_glu_sigmoid_kernel(
@@ -57,19 +63,15 @@ def tile_moe_pkd_glu_sigmoid_kernel(
         psum = ctx.enter_context(tc.psum_pool(name="psum", bufs=1))
         turns = {}
 
-        def ring_tile(pool, ring, depth, shape, dtype):
+        def ring_tile(ring, depth, shape, dtype):
             turn = turns.get(ring, 0)
             turns[ring] = turn + 1
-            tag = "%s%d" % (ring, turn % depth)
-            if ring == "bank":
-                return pool.tile(shape, dtype, name=ring, tag=tag)
-            return pool.tile(shape, dtype, name=ring, tag=tag, align_bytes=64)
-
-        def stream_tile(shape):
-            return ring_tile(rings, "stream", STREAM_BUFS, shape, F32)
+            return rings.tile(shape, dtype, name=ring, tag="%s%d" % (ring, turn % depth), align_bytes=64)
 
         def bank_tile():
-            return ring_tile(psum, "bank", 8, [P, 512], F32)
+            turn = turns.get("bank", 0)
+            turns["bank"] = turn + 1
+            return psum.tile([P, BANK], F32, name="bank", tag="bank%d" % (turn % 8))
 
         slot_list = keep.tile([P, S // 16], U16, name="slot_list")
         nc.sync.dma_start(slot_list[:], offs)
@@ -84,56 +86,68 @@ def tile_moe_pkd_glu_sigmoid_kernel(
             nc.scalar.dma_start(
                 token_scales[32 * q : 32 * q + 4 * PASSES, :], x_scales[:, 4 * q : 4 * q + 4, :].bitcast(I32)
             )
+        warm = keep.tile([P, 8], F32, name="warm")
+        nc.vector.memset(warm[:], 0.0)
+        nc.scalar.activation(warm[:], warm[:], SIGMOID)
 
-        def gather_next(tag):
-            e, part = waiting[0]
-            waiting.remove((e, part))
+        slot_words, slot_scales = {}, {}
+
+        def gather_words(e, tag):
             offsets = slot_list[:, e * C // 16 : (e + 1) * C // 16]
-            if part < PASSES:
-                window, dtype = token_words[part][:].bitcast(U32), U32
-            else:
-                window, dtype = token_scales[:].bitcast(U8), U8
-            gathered = rings.tile([P, C], dtype, name="gathered", tag=tag, align_bytes=64)
-            nc.vector.tensor_copy(gathered[:], window.indirect(offsets))
-            tokens[e].append(gathered)
+            words = rings.tile([P, PASSES * C], U32, name="slot_words", tag=tag, align_bytes=64)
+            for a in range(PASSES):
+                nc.vector.tensor_copy(words[:, a * C : (a + 1) * C], token_words[a][:].bitcast(U32).indirect(offsets))
+            slot_words[e] = words
 
-        tokens = [[] for e in range(E)]
-        waiting = [(e, part) for e in range(E) for part in range(PASSES + 1)]
-        for part in range(UPFRONT):
-            gather_next("first_tokens%d" % part)
-        if WARM:
-            warm = keep.tile([P, 8], F32, name="warm")
-            nc.vector.memset(warm[:], 0.0)
-            nc.scalar.activation(warm[:], warm[:], SIGMOID)
+        def gather_scales(e):
+            offsets = slot_list[:, e * C // 16 : (e + 1) * C // 16]
+            slot_scales[e] = keep.tile([P, C], U8, name="slot_scales%d" % e, align_bytes=64)
+            nc.vector.tensor_copy(slot_scales[e][:], token_scales[:].bitcast(U8).indirect(offsets))
 
-        def quantise_first_layer_pass(w, e, a):
-            raw = stream_tile([P, PACK, H])
+        for e in range(EARLY_EXPERTS):
+            gather_words(e, "early_words%d" % e)
+        for e in range(E):
+            gather_scales(e)
+
+        def quantise_first_layer_pass(w, e, a, vector_pairs, spare):
+            chunk = turns.get("w_codes", 0)
+            late = [x for x in WORDS_AFTER if WORDS_AFTER[x] == chunk]
+            late_expert = late[0] if late else E
+            held = ring_tile("stream", STREAM_BUFS, [P, RAW + spare], F32)
+            raw = held[:, :RAW].rearrange("p (j c) -> p j c", j=PACK)
             rows = w[e, a * K_PASS : (a + 1) * K_PASS, :]
-            grouped = ring_tile(rings, "grouped", GROUPED_BUFS, [P, PACK * H], BF16)
-            parts = 2 if SPLIT_LAST and turns["grouped"] == 4 * E else 1
+            if late_expert < E:
+                grouped = rings.tile([P, RAW], BF16, name="grouped", tag="late_words%d" % late_expert, align_bytes=64)
+            else:
+                grouped = ring_tile("grouped", GROUPED_BUFS, [P, RAW], BF16)
+            parts = LAST_PARTS if chunk == E * CHUNKS - 1 else 1
+            src = raw.rearrange("p j (m t) -> p m j t", t=PACK)
+            dst = grouped[:].rearrange("p (t m j) -> p m j t", t=PACK, j=PACK)
             for part in range(parts):
                 cols = slice(part * H // parts, (part + 1) * H // parts)
                 nc.sync.dma_start(raw[:, :, cols], rows.rearrange("(p j) c -> p j c", j=PACK)[:, :, cols])
-            src = raw[:].rearrange("p j (m t) -> p m j t", t=PACK)
-            dst = grouped[:].rearrange("p (t m j) -> p m j t", t=PACK, j=PACK)
-            chunk = turns["grouped"] - 1
             for part in range(parts):
                 ms = slice(part * P // parts, (part + 1) * P // parts)
                 for pair in range(2):
                     planes = slice(2 * pair, 2 * pair + 2)
-                    if pair < V_HALVES[chunk]:
+                    if pair < vector_pairs:
                         nc.vector.tensor_copy(dst[:, ms, :, planes], src[:, ms, :, planes])
                     else:
                         nc.scalar.copy(dst[:, ms, :, planes], src[:, ms, :, planes])
-            w_codes = ring_tile(rings, "w_codes", 8, [P, H], U32)
-            w_scales = ring_tile(rings, "w_scales", 8, [P, H], U8)
-            nc.vector.quantize_mx(out=w_codes[:].bitcast(FP8X4), scales=w_scales[:], in_=grouped[:])
-            if chunk in GATHER_AFTER:
-                gather_next("grouped%d" % (chunk % GROUPED_BUFS))
-            return w_codes, w_scales, raw, grouped
+            w_codes = ring_tile("w_codes", CODE_BUFS, [P, H], U32)
+            w_scales = ring_tile("w_scales", CODE_BUFS, [P, H], U8)
+            for part in range(parts):
+                words = slice(part * H // parts, (part + 1) * H // parts)
+                nc.vector.quantize_mx(
+                    out=w_codes[:, words].bitcast(FP8X4),
+                    scales=w_scales[:, words],
+                    in_=grouped[:, words.start * PACK : words.stop * PACK],
+                )
+            if late_expert < E:
+                gather_words(late_expert, "late_words%d" % late_expert)
+            return w_codes, w_scales, held, grouped
 
         def first_layer_product(weights, e, half):
-            words, slot_scales = tokens[e][:PASSES], tokens[e][PASSES]
             slots = slice(half * HALF, (half + 1) * HALF)
             bank = bank_tile()
             for t in range(PACK):
@@ -143,175 +157,204 @@ def tile_moe_pkd_glu_sigmoid_kernel(
                         out=bank[:, t * HALF : (t + 1) * HALF],
                         lhsT=weights[a][0][:, cols].bitcast(FP8X4),
                         lhsT_scale=weights[a][1][:, cols],
-                        rhs=words[a][:, slots].bitcast(FP8X4),
-                        rhs_scale=slot_scales[4 * a :, slots],
+                        rhs=slot_words[e][:, a * C + half * HALF : a * C + (half + 1) * HALF].bitcast(FP8X4),
+                        rhs_scale=slot_scales[e][4 * a :, slots],
                         start=(a == 0),
                         stop=(a == PASSES - 1),
                     )
             return bank[:].rearrange("p (t s) -> p s t", t=PACK)
 
         halves = range(C // HALF)
-        hidden = []
+        h_codes = [keep.tile([P, C], U32, name="h_codes%d" % e, align_bytes=64) for e in range(E)]
+        h_scales = [keep.tile([P, C], U8, name="h_scales%d" % e, align_bytes=64) for e in range(E)]
 
-        def finish_hidden(lin, sig, h_bf):
-            e = len(hidden)
-            h_codes = keep.tile([P, C], U32, name="h_codes%d" % e, align_bytes=64)
-            h_scales = keep.tile([P, C], U8, name="h_scales%d" % e, align_bytes=64)
-            width = HALF * PACK
-            for half in halves:
-                h_half = h_bf[:, half * width : (half + 1) * width].rearrange("p (s t) -> p s t", t=PACK)
-                nc.vector.tensor_tensor(h_half, lin[half], sig[half], MULT)
-            step = C // QH_SPLIT[e]
-            for s0 in range(0, C, step):
-                nc.vector.quantize_mx(
-                    out=h_codes[:, s0 : s0 + step].bitcast(FP8X4),
-                    scales=h_scales[:, s0 : s0 + step],
-                    in_=h_bf[:, s0 * PACK : (s0 + step) * PACK],
-                )
-            hidden.append((h_codes, h_scales))
+        def multiply_hidden(h_bf, lin, sig):
+            nc.vector.tensor_tensor(h_bf.rearrange("p (s t) -> p s t", t=PACK), lin, sig, MULT)
+
+        def quantise_hidden(e, slots, h_bf):
+            nc.vector.quantize_mx(out=h_codes[e][:, slots].bitcast(FP8X4), scales=h_scales[e][:, slots], in_=h_bf)
+
+        def sigmoid_into(spent, pre):
+            sig = spent.rearrange("p (s t) -> p s t", t=PACK)
+            nc.scalar.activation(sig, pre, SIGMOID)
+            return sig
+
+        gates = keep.tile([P, 2 * T], F32, name="gates", align_bytes=64)
+        identity = keep.tile([P, P], F32, name="identity")
+        make_identity(nc, identity[:])
+
+        def spread_gates():
+            blocks = 2 * T // P
+            gate_rows = keep.tile([P, P], F32, name="gate_rows")
+            nc.gpsimd.memset(gate_rows[:], 0.0)
+            nc.sync.dma_start(gate_rows[:blocks, :], gate[:, 0, :].rearrange("r (b p) -> r b p", p=P))
+
+            turned = bank_tile()
+            nc.tensor.transpose(turned[:, :P], gate_rows[:], identity[:])
+            gate_cols = keep.tile([P, blocks], F32, name="gate_cols")
+            nc.scalar.copy(gate_cols[:], turned[:, :blocks])
+            per_bank = BANK // P
+            for b0 in range(0, blocks, per_bank):
+                b1 = min(b0 + per_bank, blocks)
+                bank = bank_tile()
+                for b in range(b0, b1):
+                    nc.tensor.transpose(
+                        bank[:, (b - b0) * P : (b - b0 + 1) * P],
+                        gate_cols[:, b : b + 1].to_broadcast([P, P]),
+                        identity[:],
+                    )
+                nc.scalar.copy(gates[:, b0 * P : b1 * P], bank[:, : (b1 - b0) * P])
 
         first_list = keep.tile([P, T // 16], U16, name="first_list")
         second_list = keep.tile([P, T // 16], U16, name="second_list")
-        pending = None
-        for e in range(E):
-            chunks = []
-            sig = [None, None]
-            for c in range(4):
-                chunks.append(quantise_first_layer_pass(w1 if c < 2 else w3, e, c % 2))
-                if pending is not None and c == MULT_AFTER:
-                    finish_hidden(pending[0], pending[1], chunks[c][3])
-                if c == 1 and e == 0:
-                    nc.sync.dma_start(first_list[:], pos1)
-                    nc.sync.dma_start(second_list[:], pos2)
-                if c == 1:
-                    pre = [first_layer_product(chunks[:2], e, half) for half in halves]
-                for half in halves:
-                    if c == (SIG_AFTER_LAST if e == E - 1 else SIG_AFTER)[half]:
-                        sig[half] = chunks[c][2][:, half].rearrange("p (s t) -> p s t", t=PACK)
-                        nc.scalar.activation(sig[half], pre[half], SIGMOID)
-            lin = [first_layer_product(chunks[2:], e, half) for half in halves]
-            pending = (lin, sig)
 
-        w2_raw, spent_tag, spent_rest, gates = {}, {}, {}, {}
+        w2_raw = {}
+        w2_grouped = [rings.tile([P, E * PIECE], BF16, name="w2_grouped", tag="w2_grouped%d" % n, align_bytes=64) for n in range(N_TILES)]
+        w2_codes = [rings.tile([P, E * P], U32, name="w2_codes", tag="w2_codes%d" % n, align_bytes=64) for n in range(N_TILES)]
+        w2_scales = [rings.tile([P, E * P], U8, name="w2_scales", tag="w2_scales%d" % n, align_bytes=64) for n in range(N_TILES)]
 
-        def load_w2(n):
-            count = A_COUNT[n]
-            spent_tag[n] = "stream%d" % (turns["stream"] % STREAM_BUFS)
-            most = stream_tile([P, count * PACK * P])
-            width = max((E - count) * PACK * P, T)
-            rest = stream_tile([P, width])
-            spent_rest[n] = rest[:, width - T :]
-            for e in range(E):
-                if e < count:
-                    piece = most[:, e * PACK * P : (e + 1) * PACK * P]
-                else:
-                    piece = rest[:, width - (E - e) * PACK * P : width - (E - e - 1) * PACK * P]
+        def load_w2(first_piece, end_piece):
+            tag = "stream%d" % (turns["stream"] % STREAM_BUFS)
+            held = ring_tile("stream", STREAM_BUFS, [P, (end_piece - first_piece) * PIECE], F32)
+            for piece in range(first_piece, end_piece):
+                n, e = divmod(piece, E)
+                w2_raw[piece] = held[:, (piece - first_piece) * PIECE : (piece - first_piece + 1) * PIECE]
                 rows = w2[e, :, n * P : (n + 1) * P]
                 nc.sync.dma_start(
-                    piece.rearrange("p (j c) -> p j c", j=PACK), rows.rearrange("(p j) c -> p j c", j=PACK)
+                    w2_raw[piece].rearrange("p (j c) -> p j c", j=PACK), rows.rearrange("(p j) c -> p j c", j=PACK)
                 )
-                w2_raw[n, e] = piece
+            return tag
 
-        def load_gate(r, n):
-            gates[r, n] = stream_tile([P, T])
-            nc.sync.dma_start(gates[r, n][:], gate[r, n * P : (n + 1) * P, :])
-
-        orders = (
-            ("w0", "00", "w1", "10", "01", "w2", "11", "02", "12"),
-            ("w0", "w1", "00", "10", "w2", "01", "11", "02", "12"),
-            ("w0", "00", "w1", "10", "w2", "01", "11", "02", "12"),
-            ("w0", "w1", "00", "10", "01", "w2", "11", "02", "12"),
-            ("w0", "00", "10", "w1", "01", "11", "w2", "02", "12"),
-            ("w0", "w1", "00", "w2", "10", "01", "11", "02", "12"),
-        )
-        for item in orders[GATE_ORDER]:
-            if item[0] == "w":
-                load_w2(int(item[1]))
-            else:
-                load_gate(int(item[0]), int(item[1]))
-
-        w2_q, banks, ys = {}, {}, {}
-
-        def cast_w2(n, experts):
-            if n not in w2_q:
-                w2_q[n] = (
-                    ring_tile(rings, "grouped2", 2, [P, E, P * PACK], BF16),
-                    ring_tile(rings, "w2_codes", 2, [P, E * P], U32),
-                    ring_tile(rings, "w2_scales", 2, [P, E * P], U8),
-                )
-            grouped, w_codes, w_scales = w2_q[n]
-            for e in experts:
-                dst = grouped[:, e].rearrange("p (c i j) -> p c j i", i=4, j=PACK)
-                src = w2_raw[n, e].rearrange("p (j c i) -> p c j i", i=4, j=PACK)
-                if (n, e) in W2_ON_V:
+        def round_w2(first_piece, end_piece):
+            for piece in range(first_piece, end_piece):
+                n, e = divmod(piece, E)
+                dst = w2_grouped[n][:, e * PIECE : (e + 1) * PIECE].rearrange("p (c i j) -> p c j i", i=4, j=PACK)
+                src = w2_raw[piece].rearrange("p (j c i) -> p c j i", i=4, j=PACK)
+                if piece in ON_V:
                     nc.vector.tensor_copy(dst, src)
                 else:
                     nc.scalar.copy(dst, src)
-                for e0, e1 in Q_GROUPS[n]:
-                    if e == e1 - 1:
-                        nc.vector.quantize_mx(
-                            out=w_codes[:, e0 * P : e1 * P].bitcast(FP8X4),
-                            scales=w_scales[:, e0 * P : e1 * P],
-                            in_=grouped[:, e0:e1].rearrange("p e x -> p (e x)"),
-                        )
 
-        def slot_results(n, groups):
-            grouped, w_codes, w_scales = w2_q[n]
-            if n not in ys:
-                tag = spent_tag[n + 1] if n + 1 < N_TILES and Y_TIE[n] else "y%d" % n
-                ys[n] = rings.tile([P, S], F32, name="y", tag=tag, align_bytes=64)
-            for e0, e1 in groups:
-                parts = 2 if LAST_Y_HALVES and n == 0 and e0 == E - 1 else 1
-                for part in range(parts):
-                    bank = bank_tile()
-                    width = C // parts
-                    for e in range(e0, e1):
-                        slots = slice(part * width, (part + 1) * width)
-                        nc.tensor.matmul_mx(
-                            out=bank[:, (e - e0) * C : (e - e0) * C + width],
-                            lhsT=w_codes[:, e * P : (e + 1) * P].bitcast(FP8X4),
-                            lhsT_scale=w_scales[:, e * P : (e + 1) * P],
-                            rhs=hidden[e][0][:, slots].bitcast(FP8X4),
-                            rhs_scale=hidden[e][1][:, slots],
-                            start=True,
-                            stop=True,
-                        )
-                    total_width = (e1 - e0) * width
-                    first_slot = e0 * C + part * width
-                    nc.scalar.copy(ys[n][:, first_slot : first_slot + total_width], bank[:, :total_width])
+        def quantise_w2(n, e0, e1):
+            nc.vector.quantize_mx(
+                out=w2_codes[n][:, e0 * P : e1 * P].bitcast(FP8X4),
+                scales=w2_scales[n][:, e0 * P : e1 * P],
+                in_=w2_grouped[n][:, e0 * PIECE : e1 * PIECE],
+            )
 
-        h_last = ring_tile(rings, "h_last", 1, [P, C * PACK], BF16)
-        if EARLY_Y0:
-            cast_w2(0, range(E))
-            if Y_TIE[0]:
-                cast_w2(1, range(A_COUNT[1]))
-            slot_results(0, COPY_GROUPS[0][:-1])
-            finish_hidden(pending[0], pending[1], h_last)
-            slot_results(0, COPY_GROUPS[0][-1:])
-        else:
-            finish_hidden(pending[0], pending[1], h_last)
-            cast_w2(0, range(E))
-            if Y_TIE[0]:
-                cast_w2(1, range(A_COUNT[1]))
-            slot_results(0, COPY_GROUPS[0])
+        def slot_results(n, y, e0, e1, slots):
+            bank = bank_tile()
+            width = slots.stop - slots.start
+            for e in range(e0, e1):
+                nc.tensor.matmul_mx(
+                    out=bank[:, (e - e0) * width : (e - e0 + 1) * width],
+                    lhsT=w2_codes[n][:, e * P : (e + 1) * P].bitcast(FP8X4),
+                    lhsT_scale=w2_scales[n][:, e * P : (e + 1) * P],
+                    rhs=h_codes[e][:, slots].bitcast(FP8X4),
+                    rhs_scale=h_scales[e][:, slots],
+                    start=True,
+                    stop=True,
+                )
+            first_slot = e0 * C + slots.start
+            nc.scalar.copy(y[:, first_slot : first_slot + (e1 - e0) * width], bank[:, : (e1 - e0) * width])
+
+        all_slots = slice(0, C)
+        half_slots = [slice(half * HALF, (half + 1) * HALF) for half in halves]
+        sig = []
+        for e in range(E):
+            chunks = []
+            for c in range(CHUNKS):
+                w = w1 if c < PASSES else w3
+                takes_sig = c in (SIG0, (SIG0 + 1) % CHUNKS)
+                chunks.append(quantise_first_layer_pass(w, e, c % PASSES, 1 if e else VP0[c], SIG if takes_sig else 0))
+                behind = chunks[c][2][:, RAW - 2 :]
+                if c == (SIG0 + 1) % CHUNKS and (e > 0 or c > 0):
+                    sig.append(sigmoid_into(behind[:, :SIG], pre[1]))
+                for half in halves:
+                    if e > 0 and c == MULTC[half]:
+                        h_bf = chunks[c][3][:, half * SIG : (half + 1) * SIG]
+                        multiply_hidden(h_bf, lin[half], sig[half])
+                        if QH_PARTS == 2:
+                            quantise_hidden(e - 1, half_slots[half], h_bf)
+                        elif half == 1:
+                            quantise_hidden(e - 1, slice(0, C), chunks[c][3][:, : 2 * SIG])
+                if c == W2_AFTER and e < N0_EARLY:
+                    load_w2(e, e + 1)
+                    round_w2(e, e + 1)
+                    quantise_w2(0, e, e + 1)
+                if c == 0 and e == 2:
+                    nc.sync.dma_start(first_list[:], pos1)
+                    nc.sync.dma_start(second_list[:], pos2)
+                    spread_gates()
+                if c == PASSES - 1:
+                    pre = [first_layer_product(chunks[:PASSES], e, half) for half in halves]
+                if c == SIG0:
+                    last_sig, sig = sig, [sigmoid_into(behind[:, :SIG], pre[0])]
+            lin = [first_layer_product(chunks[PASSES:], e, half) for half in halves]
+
+        ends = [E, 2 * E + LEAD, N_TILES * E]
+        load_w2(N0_EARLY, E)
+        w2_tags = [None] + [load_w2(ends[n], ends[n + 1]) for n in range(N_TILES - 1)]
+        round_w2(N0_EARLY, E)
+        if SIG0 == 3:
+            sig.append(sigmoid_into(w2_raw[SIG_PIECE], pre[1]))
+        for e0, e1 in GROUPS0:
+            quantise_w2(0, e0, e1)
+        y = rings.tile([P, S], F32, name="y", tag="y0", align_bytes=64)
+        for e0, e1 in EXPERT_GROUPS[:-1]:
+            slot_results(0, y, e0, e1, all_slots)
+        h_last = keep.tile([P, C * PACK], BF16, name="h_last", align_bytes=64)
+        h_halves = [h_last[:, half * SIG : (half + 1) * SIG] if H_TIE[half] is None else w2_grouped[0][:, H_TIE[half] * PIECE : (H_TIE[half] + 1) * PIECE] for half in halves]
+        for half in halves:
+            multiply_hidden(h_halves[half], lin[half], sig[half])
+        for half in halves:
+            quantise_hidden(E - 1, half_slots[half], h_halves[half])
+        for half in halves:
+            slot_results(0, y, E - 1, E, slice(half * HALF, (half + 1) * HALF))
+        def turn_blocks(dst, terms):
+            for c0 in range(0, T, BANK):
+                c1 = min(c0 + BANK, T)
+                bank = bank_tile()
+                for b in range(c0, c1, P):
+                    for i, term in enumerate(terms):
+                        nc.tensor.matmul(
+                            bank[:, b - c0 : b - c0 + P], term[:, b : b + P], identity[:],
+                            start=(i == 0), stop=(i == len(terms) - 1), is_transpose=True,
+                        )
+                nc.scalar.copy(dst[:, c0:c1], bank[:, : c1 - c0])
+
+        later = []
         for n in range(N_TILES):
-            parts = FINAL_PARTS if n == N_TILES - 1 else 1
-            y = ys[n]
-            first = ring_tile(rings, "first", 2, [P, T], F32)
-            total = ring_tile(rings, "total", 2, [P, T], F32)
+            last = n + 1 == N_TILES
+            parts = FINAL_PARTS if last else 1
+            first = ring_tile("first", 3, [P, T], F32)
+            total = ring_tile("total", 3, [P, T], F32)
             for part in range(parts):
                 cols = slice(part * T // parts, (part + 1) * T // parts)
-                entries = slice(part * T // parts // 16, (part + 1) * T // parts // 16)
-                nc.vector.tensor_tensor(first[:, cols], y[:].indirect(first_list[:, entries]), gates[0, n][:, cols], MULT)
-                if n + 1 < N_TILES:
-                    cast_w2(n + 1, range(A_COUNT[n + 1] if Y_TIE[n] else 0, E))
-                    if n + 2 < N_TILES and Y_TIE[n + 1]:
-                        cast_w2(n + 2, range(A_COUNT[n + 2]))
-                    slot_results(n + 1, COPY_GROUPS[n + 1])
-                if n + 1 < N_TILES and SECOND_TIE[n]:
-                    second = spent_rest[n + 1]
-                elif part == 0:
-                    second = ring_tile(rings, "second", 1, [P, T], F32)[:]
-                nc.vector.tensor_tensor(second[:, cols], y[:].indirect(second_list[:, entries]), gates[1, n][:, cols], MULT)
+                gate_cols2 = slice(T + cols.start, T + cols.stop)
+                entries = slice(cols.start // 16, cols.stop // 16)
+                nc.vector.tensor_tensor(first[:, cols], y[:].indirect(first_list[:, entries]), gates[:, cols], MULT)
+                if not last:
+                    round_w2(ends[n], ends[n + 1])
+                    for e0, e1 in EXPERT_GROUPS:
+                        quantise_w2(n + 1, e0, e1)
+                    next_y = rings.tile([P, S], F32, name="y", tag=w2_tags[n + 1], align_bytes=64)
+                    for e0, e1 in EXPERT_GROUPS:
+                        slot_results(n + 1, next_y, e0, e1, all_slots)
+                if part == 0:
+                    tag = "second" if last or (n == 0 and not TIE0) else "w2_grouped%d" % (n + 1)
+                    second = rings.tile([P, T], F32, name="second", tag=tag, align_bytes=64)
+                nc.vector.tensor_tensor(second[:, cols], y[:].indirect(second_list[:, entries]), gates[:, gate_cols2], MULT)
+                if n in PE_ADD:
+                    later.append((n, first, second, total))
+                    continue
                 nc.vector.tensor_tensor(total[:, cols], first[:, cols], second[:, cols], ADD)
                 nc.sync.dma_start(out[n * P : (n + 1) * P, cols], total[:, cols])
+            if not last:
+                y = next_y
+            if n == N_TILES - 2:
+                for m, first, second, total in later:
+                    summed = rings.tile([P, T], F32, name="summed", tag=SUM_TAGS[m], align_bytes=64)
+                    turn_blocks(summed, [first, second])
+                    turn_blocks(total, [summed])
+                    nc.sync.dma_start(out[m * P : (m + 1) * P, :], total[:])

@@ -29,21 +29,28 @@ N_TILES = N // P
 PIECE = PACK * P
 STREAM_BUFS = 10
 GROUPED_BUFS = 6
-CODE_BUFS = 8
-LEAD = 2
-VP0 = (0, 0, 0, 0)
-MULTC = (0, 0)
-QH_PARTS = 1
+CODE_BUFS = 6
+LEAD = 4
+VP0 = (0, 0, 1, 0)
+VP = (2, 0, 2, 0)
+VP3 = (2, 0, 1, 1)
+VPL = (1, 1, 1, 1)
+SIGL = (3, 4)
+MULT_TIE = False
+TIE1 = False
+FIRST_TIE = False
+GROUPS1 = ((0, 2), (2, 4), (4, 5))
+GROUPS2 = ((0, 2), (2, 4), (4, 5))
+MULTC = 0
 WORDS_AFTER = {2: 0, 3: 1, 4: 2}
-ON_V = (0, 1, 6, 7)
+ON_V = (0, 1, 5, 6, 7, 8, 9)
 SIG_PIECE = 2
 W2_AFTER = 1
 N0_EARLY = 0
-TIE0 = True
+TIE0 = False
 LAST_PARTS = 2
 H_TIE = (None, None)
 PE_ADD = ()
-SIG0 = 3
 SUM_TAGS = ("w2_codes2", "w2_scales2")
 GROUPS0 = ((0, 2), (2, 4), (4, 5))
 EARLY_EXPERTS = 2
@@ -128,7 +135,7 @@ def tile_moe_pkd_glu_sigmoid_kernel(
                 nc.sync.dma_start(raw[:, :, cols], rows.rearrange("(p j) c -> p j c", j=PACK)[:, :, cols])
             for part in range(parts):
                 ms = slice(part * P // parts, (part + 1) * P // parts)
-                for pair in range(2):
+                for pair in (1, 0):
                     planes = slice(2 * pair, 2 * pair + 2)
                     if pair < vector_pairs:
                         nc.vector.tensor_copy(dst[:, ms, :, planes], src[:, ms, :, planes])
@@ -260,24 +267,32 @@ def tile_moe_pkd_glu_sigmoid_kernel(
 
         all_slots = slice(0, C)
         half_slots = [slice(half * HALF, (half + 1) * HALF) for half in halves]
-        sig = []
         for e in range(E):
             chunks = []
+            last = e == E - 1
             for c in range(CHUNKS):
                 w = w1 if c < PASSES else w3
-                takes_sig = c in (SIG0, (SIG0 + 1) % CHUNKS)
-                chunks.append(quantise_first_layer_pass(w, e, c % PASSES, 1 if e else VP0[c], SIG if takes_sig else 0))
-                behind = chunks[c][2][:, RAW - 2 :]
-                if c == (SIG0 + 1) % CHUNKS and (e > 0 or c > 0):
-                    sig.append(sigmoid_into(behind[:, :SIG], pre[1]))
-                for half in halves:
-                    if e > 0 and c == MULTC[half]:
-                        h_bf = chunks[c][3][:, half * SIG : (half + 1) * SIG]
-                        multiply_hidden(h_bf, lin[half], sig[half])
-                        if QH_PARTS == 2:
-                            quantise_hidden(e - 1, half_slots[half], h_bf)
-                        elif half == 1:
-                            quantise_hidden(e - 1, slice(0, C), chunks[c][3][:, : 2 * SIG])
+                shares = VP0 if e == 0 else VPL if last else VP3 if e == E - 2 else VP
+                owed = e > 0 and len(sig) == 1
+                takes_sig = (c in SIGL if last else c == CHUNKS - 1) or (c == 0 and owed)
+                vector_pairs = shares[c]
+                chunks.append(quantise_first_layer_pass(w, e, c % PASSES, vector_pairs, SIG if takes_sig else 0))
+                if c == 0 and owed:
+                    sig.append(sigmoid_into(chunks[c][2][:, RAW - 2 : RAW - 2 + SIG], pre[1]))
+                if e > 0 and c == MULTC:
+                    h_bf = chunks[c][3] if MULT_TIE else ring_tile("h_bf", 2, [P, 2 * SIG], BF16)
+                    for half in halves:
+                        multiply_hidden(h_bf[:, half * SIG : (half + 1) * SIG], lin[half], sig[half])
+                    quantise_hidden(e - 1, slice(0, C), h_bf[:, : 2 * SIG])
+                if c == CHUNKS - 1 and not last:
+                    held = chunks[c][2]
+                    sig = [sigmoid_into(held[:, RAW - 2 : RAW - 2 + SIG], pre[0])]
+                    if vector_pairs == 0:
+                        sig.append(sigmoid_into(held[:, :SIG], pre[1]))
+                if last and c == SIGL[0]:
+                    sig = [sigmoid_into(chunks[c][2][:, RAW - 2 : RAW - 2 + SIG], pre[0])]
+                if last and c == SIGL[1]:
+                    sig.append(sigmoid_into(chunks[c][2][:, RAW - 2 : RAW - 2 + SIG], pre[1]))
                 if c == W2_AFTER and e < N0_EARLY:
                     load_w2(e, e + 1)
                     round_w2(e, e + 1)
@@ -288,15 +303,13 @@ def tile_moe_pkd_glu_sigmoid_kernel(
                     spread_gates()
                 if c == PASSES - 1:
                     pre = [first_layer_product(chunks[:PASSES], e, half) for half in halves]
-                if c == SIG0:
-                    last_sig, sig = sig, [sigmoid_into(behind[:, :SIG], pre[0])]
             lin = [first_layer_product(chunks[PASSES:], e, half) for half in halves]
 
         ends = [E, 2 * E + LEAD, N_TILES * E]
         load_w2(N0_EARLY, E)
         w2_tags = [None] + [load_w2(ends[n], ends[n + 1]) for n in range(N_TILES - 1)]
         round_w2(N0_EARLY, E)
-        if SIG0 == 3:
+        if SIGL[1] == 4:
             sig.append(sigmoid_into(w2_raw[SIG_PIECE], pre[1]))
         for e0, e1 in GROUPS0:
             quantise_w2(0, e0, e1)
@@ -327,7 +340,13 @@ def tile_moe_pkd_glu_sigmoid_kernel(
         for n in range(N_TILES):
             last = n + 1 == N_TILES
             parts = FINAL_PARTS if last else 1
-            first = ring_tile("first", 3, [P, T], F32)
+            if FIRST_TIE and n == 0:
+                round_w2(E, 2 * E)
+                for e0, e1 in GROUPS1:
+                    quantise_w2(1, e0, e1)
+                first = rings.tile([P, T], F32, name="first", tag="w2_grouped1", align_bytes=64)
+            else:
+                first = ring_tile("first", 3, [P, T], F32)
             total = ring_tile("total", 3, [P, T], F32)
             for part in range(parts):
                 cols = slice(part * T // parts, (part + 1) * T // parts)
@@ -335,14 +354,14 @@ def tile_moe_pkd_glu_sigmoid_kernel(
                 entries = slice(cols.start // 16, cols.stop // 16)
                 nc.vector.tensor_tensor(first[:, cols], y[:].indirect(first_list[:, entries]), gates[:, cols], MULT)
                 if not last:
-                    round_w2(ends[n], ends[n + 1])
-                    for e0, e1 in EXPERT_GROUPS:
+                    round_w2(2 * E if FIRST_TIE and n == 0 else ends[n], ends[n + 1])
+                    for e0, e1 in () if FIRST_TIE and n == 0 else (GROUPS1, GROUPS2)[n]:
                         quantise_w2(n + 1, e0, e1)
                     next_y = rings.tile([P, S], F32, name="y", tag=w2_tags[n + 1], align_bytes=64)
                     for e0, e1 in EXPERT_GROUPS:
                         slot_results(n + 1, next_y, e0, e1, all_slots)
                 if part == 0:
-                    tag = "second" if last or (n == 0 and not TIE0) else "w2_grouped%d" % (n + 1)
+                    tag = "second%d" % n if last or (n == 0 and (FIRST_TIE or not TIE0)) or (n == 1 and not TIE1) else "w2_grouped%d" % (n + 1)
                     second = rings.tile([P, T], F32, name="second", tag=tag, align_bytes=64)
                 nc.vector.tensor_tensor(second[:, cols], y[:].indirect(second_list[:, entries]), gates[:, gate_cols2], MULT)
                 if n in PE_ADD:

@@ -28,26 +28,29 @@ BANK = 512
 N_TILES = N // P
 PIECE = PACK * P
 STREAM_BUFS = 10
-GROUPED_BUFS = 6
+GROUPED_BUFS = 5
 CODE_BUFS = 6
-LEAD = 4
+LEAD = 1
 VP0 = (0, 0, 1, 0)
 VP = (2, 0, 2, 0)
 VP3 = (2, 0, 1, 1)
 VPL = (1, 1, 1, 1)
 SIGL = (3, 4)
 MULT_TIE = False
-TIE1 = False
+TIE1 = True
+GATE_AFTER = (7, 9)
+ALIGN = 256
+LISTS_AT = 0
 FIRST_TIE = False
 GROUPS1 = ((0, 2), (2, 4), (4, 5))
 GROUPS2 = ((0, 2), (2, 4), (4, 5))
 MULTC = 0
 WORDS_AFTER = {2: 0, 3: 1, 4: 2}
-ON_V = (0, 1, 5, 6, 7, 8, 9)
+ON_V = (0, 1, 5, 6, 7)
 SIG_PIECE = 2
 W2_AFTER = 1
 N0_EARLY = 0
-TIE0 = False
+TIE0 = True
 LAST_PARTS = 2
 H_TIE = (None, None)
 PE_ADD = ()
@@ -73,7 +76,7 @@ def tile_moe_pkd_glu_sigmoid_kernel(
         def ring_tile(ring, depth, shape, dtype):
             turn = turns.get(ring, 0)
             turns[ring] = turn + 1
-            return rings.tile(shape, dtype, name=ring, tag="%s%d" % (ring, turn % depth), align_bytes=64)
+            return rings.tile(shape, dtype, name=ring, tag="%s%d" % (ring, turn % depth), align_bytes=ALIGN)
 
         def bank_tile():
             turn = turns.get("bank", 0)
@@ -82,11 +85,11 @@ def tile_moe_pkd_glu_sigmoid_kernel(
 
         slot_list = keep.tile([P, S // 16], U16, name="slot_list")
         nc.sync.dma_start(slot_list[:], offs)
-        token_scales = keep.tile([P, T // 4], I32, name="token_scales", align_bytes=64)
+        token_scales = keep.tile([P, T // 4], I32, name="token_scales", align_bytes=ALIGN)
         nc.vector.memset(token_scales[:], 0)
         token_words = []
         for a in range(PASSES):
-            words = keep.tile([P, T], I32, name="token_words%d" % a, align_bytes=64)
+            words = keep.tile([P, T], I32, name="token_words%d" % a, align_bytes=ALIGN)
             nc.sync.dma_start(words[:], x_words[a].rearrange("p t r -> p (t r)").bitcast(I32))
             token_words.append(words)
         for q in range(4):
@@ -101,14 +104,14 @@ def tile_moe_pkd_glu_sigmoid_kernel(
 
         def gather_words(e, tag):
             offsets = slot_list[:, e * C // 16 : (e + 1) * C // 16]
-            words = rings.tile([P, PASSES * C], U32, name="slot_words", tag=tag, align_bytes=64)
+            words = rings.tile([P, PASSES * C], U32, name="slot_words", tag=tag, align_bytes=ALIGN)
             for a in range(PASSES):
                 nc.vector.tensor_copy(words[:, a * C : (a + 1) * C], token_words[a][:].bitcast(U32).indirect(offsets))
             slot_words[e] = words
 
         def gather_scales(e):
             offsets = slot_list[:, e * C // 16 : (e + 1) * C // 16]
-            slot_scales[e] = keep.tile([P, C], U8, name="slot_scales%d" % e, align_bytes=64)
+            slot_scales[e] = keep.tile([P, C], U8, name="slot_scales%d" % e, align_bytes=ALIGN)
             nc.vector.tensor_copy(slot_scales[e][:], token_scales[:].bitcast(U8).indirect(offsets))
 
         for e in range(EARLY_EXPERTS):
@@ -124,7 +127,7 @@ def tile_moe_pkd_glu_sigmoid_kernel(
             raw = held[:, :RAW].rearrange("p (j c) -> p j c", j=PACK)
             rows = w[e, a * K_PASS : (a + 1) * K_PASS, :]
             if late_expert < E:
-                grouped = rings.tile([P, RAW], BF16, name="grouped", tag="late_words%d" % late_expert, align_bytes=64)
+                grouped = rings.tile([P, RAW], BF16, name="grouped", tag="late_words%d" % late_expert, align_bytes=ALIGN)
             else:
                 grouped = ring_tile("grouped", GROUPED_BUFS, [P, RAW], BF16)
             parts = LAST_PARTS if chunk == E * CHUNKS - 1 else 1
@@ -172,8 +175,8 @@ def tile_moe_pkd_glu_sigmoid_kernel(
             return bank[:].rearrange("p (t s) -> p s t", t=PACK)
 
         halves = range(C // HALF)
-        h_codes = [keep.tile([P, C], U32, name="h_codes%d" % e, align_bytes=64) for e in range(E)]
-        h_scales = [keep.tile([P, C], U8, name="h_scales%d" % e, align_bytes=64) for e in range(E)]
+        h_codes = [keep.tile([P, C], U32, name="h_codes%d" % e, align_bytes=ALIGN) for e in range(E)]
+        h_scales = [keep.tile([P, C], U8, name="h_scales%d" % e, align_bytes=ALIGN) for e in range(E)]
 
         def multiply_hidden(h_bf, lin, sig):
             nc.vector.tensor_tensor(h_bf.rearrange("p (s t) -> p s t", t=PACK), lin, sig, MULT)
@@ -186,39 +189,17 @@ def tile_moe_pkd_glu_sigmoid_kernel(
             nc.scalar.activation(sig, pre, SIGMOID)
             return sig
 
-        gates = keep.tile([P, 2 * T], F32, name="gates", align_bytes=64)
-        identity = keep.tile([P, P], F32, name="identity")
-        make_identity(nc, identity[:])
-
-        def spread_gates():
-            blocks = 2 * T // P
-            gate_rows = keep.tile([P, P], F32, name="gate_rows")
-            nc.gpsimd.memset(gate_rows[:], 0.0)
-            nc.sync.dma_start(gate_rows[:blocks, :], gate[:, 0, :].rearrange("r (b p) -> r b p", p=P))
-
-            turned = bank_tile()
-            nc.tensor.transpose(turned[:, :P], gate_rows[:], identity[:])
-            gate_cols = keep.tile([P, blocks], F32, name="gate_cols")
-            nc.scalar.copy(gate_cols[:], turned[:, :blocks])
-            per_bank = BANK // P
-            for b0 in range(0, blocks, per_bank):
-                b1 = min(b0 + per_bank, blocks)
-                bank = bank_tile()
-                for b in range(b0, b1):
-                    nc.tensor.transpose(
-                        bank[:, (b - b0) * P : (b - b0 + 1) * P],
-                        gate_cols[:, b : b + 1].to_broadcast([P, P]),
-                        identity[:],
-                    )
-                nc.scalar.copy(gates[:, b0 * P : b1 * P], bank[:, : (b1 - b0) * P])
-
+        gates = [keep.tile([P, T], F32, name="gate%d" % r, align_bytes=ALIGN) for r in range(2)]
+        if PE_ADD:
+            identity = keep.tile([P, P], F32, name="identity")
+            make_identity(nc, identity[:])
         first_list = keep.tile([P, T // 16], U16, name="first_list")
         second_list = keep.tile([P, T // 16], U16, name="second_list")
 
         w2_raw = {}
-        w2_grouped = [rings.tile([P, E * PIECE], BF16, name="w2_grouped", tag="w2_grouped%d" % n, align_bytes=64) for n in range(N_TILES)]
-        w2_codes = [rings.tile([P, E * P], U32, name="w2_codes", tag="w2_codes%d" % n, align_bytes=64) for n in range(N_TILES)]
-        w2_scales = [rings.tile([P, E * P], U8, name="w2_scales", tag="w2_scales%d" % n, align_bytes=64) for n in range(N_TILES)]
+        w2_grouped = [rings.tile([P, E * PIECE], BF16, name="w2_grouped", tag="w2_grouped%d" % n, align_bytes=ALIGN) for n in range(N_TILES)]
+        w2_codes = [rings.tile([P, E * P], U32, name="w2_codes", tag="w2_codes%d" % n, align_bytes=ALIGN) for n in range(N_TILES)]
+        w2_scales = [rings.tile([P, E * P], U8, name="w2_scales", tag="w2_scales%d" % n, align_bytes=ALIGN) for n in range(N_TILES)]
 
         def load_w2(first_piece, end_piece):
             tag = "stream%d" % (turns["stream"] % STREAM_BUFS)
@@ -230,6 +211,9 @@ def tile_moe_pkd_glu_sigmoid_kernel(
                 nc.sync.dma_start(
                     w2_raw[piece].rearrange("p (j c) -> p j c", j=PACK), rows.rearrange("(p j) c -> p j c", j=PACK)
                 )
+                for r in range(2):
+                    if GATE_AFTER[r] == piece:
+                        nc.sync.dma_start(gates[r][:], gate[r, :P, :])
             return tag
 
         def round_w2(first_piece, end_piece):
@@ -278,7 +262,7 @@ def tile_moe_pkd_glu_sigmoid_kernel(
                 vector_pairs = shares[c]
                 chunks.append(quantise_first_layer_pass(w, e, c % PASSES, vector_pairs, SIG if takes_sig else 0))
                 if c == 0 and owed:
-                    sig.append(sigmoid_into(chunks[c][2][:, RAW - 2 : RAW - 2 + SIG], pre[1]))
+                    sig.append(sigmoid_into(chunks[c][2][:, RAW - 4 : RAW - 4 + SIG], pre[1]))
                 if e > 0 and c == MULTC:
                     h_bf = chunks[c][3] if MULT_TIE else ring_tile("h_bf", 2, [P, 2 * SIG], BF16)
                     for half in halves:
@@ -286,21 +270,20 @@ def tile_moe_pkd_glu_sigmoid_kernel(
                     quantise_hidden(e - 1, slice(0, C), h_bf[:, : 2 * SIG])
                 if c == CHUNKS - 1 and not last:
                     held = chunks[c][2]
-                    sig = [sigmoid_into(held[:, RAW - 2 : RAW - 2 + SIG], pre[0])]
+                    sig = [sigmoid_into(held[:, RAW - 4 : RAW - 4 + SIG], pre[0])]
                     if vector_pairs == 0:
                         sig.append(sigmoid_into(held[:, :SIG], pre[1]))
                 if last and c == SIGL[0]:
-                    sig = [sigmoid_into(chunks[c][2][:, RAW - 2 : RAW - 2 + SIG], pre[0])]
+                    sig = [sigmoid_into(chunks[c][2][:, RAW - 4 : RAW - 4 + SIG], pre[0])]
                 if last and c == SIGL[1]:
-                    sig.append(sigmoid_into(chunks[c][2][:, RAW - 2 : RAW - 2 + SIG], pre[1]))
+                    sig.append(sigmoid_into(chunks[c][2][:, RAW - 4 : RAW - 4 + SIG], pre[1]))
                 if c == W2_AFTER and e < N0_EARLY:
                     load_w2(e, e + 1)
                     round_w2(e, e + 1)
                     quantise_w2(0, e, e + 1)
-                if c == 0 and e == 2:
+                if c == 1 and e == LISTS_AT:
                     nc.sync.dma_start(first_list[:], pos1)
                     nc.sync.dma_start(second_list[:], pos2)
-                    spread_gates()
                 if c == PASSES - 1:
                     pre = [first_layer_product(chunks[:PASSES], e, half) for half in halves]
             lin = [first_layer_product(chunks[PASSES:], e, half) for half in halves]
@@ -313,10 +296,10 @@ def tile_moe_pkd_glu_sigmoid_kernel(
             sig.append(sigmoid_into(w2_raw[SIG_PIECE], pre[1]))
         for e0, e1 in GROUPS0:
             quantise_w2(0, e0, e1)
-        y = rings.tile([P, S], F32, name="y", tag="y0", align_bytes=64)
+        y = rings.tile([P, S], F32, name="y", tag="y0", align_bytes=ALIGN)
         for e0, e1 in EXPERT_GROUPS[:-1]:
             slot_results(0, y, e0, e1, all_slots)
-        h_last = keep.tile([P, C * PACK], BF16, name="h_last", align_bytes=64)
+        h_last = keep.tile([P, C * PACK], BF16, name="h_last", align_bytes=ALIGN)
         h_halves = [h_last[:, half * SIG : (half + 1) * SIG] if H_TIE[half] is None else w2_grouped[0][:, H_TIE[half] * PIECE : (H_TIE[half] + 1) * PIECE] for half in halves]
         for half in halves:
             multiply_hidden(h_halves[half], lin[half], sig[half])
@@ -344,26 +327,25 @@ def tile_moe_pkd_glu_sigmoid_kernel(
                 round_w2(E, 2 * E)
                 for e0, e1 in GROUPS1:
                     quantise_w2(1, e0, e1)
-                first = rings.tile([P, T], F32, name="first", tag="w2_grouped1", align_bytes=64)
+                first = rings.tile([P, T], F32, name="first", tag="w2_grouped1", align_bytes=ALIGN)
             else:
                 first = ring_tile("first", 3, [P, T], F32)
             total = ring_tile("total", 3, [P, T], F32)
             for part in range(parts):
                 cols = slice(part * T // parts, (part + 1) * T // parts)
-                gate_cols2 = slice(T + cols.start, T + cols.stop)
                 entries = slice(cols.start // 16, cols.stop // 16)
-                nc.vector.tensor_tensor(first[:, cols], y[:].indirect(first_list[:, entries]), gates[:, cols], MULT)
+                nc.vector.tensor_tensor(first[:, cols], y[:].indirect(first_list[:, entries]), gates[0][:, cols], MULT)
                 if not last:
                     round_w2(2 * E if FIRST_TIE and n == 0 else ends[n], ends[n + 1])
                     for e0, e1 in () if FIRST_TIE and n == 0 else (GROUPS1, GROUPS2)[n]:
                         quantise_w2(n + 1, e0, e1)
-                    next_y = rings.tile([P, S], F32, name="y", tag=w2_tags[n + 1], align_bytes=64)
+                    next_y = rings.tile([P, S], F32, name="y", tag=w2_tags[n + 1], align_bytes=ALIGN)
                     for e0, e1 in EXPERT_GROUPS:
                         slot_results(n + 1, next_y, e0, e1, all_slots)
                 if part == 0:
                     tag = "second%d" % n if last or (n == 0 and (FIRST_TIE or not TIE0)) or (n == 1 and not TIE1) else "w2_grouped%d" % (n + 1)
-                    second = rings.tile([P, T], F32, name="second", tag=tag, align_bytes=64)
-                nc.vector.tensor_tensor(second[:, cols], y[:].indirect(second_list[:, entries]), gates[:, gate_cols2], MULT)
+                    second = rings.tile([P, T], F32, name="second", tag=tag, align_bytes=ALIGN)
+                nc.vector.tensor_tensor(second[:, cols], y[:].indirect(second_list[:, entries]), gates[1][:, cols], MULT)
                 if n in PE_ADD:
                     later.append((n, first, second, total))
                     continue
@@ -373,7 +355,7 @@ def tile_moe_pkd_glu_sigmoid_kernel(
                 y = next_y
             if n == N_TILES - 2:
                 for m, first, second, total in later:
-                    summed = rings.tile([P, T], F32, name="summed", tag=SUM_TAGS[m], align_bytes=64)
+                    summed = rings.tile([P, T], F32, name="summed", tag=SUM_TAGS[m], align_bytes=ALIGN)
                     turn_blocks(summed, [first, second])
                     turn_blocks(total, [summed])
                     nc.sync.dma_start(out[m * P : (m + 1) * P, :], total[:])

@@ -35,10 +35,21 @@ VP0 = (0, 0, 1, 0)
 VP = (2, 0, 2, 0)
 VP3 = (2, 0, 1, 1)
 VPL = (1, 1, 1, 1)
-SIGL = (3, 4)
+SIGL = (1, 4)
+WARM = False
+TURNED = (0,)
+TURN_BACK = 3
+GATE_COLS_AT = 1
+COPY = mybir.ActivationFunctionType.Copy
+Y0_TIE = False
+MERGE_FROM = 2
+MERGE_TO = 0
+PAIR_BUFS = 4
+LISTS_AFTER = 7
+FINAL_CUTS = (0, 384, 640)
 MULT_TIE = False
-TIE1 = True
-GATE_AFTER = (7, 9)
+TIE1 = False
+GATE_AFTER = (11, 14)
 ALIGN = 256
 LISTS_AT = 0
 FIRST_TIE = False
@@ -78,10 +89,10 @@ def tile_moe_pkd_glu_sigmoid_kernel(
             turns[ring] = turn + 1
             return rings.tile(shape, dtype, name=ring, tag="%s%d" % (ring, turn % depth), align_bytes=ALIGN)
 
-        def bank_tile():
+        def bank_tile(back=0):
             turn = turns.get("bank", 0)
-            turns["bank"] = turn + 1
-            return psum.tile([P, BANK], F32, name="bank", tag="bank%d" % (turn % 8))
+            turns["bank"] = turn + (0 if back else 1)
+            return psum.tile([P, BANK], F32, name="bank", tag="bank%d" % ((turn - back) % 8))
 
         slot_list = keep.tile([P, S // 16], U16, name="slot_list")
         nc.sync.dma_start(slot_list[:], offs)
@@ -96,9 +107,10 @@ def tile_moe_pkd_glu_sigmoid_kernel(
             nc.scalar.dma_start(
                 token_scales[32 * q : 32 * q + 4 * PASSES, :], x_scales[:, 4 * q : 4 * q + 4, :].bitcast(I32)
             )
-        warm = keep.tile([P, 8], F32, name="warm")
-        nc.vector.memset(warm[:], 0.0)
-        nc.scalar.activation(warm[:], warm[:], SIGMOID)
+        if WARM:
+            warm = keep.tile([P, 8], F32, name="warm")
+            nc.vector.memset(warm[:], 0.0)
+            nc.scalar.activation(warm[:], warm[:], SIGMOID)
 
         slot_words, slot_scales = {}, {}
 
@@ -119,31 +131,43 @@ def tile_moe_pkd_glu_sigmoid_kernel(
         for e in range(E):
             gather_scales(e)
 
+        merged = []
+
         def quantise_first_layer_pass(w, e, a, vector_pairs, spare):
             chunk = turns.get("w_codes", 0)
             late = [x for x in WORDS_AFTER if WORDS_AFTER[x] == chunk]
             late_expert = late[0] if late else E
-            held = ring_tile("stream", STREAM_BUFS, [P, RAW + spare], F32)
-            raw = held[:, :RAW].rearrange("p (j c) -> p j c", j=PACK)
-            rows = w[e, a * K_PASS : (a + 1) * K_PASS, :]
+            rows = w[e, a * K_PASS : (a + 1) * K_PASS, :].rearrange("(p j) c -> p j c", j=PACK)
             if late_expert < E:
                 grouped = rings.tile([P, RAW], BF16, name="grouped", tag="late_words%d" % late_expert, align_bytes=ALIGN)
             else:
                 grouped = ring_tile("grouped", GROUPED_BUFS, [P, RAW], BF16)
             parts = LAST_PARTS if chunk == E * CHUNKS - 1 else 1
-            src = raw.rearrange("p j (m t) -> p m j t", t=PACK)
             dst = grouped[:].rearrange("p (t m j) -> p m j t", t=PACK, j=PACK)
+            width = H // parts
+            held = []
+            if MERGE_FROM <= chunk < MERGE_TO:
+                if a == 0:
+                    both = ring_tile("pairs", PAIR_BUFS, [P, PASSES * RAW], F32)
+                    nc.sync.dma_start(
+                        both[:].rearrange("p (o x) -> p o x", o=PASSES),
+                        w[e].rearrange("(o p j) c -> p o (j c)", o=PASSES, j=PACK),
+                    )
+                    merged.append(both)
+                held.append(merged[-1][:, a * RAW : (a + 1) * RAW])
+            else:
+                for part in range(parts):
+                    held.append(ring_tile("stream", STREAM_BUFS, [P, PACK * width], F32)[:])
+                    nc.sync.dma_start(held[part].rearrange("p (j c) -> p j c", j=PACK), rows[:, :, part * width : (part + 1) * width])
             for part in range(parts):
-                cols = slice(part * H // parts, (part + 1) * H // parts)
-                nc.sync.dma_start(raw[:, :, cols], rows.rearrange("(p j) c -> p j c", j=PACK)[:, :, cols])
-            for part in range(parts):
+                src = held[part].rearrange("p (j m t) -> p m j t", j=PACK, t=PACK)
                 ms = slice(part * P // parts, (part + 1) * P // parts)
-                for pair in (1, 0):
+                for pair in range(2):
                     planes = slice(2 * pair, 2 * pair + 2)
                     if pair < vector_pairs:
-                        nc.vector.tensor_copy(dst[:, ms, :, planes], src[:, ms, :, planes])
+                        nc.vector.tensor_copy(dst[:, ms, :, planes], src[:, :, :, planes])
                     else:
-                        nc.scalar.copy(dst[:, ms, :, planes], src[:, ms, :, planes])
+                        nc.scalar.copy(dst[:, ms, :, planes], src[:, :, :, planes])
             w_codes = ring_tile("w_codes", CODE_BUFS, [P, H], U32)
             w_scales = ring_tile("w_scales", CODE_BUFS, [P, H], U8)
             for part in range(parts):
@@ -190,7 +214,7 @@ def tile_moe_pkd_glu_sigmoid_kernel(
             return sig
 
         gates = [keep.tile([P, T], F32, name="gate%d" % r, align_bytes=ALIGN) for r in range(2)]
-        if PE_ADD:
+        if PE_ADD or TURNED:
             identity = keep.tile([P, P], F32, name="identity")
             make_identity(nc, identity[:])
         first_list = keep.tile([P, T // 16], U16, name="first_list")
@@ -211,6 +235,9 @@ def tile_moe_pkd_glu_sigmoid_kernel(
                 nc.sync.dma_start(
                     w2_raw[piece].rearrange("p (j c) -> p j c", j=PACK), rows.rearrange("(p j) c -> p j c", j=PACK)
                 )
+                if piece == LISTS_AFTER:
+                    nc.sync.dma_start(first_list[:], pos1)
+                    nc.sync.dma_start(second_list[:], pos2)
                 for r in range(2):
                     if GATE_AFTER[r] == piece:
                         nc.sync.dma_start(gates[r][:], gate[r, :P, :])
@@ -262,41 +289,38 @@ def tile_moe_pkd_glu_sigmoid_kernel(
                 vector_pairs = shares[c]
                 chunks.append(quantise_first_layer_pass(w, e, c % PASSES, vector_pairs, SIG if takes_sig else 0))
                 if c == 0 and owed:
-                    sig.append(sigmoid_into(chunks[c][2][:, RAW - 4 : RAW - 4 + SIG], pre[1]))
+                    sig.append(sigmoid_into(chunks[c][2][0][:, :SIG], pre[1]))
                 if e > 0 and c == MULTC:
                     h_bf = chunks[c][3] if MULT_TIE else ring_tile("h_bf", 2, [P, 2 * SIG], BF16)
                     for half in halves:
                         multiply_hidden(h_bf[:, half * SIG : (half + 1) * SIG], lin[half], sig[half])
                     quantise_hidden(e - 1, slice(0, C), h_bf[:, : 2 * SIG])
                 if c == CHUNKS - 1 and not last:
-                    held = chunks[c][2]
-                    sig = [sigmoid_into(held[:, RAW - 4 : RAW - 4 + SIG], pre[0])]
+                    held = chunks[c][2][0]
+                    sig = [sigmoid_into(held[:, SIG : 2 * SIG], pre[0])]
                     if vector_pairs == 0:
                         sig.append(sigmoid_into(held[:, :SIG], pre[1]))
-                if last and c == SIGL[0]:
-                    sig = [sigmoid_into(chunks[c][2][:, RAW - 4 : RAW - 4 + SIG], pre[0])]
-                if last and c == SIGL[1]:
-                    sig.append(sigmoid_into(chunks[c][2][:, RAW - 4 : RAW - 4 + SIG], pre[1]))
+                if last and c == CHUNKS - 1:
+                    sig = [sigmoid_into(chunks[c][2][SIGL[0]][:, :SIG], pre[0])]
+                    if SIGL[1] != 4:
+                        sig.append(sigmoid_into(chunks[c][2][SIGL[1]][:, SIG : 2 * SIG], pre[1]))
                 if c == W2_AFTER and e < N0_EARLY:
                     load_w2(e, e + 1)
                     round_w2(e, e + 1)
                     quantise_w2(0, e, e + 1)
-                if c == 1 and e == LISTS_AT:
-                    nc.sync.dma_start(first_list[:], pos1)
-                    nc.sync.dma_start(second_list[:], pos2)
                 if c == PASSES - 1:
                     pre = [first_layer_product(chunks[:PASSES], e, half) for half in halves]
             lin = [first_layer_product(chunks[PASSES:], e, half) for half in halves]
 
         ends = [E, 2 * E + LEAD, N_TILES * E]
-        load_w2(N0_EARLY, E)
+        first_tag = load_w2(N0_EARLY, E)
         w2_tags = [None] + [load_w2(ends[n], ends[n + 1]) for n in range(N_TILES - 1)]
         round_w2(N0_EARLY, E)
         if SIGL[1] == 4:
             sig.append(sigmoid_into(w2_raw[SIG_PIECE], pre[1]))
         for e0, e1 in GROUPS0:
             quantise_w2(0, e0, e1)
-        y = rings.tile([P, S], F32, name="y", tag="y0", align_bytes=ALIGN)
+        y = rings.tile([P, S], F32, name="y", tag=first_tag if Y0_TIE else "y0", align_bytes=ALIGN)
         for e0, e1 in EXPERT_GROUPS[:-1]:
             slot_results(0, y, e0, e1, all_slots)
         h_last = keep.tile([P, C * PACK], BF16, name="h_last", align_bytes=ALIGN)
@@ -319,10 +343,12 @@ def tile_moe_pkd_glu_sigmoid_kernel(
                         )
                 nc.scalar.copy(dst[:, c0:c1], bank[:, : c1 - c0])
 
-        later = []
+        later, weighted = [], []
+
         for n in range(N_TILES):
             last = n + 1 == N_TILES
-            parts = FINAL_PARTS if last else 1
+            cuts = FINAL_CUTS if last else (0, T)
+            parts = len(cuts) - 1
             if FIRST_TIE and n == 0:
                 round_w2(E, 2 * E)
                 for e0, e1 in GROUPS1:
@@ -332,9 +358,12 @@ def tile_moe_pkd_glu_sigmoid_kernel(
                 first = ring_tile("first", 3, [P, T], F32)
             total = ring_tile("total", 3, [P, T], F32)
             for part in range(parts):
-                cols = slice(part * T // parts, (part + 1) * T // parts)
+                cols = slice(cuts[part], cuts[part + 1])
                 entries = slice(cols.start // 16, cols.stop // 16)
-                nc.vector.tensor_tensor(first[:, cols], y[:].indirect(first_list[:, entries]), gates[0][:, cols], MULT)
+                if n in TURNED:
+                    nc.vector.tensor_copy(first[:, cols], y[:].indirect(first_list[:, entries]))
+                else:
+                    nc.vector.tensor_tensor(first[:, cols], y[:].indirect(first_list[:, entries]), gates[0][:, cols], MULT)
                 if not last:
                     round_w2(2 * E if FIRST_TIE and n == 0 else ends[n], ends[n + 1])
                     for e0, e1 in () if FIRST_TIE and n == 0 else (GROUPS1, GROUPS2)[n]:
@@ -345,6 +374,17 @@ def tile_moe_pkd_glu_sigmoid_kernel(
                 if part == 0:
                     tag = "second%d" % n if last or (n == 0 and (FIRST_TIE or not TIE0)) or (n == 1 and not TIE1) else "w2_grouped%d" % (n + 1)
                     second = rings.tile([P, T], F32, name="second", tag=tag, align_bytes=ALIGN)
+                if n in TURNED:
+                    nc.vector.tensor_copy(second[:, cols], y[:].indirect(second_list[:, entries]))
+                    blocks = [(term, b) for term in (first, second) for b in range(T // P)]
+                    turned = []
+                    for i, (term, b) in enumerate(blocks):
+                        if i % 4 == 0:
+                            bank = bank_tile(back=TURN_BACK - i // 4) if TURN_BACK else bank_tile()
+                        turned.append(bank[:, i % 4 * P : (i % 4 + 1) * P])
+                        nc.tensor.transpose(turned[i], term[:, b * P : (b + 1) * P], identity[:])
+                    weighted.append((n, turned, total))
+                    continue
                 nc.vector.tensor_tensor(second[:, cols], y[:].indirect(second_list[:, entries]), gates[1][:, cols], MULT)
                 if n in PE_ADD:
                     later.append((n, first, second, total))
@@ -353,7 +393,20 @@ def tile_moe_pkd_glu_sigmoid_kernel(
                 nc.sync.dma_start(out[n * P : (n + 1) * P, cols], total[:, cols])
             if not last:
                 y = next_y
+            if n == GATE_COLS_AT and TURNED:
+                gate_cols = keep.tile([P, 2 * T // P], F32, name="gate_cols")
+                bank = bank_tile()
+                for i in range(2 * T // P):
+                    r, b = divmod(i, T // P)
+                    nc.tensor.transpose(bank[:, 32 * i : 32 * i + P], gates[r][:, b * P : (b + 1) * P], identity[:])
+                nc.scalar.copy(gate_cols[:], bank[:, 0 : 32 * (2 * T // P) : 32])
             if n == N_TILES - 2:
+                for m, turned, total in weighted:
+                    scaled = rings.tile([P, 2 * T], F32, name="scaled", tag=SUM_TAGS[m], align_bytes=ALIGN)
+                    for i, block in enumerate(turned):
+                        nc.scalar.activation(scaled[:, i * P : (i + 1) * P], block, COPY, scale=gate_cols[:, i : i + 1])
+                    turn_blocks(total, [scaled[:, :T], scaled[:, T:]])
+                    nc.sync.dma_start(out[m * P : (m + 1) * P, :], total[:])
                 for m, first, second, total in later:
                     summed = rings.tile([P, T], F32, name="summed", tag=SUM_TAGS[m], align_bytes=ALIGN)
                     turn_blocks(summed, [first, second])

@@ -6,6 +6,7 @@ from concourse.masks import make_identity
 K, T, E, C, H, N = 1024, 640, 5, 256, 512, 384
 S = E * C
 FLOPS = 2 * S * (2 * K * H + H * N)
+BYTES = 4 * (2 * E * K * H + E * H * N + 2 * 128 * T + N * T) + K * T + K * T // 32 + 2 * 128 * (S + 2 * T) // 16
 
 F32 = mybir.dt.float32
 BF16 = mybir.dt.bfloat16
@@ -17,61 +18,34 @@ FP8X4 = mybir.dt.float8_e4m3fn_x4
 MULT = mybir.AluOpType.mult
 ADD = mybir.AluOpType.add
 SIGMOID = mybir.ActivationFunctionType.Sigmoid
+COPY = mybir.ActivationFunctionType.Copy
 
 P = 128
 PACK = 4
-K_PASS = P * PACK
-PASSES = K // K_PASS
+PASSES = K // (P * PACK)
 CHUNKS = 2 * PASSES
-HALF = 128
+LAST_CHUNK = E * CHUNKS - 1
+RAW = PACK * H
+PIECE = PACK * P
+HALF = C // 2
 BANK = 512
 N_TILES = N // P
-PIECE = PACK * P
-STREAM_BUFS = 10
-GROUPED_BUFS = 5
-CODE_BUFS = 6
-LEAD = 1
-VP0 = (0, 0, 1, 0)
-VP = (2, 0, 2, 0)
-VP3 = (2, 0, 1, 1)
-VPL = (1, 1, 1, 1)
-SIGL = (1, 4)
-WARM = False
-TURNED = (0,)
-TURN_BACK = 3
-GATE_COLS_AT = 1
-COPY = mybir.ActivationFunctionType.Copy
-Y0_TIE = False
-MERGE_FROM = 2
-MERGE_TO = 0
-PAIR_BUFS = 4
-LISTS_AFTER = 7
-FINAL_CUTS = (0, 384, 640)
-MULT_TIE = False
-TIE1 = False
-GATE_AFTER = (11, 14)
+LIST_COLUMN = 16
 ALIGN = 256
-LISTS_AT = 0
-FIRST_TIE = False
-GROUPS1 = ((0, 2), (2, 4), (4, 5))
-GROUPS2 = ((0, 2), (2, 4), (4, 5))
-MULTC = 0
-WORDS_AFTER = {2: 0, 3: 1, 4: 2}
-ON_V = (0, 1, 5, 6, 7)
-SIG_PIECE = 2
-W2_AFTER = 1
-N0_EARLY = 0
-TIE0 = True
-LAST_PARTS = 2
-H_TIE = (None, None)
-PE_ADD = ()
-SUM_TAGS = ("w2_codes2", "w2_scales2")
-GROUPS0 = ((0, 2), (2, 4), (4, 5))
+
+TOKEN_BLOCKS = T // P
+BANKS = 8
+
+SHARED_FROM = LAST_CHUNK - 5
 EARLY_EXPERTS = 2
-RAW = PACK * H
-SIG = PACK * HALF
-FINAL_PARTS = 2
+VECTOR_PIECES = (2, 3, 0)
+LEAD = 1
 EXPERT_GROUPS = ((0, 2), (2, 4), (4, 5))
+LAST_CUT = 384
+
+STREAM_BUFS = 10
+ROUNDED_BUFS = 5
+CODE_BUFS = 6
 
 
 def tile_moe_pkd_glu_sigmoid_kernel(
@@ -84,184 +58,208 @@ def tile_moe_pkd_glu_sigmoid_kernel(
         psum = ctx.enter_context(tc.psum_pool(name="psum", bufs=1))
         turns = {}
 
-        def ring_tile(ring, depth, shape, dtype):
+        def next_tag(ring, depth):
             turn = turns.get(ring, 0)
             turns[ring] = turn + 1
-            return rings.tile(shape, dtype, name=ring, tag="%s%d" % (ring, turn % depth), align_bytes=ALIGN)
+            return "%s%d" % (ring, turn % depth)
 
-        def bank_tile(back=0):
-            turn = turns.get("bank", 0)
-            turns["bank"] = turn + (0 if back else 1)
-            return psum.tile([P, BANK], F32, name="bank", tag="bank%d" % ((turn - back) % 8))
+        def tile_on(tag, shape, dtype):
+            return rings.tile(shape, dtype, name="tile", tag=tag, align_bytes=ALIGN)
 
-        slot_list = keep.tile([P, S // 16], U16, name="slot_list")
+        def bank_on(tag):
+            return psum.tile([P, BANK], F32, name="bank", tag=tag)
+
+        def bank_tile():
+            return bank_on(next_tag("bank", BANKS))
+
+        slot_list = keep.tile([P, S // LIST_COLUMN], U16, name="slot_list")
         nc.sync.dma_start(slot_list[:], offs)
         token_scales = keep.tile([P, T // 4], I32, name="token_scales", align_bytes=ALIGN)
         nc.vector.memset(token_scales[:], 0)
         token_words = []
-        for a in range(PASSES):
-            words = keep.tile([P, T], I32, name="token_words%d" % a, align_bytes=ALIGN)
-            nc.sync.dma_start(words[:], x_words[a].rearrange("p t r -> p (t r)").bitcast(I32))
-            token_words.append(words)
+        for o in range(PASSES):
+            token_words.append(keep.tile([P, T], I32, name="token_words%d" % o, align_bytes=ALIGN))
+            nc.sync.dma_start(token_words[o][:], x_words[o].rearrange("p t r -> p (t r)").bitcast(I32))
         for q in range(4):
             nc.scalar.dma_start(
                 token_scales[32 * q : 32 * q + 4 * PASSES, :], x_scales[:, 4 * q : 4 * q + 4, :].bitcast(I32)
             )
-        if WARM:
-            warm = keep.tile([P, 8], F32, name="warm")
-            nc.vector.memset(warm[:], 0.0)
-            nc.scalar.activation(warm[:], warm[:], SIGMOID)
+
+        warm = keep.tile([P, 8], F32, name="warm")
+        nc.vector.memset(warm[:], 0.0)
+        nc.scalar.activation(warm[:], warm[:], SIGMOID)
 
         slot_words, slot_scales = {}, {}
 
-        def gather_words(e, tag):
-            offsets = slot_list[:, e * C // 16 : (e + 1) * C // 16]
-            words = rings.tile([P, PASSES * C], U32, name="slot_words", tag=tag, align_bytes=ALIGN)
-            for a in range(PASSES):
-                nc.vector.tensor_copy(words[:, a * C : (a + 1) * C], token_words[a][:].bitcast(U32).indirect(offsets))
-            slot_words[e] = words
+        def expert_offsets(e):
+            return slot_list[:, e * C // LIST_COLUMN : (e + 1) * C // LIST_COLUMN]
 
-        def gather_scales(e):
-            offsets = slot_list[:, e * C // 16 : (e + 1) * C // 16]
-            slot_scales[e] = keep.tile([P, C], U8, name="slot_scales%d" % e, align_bytes=ALIGN)
-            nc.vector.tensor_copy(slot_scales[e][:], token_scales[:].bitcast(U8).indirect(offsets))
+        def gather_words(e):
+            slot_words[e] = tile_on("words%d" % e, [P, PASSES * C], U32)
+            for o in range(PASSES):
+                window = token_words[o][:].bitcast(U32)
+                nc.vector.tensor_copy(slot_words[e][:, o * C : (o + 1) * C], window.indirect(expert_offsets(e)))
 
         for e in range(EARLY_EXPERTS):
-            gather_words(e, "early_words%d" % e)
+            gather_words(e)
         for e in range(E):
-            gather_scales(e)
+            slot_scales[e] = keep.tile([P, C], U8, name="slot_scales%d" % e, align_bytes=ALIGN)
+            nc.vector.tensor_copy(slot_scales[e][:], token_scales[:].bitcast(U8).indirect(expert_offsets(e)))
 
-        merged = []
+        def vector_planes(chunk):
+            if chunk >= SHARED_FROM:
+                return PACK // 2
+            if chunk % PASSES > 0 or chunk == 0:
+                return 0
+            if chunk < CHUNKS:
+                return PACK // 2
+            return PACK
 
-        def quantise_first_layer_pass(w, e, a, vector_pairs, spare):
-            chunk = turns.get("w_codes", 0)
-            late = [x for x in WORDS_AFTER if WORDS_AFTER[x] == chunk]
-            late_expert = late[0] if late else E
-            rows = w[e, a * K_PASS : (a + 1) * K_PASS, :].rearrange("(p j) c -> p j c", j=PACK)
-            if late_expert < E:
-                grouped = rings.tile([P, RAW], BF16, name="grouped", tag="late_words%d" % late_expert, align_bytes=ALIGN)
-            else:
-                grouped = ring_tile("grouped", GROUPED_BUFS, [P, RAW], BF16)
-            parts = LAST_PARTS if chunk == E * CHUNKS - 1 else 1
-            dst = grouped[:].rearrange("p (t m j) -> p m j t", t=PACK, j=PACK)
-            width = H // parts
-            held = []
-            if MERGE_FROM <= chunk < MERGE_TO:
-                if a == 0:
-                    both = ring_tile("pairs", PAIR_BUFS, [P, PASSES * RAW], F32)
-                    nc.sync.dma_start(
-                        both[:].rearrange("p (o x) -> p o x", o=PASSES),
-                        w[e].rearrange("(o p j) c -> p o (j c)", o=PASSES, j=PACK),
-                    )
-                    merged.append(both)
-                held.append(merged[-1][:, a * RAW : (a + 1) * RAW])
-            else:
-                for part in range(parts):
-                    held.append(ring_tile("stream", STREAM_BUFS, [P, PACK * width], F32)[:])
-                    nc.sync.dma_start(held[part].rearrange("p (j c) -> p j c", j=PACK), rows[:, :, part * width : (part + 1) * width])
-            for part in range(parts):
-                src = held[part].rearrange("p (j m t) -> p m j t", j=PACK, t=PACK)
-                ms = slice(part * P // parts, (part + 1) * P // parts)
-                for pair in range(2):
-                    planes = slice(2 * pair, 2 * pair + 2)
-                    if pair < vector_pairs:
-                        nc.vector.tensor_copy(dst[:, ms, :, planes], src[:, :, :, planes])
-                    else:
-                        nc.scalar.copy(dst[:, ms, :, planes], src[:, :, :, planes])
-            w_codes = ring_tile("w_codes", CODE_BUFS, [P, H], U32)
-            w_scales = ring_tile("w_scales", CODE_BUFS, [P, H], U8)
-            for part in range(parts):
-                words = slice(part * H // parts, (part + 1) * H // parts)
+        def load_chunk(chunk):
+            e, c = divmod(chunk, CHUNKS)
+            w, o = (w1, w3)[c // PASSES], c % PASSES
+            rows = w[e, o * P * PACK : (o + 1) * P * PACK, :].rearrange("(p j) c -> p j c", j=PACK)
+            width = H // 2 if chunk == LAST_CHUNK else H
+            parts = []
+            for c0 in range(0, H, width):
+                parts.append(tile_on(next_tag("stream", STREAM_BUFS), [P, PACK * width], F32)[:])
+                nc.sync.dma_start(parts[-1].rearrange("p (j c) -> p j c", j=PACK), rows[:, :, c0 : c0 + width])
+            return parts
+
+        def quantise_chunk(chunk):
+            late = EARLY_EXPERTS + chunk
+            tag = "words%d" % late if late < E else next_tag("rounded", ROUNDED_BUFS)
+            rounded = tile_on(tag, [P, RAW], BF16)
+            parts = load_chunk(chunk)
+            dst = rounded[:].rearrange("p (t m j) -> p m j t", t=PACK, j=PACK)
+            for n_part, part in enumerate(parts):
+                src = part.rearrange("p (j m t) -> p m j t", j=PACK, t=PACK)
+                ms = slice(n_part * P // len(parts), (n_part + 1) * P // len(parts))
+                for t0 in range(0, PACK, 2):
+                    copy = nc.vector.tensor_copy if t0 < vector_planes(chunk) else nc.scalar.copy
+                    copy(dst[:, ms, :, t0 : t0 + 2], src[:, :, :, t0 : t0 + 2])
+            codes = tile_on(next_tag("codes", CODE_BUFS), [P, H], U32)
+            scales = tile_on(next_tag("scales", CODE_BUFS), [P, H], U8)
+            step = H // len(parts)
+            for w0 in range(0, H, step):
                 nc.vector.quantize_mx(
-                    out=w_codes[:, words].bitcast(FP8X4),
-                    scales=w_scales[:, words],
-                    in_=grouped[:, words.start * PACK : words.stop * PACK],
+                    out=codes[:, w0 : w0 + step].bitcast(FP8X4),
+                    scales=scales[:, w0 : w0 + step],
+                    in_=rounded[:, w0 * PACK : (w0 + step) * PACK],
                 )
-            if late_expert < E:
-                gather_words(late_expert, "late_words%d" % late_expert)
-            return w_codes, w_scales, held, grouped
+            if late < E:
+                gather_words(late)
+            return codes, scales, parts
 
-        def first_layer_product(weights, e, half):
-            slots = slice(half * HALF, (half + 1) * HALF)
+        halves = range(C // HALF)
+
+        def half_slots(half):
+            return slice(half * HALF, (half + 1) * HALF)
+
+        def first_layer_product(passes, e, half):
             bank = bank_tile()
             for t in range(PACK):
                 cols = slice(t * P, (t + 1) * P)
-                for a in range(PASSES):
+                for o, (codes, scales, parts) in enumerate(passes):
                     nc.tensor.matmul_mx(
                         out=bank[:, t * HALF : (t + 1) * HALF],
-                        lhsT=weights[a][0][:, cols].bitcast(FP8X4),
-                        lhsT_scale=weights[a][1][:, cols],
-                        rhs=slot_words[e][:, a * C + half * HALF : a * C + (half + 1) * HALF].bitcast(FP8X4),
-                        rhs_scale=slot_scales[e][4 * a :, slots],
-                        start=(a == 0),
-                        stop=(a == PASSES - 1),
+                        lhsT=codes[:, cols].bitcast(FP8X4),
+                        lhsT_scale=scales[:, cols],
+                        rhs=slot_words[e][:, o * C + half * HALF : o * C + (half + 1) * HALF].bitcast(FP8X4),
+                        rhs_scale=slot_scales[e][4 * o :, half_slots(half)],
+                        start=(o == 0),
+                        stop=(o == PASSES - 1),
                     )
             return bank[:].rearrange("p (t s) -> p s t", t=PACK)
 
-        halves = range(C // HALF)
-        h_codes = [keep.tile([P, C], U32, name="h_codes%d" % e, align_bytes=ALIGN) for e in range(E)]
-        h_scales = [keep.tile([P, C], U8, name="h_scales%d" % e, align_bytes=ALIGN) for e in range(E)]
-
-        def multiply_hidden(h_bf, lin, sig):
-            nc.vector.tensor_tensor(h_bf.rearrange("p (s t) -> p s t", t=PACK), lin, sig, MULT)
-
-        def quantise_hidden(e, slots, h_bf):
-            nc.vector.quantize_mx(out=h_codes[e][:, slots].bitcast(FP8X4), scales=h_scales[e][:, slots], in_=h_bf)
-
-        def sigmoid_into(spent, pre):
+        def sigmoid_onto(spent, pre):
             sig = spent.rearrange("p (s t) -> p s t", t=PACK)
             nc.scalar.activation(sig, pre, SIGMOID)
             return sig
 
-        gates = [keep.tile([P, T], F32, name="gate%d" % r, align_bytes=ALIGN) for r in range(2)]
-        if PE_ADD or TURNED:
-            identity = keep.tile([P, P], F32, name="identity")
-            make_identity(nc, identity[:])
-        first_list = keep.tile([P, T // 16], U16, name="first_list")
-        second_list = keep.tile([P, T // 16], U16, name="second_list")
+        h_codes = [keep.tile([P, C], U32, name="h_codes%d" % e, align_bytes=ALIGN) for e in range(E)]
+        h_scales = [keep.tile([P, C], U8, name="h_scales%d" % e, align_bytes=ALIGN) for e in range(E)]
 
-        w2_raw = {}
-        w2_grouped = [rings.tile([P, E * PIECE], BF16, name="w2_grouped", tag="w2_grouped%d" % n, align_bytes=ALIGN) for n in range(N_TILES)]
-        w2_codes = [rings.tile([P, E * P], U32, name="w2_codes", tag="w2_codes%d" % n, align_bytes=ALIGN) for n in range(N_TILES)]
-        w2_scales = [rings.tile([P, E * P], U8, name="w2_scales", tag="w2_scales%d" % n, align_bytes=ALIGN) for n in range(N_TILES)]
+        def hidden_values(h_bf, lin, sig):
+            for half in halves:
+                h_half = h_bf[:, half * BANK : (half + 1) * BANK].rearrange("p (s t) -> p s t", t=PACK)
+                nc.vector.tensor_tensor(h_half, lin[half], sig[half], MULT)
 
-        def load_w2(first_piece, end_piece):
-            tag = "stream%d" % (turns["stream"] % STREAM_BUFS)
-            held = ring_tile("stream", STREAM_BUFS, [P, (end_piece - first_piece) * PIECE], F32)
-            for piece in range(first_piece, end_piece):
-                n, e = divmod(piece, E)
-                w2_raw[piece] = held[:, (piece - first_piece) * PIECE : (piece - first_piece + 1) * PIECE]
-                rows = w2[e, :, n * P : (n + 1) * P]
-                nc.sync.dma_start(
-                    w2_raw[piece].rearrange("p (j c) -> p j c", j=PACK), rows.rearrange("(p j) c -> p j c", j=PACK)
-                )
-                if piece == LISTS_AFTER:
-                    nc.sync.dma_start(first_list[:], pos1)
-                    nc.sync.dma_start(second_list[:], pos2)
-                for r in range(2):
-                    if GATE_AFTER[r] == piece:
-                        nc.sync.dma_start(gates[r][:], gate[r, :P, :])
-            return tag
-
-        def round_w2(first_piece, end_piece):
-            for piece in range(first_piece, end_piece):
-                n, e = divmod(piece, E)
-                dst = w2_grouped[n][:, e * PIECE : (e + 1) * PIECE].rearrange("p (c i j) -> p c j i", i=4, j=PACK)
-                src = w2_raw[piece].rearrange("p (j c i) -> p c j i", i=4, j=PACK)
-                if piece in ON_V:
-                    nc.vector.tensor_copy(dst, src)
-                else:
-                    nc.scalar.copy(dst, src)
-
-        def quantise_w2(n, e0, e1):
+        def quantise_hidden(e, slots, h_bf):
             nc.vector.quantize_mx(
-                out=w2_codes[n][:, e0 * P : e1 * P].bitcast(FP8X4),
-                scales=w2_scales[n][:, e0 * P : e1 * P],
-                in_=w2_grouped[n][:, e0 * PIECE : e1 * PIECE],
+                out=h_codes[e][:, slots].bitcast(FP8X4),
+                scales=h_scales[e][:, slots],
+                in_=h_bf[:, slots.start * PACK : slots.stop * PACK],
             )
 
+        gates = [keep.tile([P, T], F32, name="gate%d" % r, align_bytes=ALIGN) for r in range(2)]
+        identity = keep.tile([P, P], F32, name="identity")
+        make_identity(nc, identity[:])
+        first_list = keep.tile([P, T // LIST_COLUMN], U16, name="first_list")
+        second_list = keep.tile([P, T // LIST_COLUMN], U16, name="second_list")
+        w2_rounded = [tile_on("w2_rounded%d" % n, [P, E * PIECE], BF16) for n in range(N_TILES)]
+        w2_codes = [tile_on("w2_codes%d" % n, [P, E * P], U32) for n in range(N_TILES)]
+        w2_scales = [tile_on("w2_scales%d" % n, [P, E * P], U8) for n in range(N_TILES)]
+
+        all_slots = slice(0, C)
+        for e in range(E):
+            done = []
+            for c in range(CHUNKS):
+                chunk = e * CHUNKS + c
+                done.append(quantise_chunk(chunk))
+                spent = done[c][2][-1]
+                if c == 0 and e > 0:
+                    if len(sig) == 1:
+                        sig.append(sigmoid_onto(spent[:, :BANK], pre[1]))
+                    h_bf = tile_on(next_tag("h_bf", 2), [P, C * PACK], BF16)
+                    hidden_values(h_bf, lin, sig)
+                    quantise_hidden(e - 1, all_slots, h_bf)
+                if c == PASSES - 1:
+                    pre = [first_layer_product(done[:PASSES], e, half) for half in halves]
+            sig = [sigmoid_onto(spent[:, :BANK] if chunk == LAST_CHUNK else spent[:, BANK : 2 * BANK], pre[0])]
+            if vector_planes(chunk) == 0:
+                sig.append(sigmoid_onto(spent[:, :BANK], pre[1]))
+            lin = [first_layer_product(done[PASSES:], e, half) for half in halves]
+
+        ends = (E, 2 * E + LEAD, N_TILES * E)
+        pieces, piece_tags = [], []
+        for n in range(N_TILES):
+            piece_tags.append(next_tag("stream", STREAM_BUFS))
+            held = tile_on(piece_tags[n], [P, (ends[n] - len(pieces)) * PIECE], F32)
+            for place, number in enumerate(range(len(pieces), ends[n])):
+                tile_n, e = divmod(number, E)
+                pieces.append(held[:, place * PIECE : (place + 1) * PIECE])
+                nc.sync.dma_start(
+                    pieces[number].rearrange("p (j c) -> p j c", j=PACK),
+                    w2[e, :, tile_n * P : (tile_n + 1) * P].rearrange("(p j) c -> p j c", j=PACK),
+                )
+                if number == E + VECTOR_PIECES[1] - 1:
+                    nc.sync.dma_start(first_list[:], pos1)
+                    nc.sync.dma_start(second_list[:], pos2)
+                if number == ends[1]:
+                    nc.sync.dma_start(gates[0][:], gate[0, :P, :])
+                if number == ends[2] - 1:
+                    nc.sync.dma_start(gates[1][:], gate[1, :P, :])
+
+        def round_pieces(numbers):
+            for number in numbers:
+                n, e = divmod(number, E)
+                dst = w2_rounded[n][:, e * PIECE : (e + 1) * PIECE].rearrange("p (c i j) -> p c j i", i=4, j=PACK)
+                src = pieces[number].rearrange("p (j c i) -> p c j i", i=4, j=PACK)
+                copy = nc.vector.tensor_copy if e < VECTOR_PIECES[n] else nc.scalar.copy
+                copy(dst, src)
+
+        def quantise_pieces(n):
+            for e0, e1 in EXPERT_GROUPS:
+                nc.vector.quantize_mx(
+                    out=w2_codes[n][:, e0 * P : e1 * P].bitcast(FP8X4),
+                    scales=w2_scales[n][:, e0 * P : e1 * P],
+                    in_=w2_rounded[n][:, e0 * PIECE : e1 * PIECE],
+                )
+
         def slot_results(n, y, e0, e1, slots):
-            bank = bank_tile()
+            tag = next_tag("bank", BANKS)
+            bank = bank_on(tag)
             width = slots.stop - slots.start
             for e in range(e0, e1):
                 nc.tensor.matmul_mx(
@@ -275,140 +273,95 @@ def tile_moe_pkd_glu_sigmoid_kernel(
                 )
             first_slot = e0 * C + slots.start
             nc.scalar.copy(y[:, first_slot : first_slot + (e1 - e0) * width], bank[:, : (e1 - e0) * width])
+            return tag
 
-        all_slots = slice(0, C)
-        half_slots = [slice(half * HALF, (half + 1) * HALF) for half in halves]
-        for e in range(E):
-            chunks = []
-            last = e == E - 1
-            for c in range(CHUNKS):
-                w = w1 if c < PASSES else w3
-                shares = VP0 if e == 0 else VPL if last else VP3 if e == E - 2 else VP
-                owed = e > 0 and len(sig) == 1
-                takes_sig = (c in SIGL if last else c == CHUNKS - 1) or (c == 0 and owed)
-                vector_pairs = shares[c]
-                chunks.append(quantise_first_layer_pass(w, e, c % PASSES, vector_pairs, SIG if takes_sig else 0))
-                if c == 0 and owed:
-                    sig.append(sigmoid_into(chunks[c][2][0][:, :SIG], pre[1]))
-                if e > 0 and c == MULTC:
-                    h_bf = chunks[c][3] if MULT_TIE else ring_tile("h_bf", 2, [P, 2 * SIG], BF16)
-                    for half in halves:
-                        multiply_hidden(h_bf[:, half * SIG : (half + 1) * SIG], lin[half], sig[half])
-                    quantise_hidden(e - 1, slice(0, C), h_bf[:, : 2 * SIG])
-                if c == CHUNKS - 1 and not last:
-                    held = chunks[c][2][0]
-                    sig = [sigmoid_into(held[:, SIG : 2 * SIG], pre[0])]
-                    if vector_pairs == 0:
-                        sig.append(sigmoid_into(held[:, :SIG], pre[1]))
-                if last and c == CHUNKS - 1:
-                    sig = [sigmoid_into(chunks[c][2][SIGL[0]][:, :SIG], pre[0])]
-                    if SIGL[1] != 4:
-                        sig.append(sigmoid_into(chunks[c][2][SIGL[1]][:, SIG : 2 * SIG], pre[1]))
-                if c == W2_AFTER and e < N0_EARLY:
-                    load_w2(e, e + 1)
-                    round_w2(e, e + 1)
-                    quantise_w2(0, e, e + 1)
-                if c == PASSES - 1:
-                    pre = [first_layer_product(chunks[:PASSES], e, half) for half in halves]
-            lin = [first_layer_product(chunks[PASSES:], e, half) for half in halves]
-
-        ends = [E, 2 * E + LEAD, N_TILES * E]
-        first_tag = load_w2(N0_EARLY, E)
-        w2_tags = [None] + [load_w2(ends[n], ends[n + 1]) for n in range(N_TILES - 1)]
-        round_w2(N0_EARLY, E)
-        if SIGL[1] == 4:
-            sig.append(sigmoid_into(w2_raw[SIG_PIECE], pre[1]))
-        for e0, e1 in GROUPS0:
-            quantise_w2(0, e0, e1)
-        y = rings.tile([P, S], F32, name="y", tag=first_tag if Y0_TIE else "y0", align_bytes=ALIGN)
+        round_pieces(range(E))
+        sig.append(sigmoid_onto(pieces[VECTOR_PIECES[0]], pre[1]))
+        quantise_pieces(0)
+        y = tile_on("y0", [P, S], F32)
         for e0, e1 in EXPERT_GROUPS[:-1]:
             slot_results(0, y, e0, e1, all_slots)
-        h_last = keep.tile([P, C * PACK], BF16, name="h_last", align_bytes=ALIGN)
-        h_halves = [h_last[:, half * SIG : (half + 1) * SIG] if H_TIE[half] is None else w2_grouped[0][:, H_TIE[half] * PIECE : (H_TIE[half] + 1) * PIECE] for half in halves]
+        h_bf = keep.tile([P, C * PACK], BF16, name="h_last", align_bytes=ALIGN)
+        hidden_values(h_bf, lin, sig)
         for half in halves:
-            multiply_hidden(h_halves[half], lin[half], sig[half])
+            quantise_hidden(E - 1, half_slots(half), h_bf)
         for half in halves:
-            quantise_hidden(E - 1, half_slots[half], h_halves[half])
-        for half in halves:
-            slot_results(0, y, E - 1, E, slice(half * HALF, (half + 1) * HALF))
-        def turn_blocks(dst, terms):
-            for c0 in range(0, T, BANK):
-                c1 = min(c0 + BANK, T)
-                bank = bank_tile()
-                for b in range(c0, c1, P):
-                    for i, term in enumerate(terms):
-                        nc.tensor.matmul(
-                            bank[:, b - c0 : b - c0 + P], term[:, b : b + P], identity[:],
-                            start=(i == 0), stop=(i == len(terms) - 1), is_transpose=True,
-                        )
-                nc.scalar.copy(dst[:, c0:c1], bank[:, : c1 - c0])
+            slot_results(0, y, E - 1, E, half_slots(half))
 
-        later, weighted = [], []
+        def entries(inverse_list, cols):
+            return inverse_list[:, cols.start // LIST_COLUMN : cols.stop // LIST_COLUMN]
 
-        for n in range(N_TILES):
-            last = n + 1 == N_TILES
-            cuts = FINAL_CUTS if last else (0, T)
-            parts = len(cuts) - 1
-            if FIRST_TIE and n == 0:
-                round_w2(E, 2 * E)
-                for e0, e1 in GROUPS1:
-                    quantise_w2(1, e0, e1)
-                first = rings.tile([P, T], F32, name="first", tag="w2_grouped1", align_bytes=ALIGN)
-            else:
-                first = ring_tile("first", 3, [P, T], F32)
-            total = ring_tile("total", 3, [P, T], F32)
-            for part in range(parts):
-                cols = slice(cuts[part], cuts[part + 1])
-                entries = slice(cols.start // 16, cols.stop // 16)
-                if n in TURNED:
-                    nc.vector.tensor_copy(first[:, cols], y[:].indirect(first_list[:, entries]))
-                else:
-                    nc.vector.tensor_tensor(first[:, cols], y[:].indirect(first_list[:, entries]), gates[0][:, cols], MULT)
-                if not last:
-                    round_w2(2 * E if FIRST_TIE and n == 0 else ends[n], ends[n + 1])
-                    for e0, e1 in () if FIRST_TIE and n == 0 else (GROUPS1, GROUPS2)[n]:
-                        quantise_w2(n + 1, e0, e1)
-                    next_y = rings.tile([P, S], F32, name="y", tag=w2_tags[n + 1], align_bytes=ALIGN)
-                    for e0, e1 in EXPERT_GROUPS:
-                        slot_results(n + 1, next_y, e0, e1, all_slots)
-                if part == 0:
-                    tag = "second%d" % n if last or (n == 0 and (FIRST_TIE or not TIE0)) or (n == 1 and not TIE1) else "w2_grouped%d" % (n + 1)
-                    second = rings.tile([P, T], F32, name="second", tag=tag, align_bytes=ALIGN)
-                if n in TURNED:
-                    nc.vector.tensor_copy(second[:, cols], y[:].indirect(second_list[:, entries]))
-                    blocks = [(term, b) for term in (first, second) for b in range(T // P)]
-                    turned = []
-                    for i, (term, b) in enumerate(blocks):
-                        if i % 4 == 0:
-                            bank = bank_tile(back=TURN_BACK - i // 4) if TURN_BACK else bank_tile()
-                        turned.append(bank[:, i % 4 * P : (i % 4 + 1) * P])
-                        nc.tensor.transpose(turned[i], term[:, b * P : (b + 1) * P], identity[:])
-                    weighted.append((n, turned, total))
-                    continue
-                nc.vector.tensor_tensor(second[:, cols], y[:].indirect(second_list[:, entries]), gates[1][:, cols], MULT)
-                if n in PE_ADD:
-                    later.append((n, first, second, total))
-                    continue
-                nc.vector.tensor_tensor(total[:, cols], first[:, cols], second[:, cols], ADD)
-                nc.sync.dma_start(out[n * P : (n + 1) * P, cols], total[:, cols])
-            if not last:
-                y = next_y
-            if n == GATE_COLS_AT and TURNED:
-                gate_cols = keep.tile([P, 2 * T // P], F32, name="gate_cols")
-                bank = bank_tile()
-                for i in range(2 * T // P):
-                    r, b = divmod(i, T // P)
-                    nc.tensor.transpose(bank[:, 32 * i : 32 * i + P], gates[r][:, b * P : (b + 1) * P], identity[:])
-                nc.scalar.copy(gate_cols[:], bank[:, 0 : 32 * (2 * T // P) : 32])
-            if n == N_TILES - 2:
-                for m, turned, total in weighted:
-                    scaled = rings.tile([P, 2 * T], F32, name="scaled", tag=SUM_TAGS[m], align_bytes=ALIGN)
-                    for i, block in enumerate(turned):
-                        nc.scalar.activation(scaled[:, i * P : (i + 1) * P], block, COPY, scale=gate_cols[:, i : i + 1])
-                    turn_blocks(total, [scaled[:, :T], scaled[:, T:]])
-                    nc.sync.dma_start(out[m * P : (m + 1) * P, :], total[:])
-                for m, first, second, total in later:
-                    summed = rings.tile([P, T], F32, name="summed", tag=SUM_TAGS[m], align_bytes=ALIGN)
-                    turn_blocks(summed, [first, second])
-                    turn_blocks(total, [summed])
-                    nc.sync.dma_start(out[m * P : (m + 1) * P, :], total[:])
+        def gated(result, y, inverse_list, gate_tile, cols):
+            nc.vector.tensor_tensor(result[:, cols], y[:].indirect(entries(inverse_list, cols)), gate_tile[:, cols], MULT)
+
+        def add_and_store(n, total, first, second, cols):
+            nc.vector.tensor_tensor(total[:, cols], first[:, cols], second[:, cols], ADD)
+            nc.sync.dma_start(out[n * P : (n + 1) * P, cols], total[:, cols])
+
+        def make_y(n):
+            round_pieces(range(ends[n - 1], ends[n]))
+            quantise_pieces(n)
+            y = tile_on(piece_tags[n], [P, S], F32)
+            return y, [slot_results(n, y, e0, e1, all_slots) for e0, e1 in EXPERT_GROUPS]
+
+        def token_block(tile, b):
+            return tile[:, b * P : (b + 1) * P]
+
+        all_tokens = slice(0, T)
+        firsts = [tile_on("first0", [P, T], F32)]
+        totals = [tile_on("total0", [P, T], F32)]
+
+        nc.vector.tensor_copy(firsts[0][:], y[:].indirect(first_list[:]))
+        middle_y, middle_banks = make_y(1)
+        second = tile_on("w2_rounded1", [P, T], F32)
+        nc.vector.tensor_copy(second[:], y[:].indirect(second_list[:]))
+        turned = []
+        for term in (firsts[0], second):
+            for b in range(TOKEN_BLOCKS):
+                place = len(turned) % (BANK // P)
+                if place == 0:
+                    bank = bank_on(middle_banks[len(turned) // (BANK // P)])
+                turned.append(token_block(bank, place))
+                nc.tensor.transpose(turned[-1], token_block(term, b), identity[:])
+
+        firsts.append(tile_on("first1", [P, T], F32))
+        totals.append(tile_on("total1", [P, T], F32))
+        gated(firsts[1], middle_y, first_list, gates[0], all_tokens)
+        last_y, last_banks = make_y(2)
+        second = tile_on("second1", [P, T], F32)
+        gated(second, middle_y, second_list, gates[1], all_tokens)
+        add_and_store(1, totals[1], firsts[1], second, all_tokens)
+
+        gate_cols = keep.tile([P, 2 * TOKEN_BLOCKS], F32, name="gate_cols")
+        for r in range(2):
+            bank = bank_tile()
+            for b in range(TOKEN_BLOCKS):
+                nc.tensor.transpose(bank[:, 32 * b : 32 * b + P], token_block(gates[r], b), identity[:])
+            nc.scalar.copy(gate_cols[:, r * TOKEN_BLOCKS : (r + 1) * TOKEN_BLOCKS], bank[:, 0 : 32 * TOKEN_BLOCKS : 32])
+        scaled = tile_on("w2_codes2", [P, 2 * T], F32)
+        for b in range(TOKEN_BLOCKS):
+            for i in (b, TOKEN_BLOCKS + b):
+                nc.scalar.activation(token_block(scaled, i), turned[i], COPY, scale=gate_cols[:, i : i + 1])
+        for c0 in range(0, T, BANK):
+            c1 = min(c0 + BANK, T)
+            bank = bank_on(last_banks[c0 // BANK])
+            for b in range(c0 // P, c1 // P):
+                for r in range(2):
+                    nc.tensor.matmul(
+                        token_block(bank, b - c0 // P),
+                        token_block(scaled, r * TOKEN_BLOCKS + b),
+                        identity[:],
+                        start=(r == 0),
+                        stop=(r == 1),
+                        is_transpose=True,
+                    )
+            nc.scalar.copy(totals[0][:, c0:c1], bank[:, : c1 - c0])
+        nc.sync.dma_start(out[:P, :], totals[0][:])
+
+        first = tile_on("first2", [P, T], F32)
+        total = tile_on("total2", [P, T], F32)
+        second = tile_on("second2", [P, T], F32)
+        for cols in (slice(0, LAST_CUT), slice(LAST_CUT, T)):
+            gated(first, last_y, first_list, gates[0], cols)
+            gated(second, last_y, second_list, gates[1], cols)
+            add_and_store(2, total, first, second, cols)

@@ -36,14 +36,30 @@ ALIGN = 256
 TOKEN_BLOCKS = T // P
 BANKS = 8
 
-SHARED_FROM = LAST_CHUNK - 5
-EARLY_EXPERTS = 2
-VECTOR_PIECES = (2, 3, 0)
-LEAD = 1
-EXPERT_GROUPS = ((0, 2), (2, 4), (4, 5))
-LAST_CUT = 384
+PAIRS_FROM = 2
+PAIRS_TO = 12
+EARLY_PIECES = 0
+PE_ADD = ()
+SIG_TIE = (20, 21)
+SHARED_FROM = 14
+HEAD_V = 4
+SIG_EARLY = (3, 3)
+SIG_3 = (3, 4)
+H_EARLY = (4, False)
+H_3 = (5, False)
 
-STREAM_BUFS = 10
+SLOTS = 12
+SLOT = RAW * 4
+V_PIECES = (0, 1, 2, 5, 6)
+Y_AFTER = (10, 14)
+SECOND_AFTER = (9, 14)
+LISTS_AFTER = 6
+CUTS = (0, 320, 512, 640)
+WHOLE_FIRST = False
+GROUPS = (((0, 2), (2, 3), (3, 4), (4, 5)), ((0, 2), (2, 4), (4, 5)), ((0, 2), (2, 4), (4, 5)))
+SPLIT_ADD = 320
+SMALL_ON_SYNC = False
+LAST_WHOLE = False
 ROUNDED_BUFS = 5
 CODE_BUFS = 6
 
@@ -55,6 +71,7 @@ def tile_moe_pkd_glu_sigmoid_kernel(
     with ExitStack() as ctx:
         keep = ctx.enter_context(tc.tile_pool(name="keep", bufs=1))
         rings = ctx.enter_context(tc.tile_pool(name="rings", bufs=1))
+        stream = ctx.enter_context(tc.tile_pool(name="stream", bufs=1))
         psum = ctx.enter_context(tc.psum_pool(name="psum", bufs=1))
         turns = {}
 
@@ -66,71 +83,107 @@ def tile_moe_pkd_glu_sigmoid_kernel(
         def tile_on(tag, shape, dtype):
             return rings.tile(shape, dtype, name="tile", tag=tag, align_bytes=ALIGN)
 
+        def tile_at(name, offset, columns):
+            return stream.tile([P, columns], F32, name=name, align_bytes=ALIGN, offset=offset)
+
         def bank_on(tag):
             return psum.tile([P, BANK], F32, name="bank", tag=tag)
 
         def bank_tile():
             return bank_on(next_tag("bank", BANKS))
 
+        def token_block(tile, b):
+            return tile[:, b * P : (b + 1) * P]
+
         slot_list = keep.tile([P, S // LIST_COLUMN], U16, name="slot_list")
         nc.sync.dma_start(slot_list[:], offs)
         token_scales = keep.tile([P, T // 4], I32, name="token_scales", align_bytes=ALIGN)
         nc.vector.memset(token_scales[:], 0)
-        token_words = []
-        for o in range(PASSES):
-            token_words.append(keep.tile([P, T], I32, name="token_words%d" % o, align_bytes=ALIGN))
-            nc.sync.dma_start(token_words[o][:], x_words[o].rearrange("p t r -> p (t r)").bitcast(I32))
+        token_words = keep.tile([P, PASSES * T], I32, name="token_words", align_bytes=ALIGN)
+        nc.sync.dma_start(
+            token_words[:].rearrange("p (o t) -> p o t", o=PASSES),
+            x_words.rearrange("o p t r -> p o (t r)").bitcast(I32),
+        )
+        small = nc.sync if SMALL_ON_SYNC else nc.scalar
         for q in range(4):
-            nc.scalar.dma_start(
+            small.dma_start(
                 token_scales[32 * q : 32 * q + 4 * PASSES, :], x_scales[:, 4 * q : 4 * q + 4, :].bitcast(I32)
             )
+        gate_rows = keep.tile([P, T], F32, name="gate_rows", align_bytes=ALIGN)
+        nc.gpsimd.memset(gate_rows[:], 0.0)
+        small.dma_start(gate_rows[0:2, :], gate[:, 0, :])
+        identity = keep.tile([P, P], F32, name="identity")
+        make_identity(nc, identity[:])
 
         warm = keep.tile([P, 8], F32, name="warm")
         nc.vector.memset(warm[:], 0.0)
         nc.scalar.activation(warm[:], warm[:], SIGMOID)
 
+        gates = [keep.tile([P, T], F32, name="gate%d" % r, align_bytes=ALIGN) for r in range(2)]
+        gate_cols = keep.tile([P, 2 * TOKEN_BLOCKS], F32, name="gate_cols")
+        bank = bank_tile()
+        for b in range(TOKEN_BLOCKS):
+            nc.tensor.transpose(bank[:, 32 * b : 32 * b + P], token_block(gate_rows, b), identity[:])
+        nc.scalar.copy(
+            gate_cols[:].rearrange("p (b r) -> p b r", r=2),
+            bank[:, : 32 * TOKEN_BLOCKS].rearrange("p (b c) -> p b c", c=32)[:, :, 0:2],
+        )
+        for r in range(2):
+            for c0 in range(0, T, BANK):
+                c1 = min(c0 + BANK, T)
+                bank = bank_tile()
+                for b in range(c0 // P, c1 // P):
+                    column = gate_cols[:, 2 * b + r : 2 * b + r + 1].to_broadcast([P, P])
+                    nc.tensor.transpose(token_block(bank, b - c0 // P), column, identity[:])
+                nc.scalar.copy(gates[r][:, c0:c1], bank[:, : c1 - c0])
+
         slot_words, slot_scales = {}, {}
-
-        def expert_offsets(e):
-            return slot_list[:, e * C // LIST_COLUMN : (e + 1) * C // LIST_COLUMN]
-
-        def gather_words(e):
-            slot_words[e] = tile_on("words%d" % e, [P, PASSES * C], U32)
-            for o in range(PASSES):
-                window = token_words[o][:].bitcast(U32)
-                nc.vector.tensor_copy(slot_words[e][:, o * C : (o + 1) * C], window.indirect(expert_offsets(e)))
-
-        for e in range(EARLY_EXPERTS):
-            gather_words(e)
         for e in range(E):
+            offsets = slot_list[:, e * C // LIST_COLUMN : (e + 1) * C // LIST_COLUMN]
+            slot_words[e] = keep.tile([P, PASSES * C], U32, name="slot_words%d" % e, align_bytes=ALIGN)
+            for o in range(PASSES):
+                window = token_words[:, o * T : (o + 1) * T].bitcast(U32)
+                nc.vector.tensor_copy(slot_words[e][:, o * C : (o + 1) * C], window.indirect(offsets))
             slot_scales[e] = keep.tile([P, C], U8, name="slot_scales%d" % e, align_bytes=ALIGN)
-            nc.vector.tensor_copy(slot_scales[e][:], token_scales[:].bitcast(U8).indirect(expert_offsets(e)))
+            nc.vector.tensor_copy(slot_scales[e][:], token_scales[:].bitcast(U8).indirect(offsets))
 
         def vector_planes(chunk):
             if chunk >= SHARED_FROM:
                 return PACK // 2
-            if chunk % PASSES > 0 or chunk == 0:
+            if chunk < PASSES or chunk % PASSES > 0:
                 return 0
-            if chunk < CHUNKS:
-                return PACK // 2
+            if chunk == PASSES:
+                return HEAD_V
             return PACK
+
+        loaded, rounded_tags = {}, {}
 
         def load_chunk(chunk):
             e, c = divmod(chunk, CHUNKS)
             w, o = (w1, w3)[c // PASSES], c % PASSES
+            if PAIRS_FROM <= chunk < PAIRS_TO:
+                if o == 0:
+                    pair = tile_at("pair%d" % chunk, chunk % SLOTS * SLOT, PASSES * RAW)
+                    nc.sync.dma_start(
+                        pair[:].rearrange("p (o x) -> p o x", o=PASSES),
+                        w[e].rearrange("(o p j) c -> p o (j c)", o=PASSES, j=PACK),
+                    )
+                    for k in range(PASSES):
+                        loaded[chunk + k] = [pair[:, k * RAW : (k + 1) * RAW]]
+                return
             rows = w[e, o * P * PACK : (o + 1) * P * PACK, :].rearrange("(p j) c -> p j c", j=PACK)
             width = H // 2 if chunk == LAST_CHUNK else H
             parts = []
             for c0 in range(0, H, width):
-                parts.append(tile_on(next_tag("stream", STREAM_BUFS), [P, PACK * width], F32)[:])
+                offset = chunk % SLOTS * SLOT + c0 * PACK * 4
+                parts.append(tile_at("part%d_%d" % (chunk, c0), offset, PACK * width)[:])
                 nc.sync.dma_start(parts[-1].rearrange("p (j c) -> p j c", j=PACK), rows[:, :, c0 : c0 + width])
-            return parts
+            loaded[chunk] = parts
 
         def quantise_chunk(chunk):
-            late = EARLY_EXPERTS + chunk
-            tag = "words%d" % late if late < E else next_tag("rounded", ROUNDED_BUFS)
-            rounded = tile_on(tag, [P, RAW], BF16)
-            parts = load_chunk(chunk)
+            rounded_tags[chunk] = next_tag("rounded", ROUNDED_BUFS)
+            rounded = tile_on(rounded_tags[chunk], [P, RAW], BF16)
+            parts = loaded[chunk]
             dst = rounded[:].rearrange("p (t m j) -> p m j t", t=PACK, j=PACK)
             for n_part, part in enumerate(parts):
                 src = part.rearrange("p (j m t) -> p m j t", j=PACK, t=PACK)
@@ -147,9 +200,7 @@ def tile_moe_pkd_glu_sigmoid_kernel(
                     scales=scales[:, w0 : w0 + step],
                     in_=rounded[:, w0 * PACK : (w0 + step) * PACK],
                 )
-            if late < E:
-                gather_words(late)
-            return codes, scales, parts
+            return codes, scales
 
         halves = range(C // HALF)
 
@@ -160,7 +211,7 @@ def tile_moe_pkd_glu_sigmoid_kernel(
             bank = bank_tile()
             for t in range(PACK):
                 cols = slice(t * P, (t + 1) * P)
-                for o, (codes, scales, parts) in enumerate(passes):
+                for o, (codes, scales) in enumerate(passes):
                     nc.tensor.matmul_mx(
                         out=bank[:, t * HALF : (t + 1) * HALF],
                         lhsT=codes[:, cols].bitcast(FP8X4),
@@ -192,65 +243,89 @@ def tile_moe_pkd_glu_sigmoid_kernel(
                 in_=h_bf[:, slots.start * PACK : slots.stop * PACK],
             )
 
-        gates = [keep.tile([P, T], F32, name="gate%d" % r, align_bytes=ALIGN) for r in range(2)]
-        identity = keep.tile([P, P], F32, name="identity")
-        make_identity(nc, identity[:])
         first_list = keep.tile([P, T // LIST_COLUMN], U16, name="first_list")
         second_list = keep.tile([P, T // LIST_COLUMN], U16, name="second_list")
         w2_rounded = [tile_on("w2_rounded%d" % n, [P, E * PIECE], BF16) for n in range(N_TILES)]
         w2_codes = [tile_on("w2_codes%d" % n, [P, E * P], U32) for n in range(N_TILES)]
         w2_scales = [tile_on("w2_scales%d" % n, [P, E * P], U8) for n in range(N_TILES)]
 
-        all_slots = slice(0, C)
-        for e in range(E):
-            done = []
-            for c in range(CHUNKS):
-                chunk = e * CHUNKS + c
-                done.append(quantise_chunk(chunk))
-                spent = done[c][2][-1]
-                if c == 0 and e > 0:
-                    if len(sig) == 1:
-                        sig.append(sigmoid_onto(spent[:, :BANK], pre[1]))
-                    h_bf = tile_on(next_tag("h_bf", 2), [P, C * PACK], BF16)
-                    hidden_values(h_bf, lin, sig)
-                    quantise_hidden(e - 1, all_slots, h_bf)
-                if c == PASSES - 1:
-                    pre = [first_layer_product(done[:PASSES], e, half) for half in halves]
-            sig = [sigmoid_onto(spent[:, :BANK] if chunk == LAST_CHUNK else spent[:, BANK : 2 * BANK], pre[0])]
-            if vector_planes(chunk) == 0:
-                sig.append(sigmoid_onto(spent[:, :BANK], pre[1]))
-            lin = [first_layer_product(done[PASSES:], e, half) for half in halves]
+        pieces, y_at, second_at = [], {}, {}
+        piece_at = []
+        offset = (LAST_CHUNK + 1) % SLOTS * SLOT
+        for number in range(N_TILES * E):
+            if offset + 4 * (S + PIECE + T) > SLOTS * SLOT:
+                offset = 0
+            if number in Y_AFTER:
+                y_at[Y_AFTER.index(number) + 1] = offset
+                offset += 4 * S - ALIGN
+            piece_at.append(offset)
+            offset += 4 * PIECE
+            if number in SECOND_AFTER:
+                second_at[SECOND_AFTER.index(number)] = offset - ALIGN
+                offset += 4 * T - ALIGN
 
-        ends = (E, 2 * E + LEAD, N_TILES * E)
-        pieces, piece_tags = [], []
-        for n in range(N_TILES):
-            piece_tags.append(next_tag("stream", STREAM_BUFS))
-            held = tile_on(piece_tags[n], [P, (ends[n] - len(pieces)) * PIECE], F32)
-            for place, number in enumerate(range(len(pieces), ends[n])):
-                tile_n, e = divmod(number, E)
-                pieces.append(held[:, place * PIECE : (place + 1) * PIECE])
-                nc.sync.dma_start(
-                    pieces[number].rearrange("p (j c) -> p j c", j=PACK),
-                    w2[e, :, tile_n * P : (tile_n + 1) * P].rearrange("(p j) c -> p j c", j=PACK),
-                )
-                if number == E + VECTOR_PIECES[1] - 1:
-                    nc.sync.dma_start(first_list[:], pos1)
-                    nc.sync.dma_start(second_list[:], pos2)
-                if number == ends[1]:
-                    nc.sync.dma_start(gates[0][:], gate[0, :P, :])
-                if number == ends[2] - 1:
-                    nc.sync.dma_start(gates[1][:], gate[1, :P, :])
+        def load_piece(number):
+            tile_n, e = divmod(number, E)
+            pieces.append(tile_at("piece%d" % number, piece_at[number], PIECE)[:])
+            nc.sync.dma_start(
+                pieces[number].rearrange("p (j c) -> p j c", j=PACK),
+                w2[e, :, tile_n * P : (tile_n + 1) * P].rearrange("(p j) c -> p j c", j=PACK),
+            )
 
         def round_pieces(numbers):
             for number in numbers:
                 n, e = divmod(number, E)
                 dst = w2_rounded[n][:, e * PIECE : (e + 1) * PIECE].rearrange("p (c i j) -> p c j i", i=4, j=PACK)
                 src = pieces[number].rearrange("p (j c i) -> p c j i", i=4, j=PACK)
-                copy = nc.vector.tensor_copy if e < VECTOR_PIECES[n] else nc.scalar.copy
+                copy = nc.vector.tensor_copy if number in V_PIECES else nc.scalar.copy
                 copy(dst, src)
 
+        all_slots = slice(0, C)
+        pre, lin, sig = {}, {}, {}
+
+        def spent(place, half):
+            if place < LAST_CHUNK:
+                return loaded[place][0][:, half * BANK : (half + 1) * BANK]
+            if place < LAST_CHUNK + 2:
+                return loaded[LAST_CHUNK][place - LAST_CHUNK][:, half * BANK : (half + 1) * BANK]
+            return pieces[place - LAST_CHUNK - 2]
+
+        def after(place):
+            for e in range(E):
+                ties = SIG_TIE if e == E - 1 else [e * CHUNKS + k for k in (SIG_3 if e == E - 2 else SIG_EARLY)]
+                for half in halves:
+                    if ties[half] == place:
+                        sig[e, half] = sigmoid_onto(spent(place, half), pre[e][half])
+            for e in range(E - 1):
+                offset, tied = H_3 if e == E - 2 else H_EARLY
+                if e * CHUNKS + offset == place:
+                    h_bf = tile_on(rounded_tags[place] if tied else next_tag("h_bf", 2), [P, C * PACK], BF16)
+                    hidden_values(h_bf, lin[e], [sig[e, half] for half in halves])
+                    quantise_hidden(e, all_slots, h_bf)
+
+        for e in range(E):
+            done = []
+            for c in range(CHUNKS):
+                chunk = e * CHUNKS + c
+                if chunk == LAST_CHUNK:
+                    for number in range(EARLY_PIECES):
+                        load_piece(number)
+                load_chunk(chunk)
+                done.append(quantise_chunk(chunk))
+                if c == PASSES - 1:
+                    pre[e] = [first_layer_product(done[:PASSES], e, half) for half in halves]
+                after(chunk)
+            lin[e] = [first_layer_product(done[PASSES:], e, half) for half in halves]
+        after(LAST_CHUNK + 1)
+
+        for number in range(EARLY_PIECES, N_TILES * E):
+            load_piece(number)
+            if number == LISTS_AFTER:
+                nc.sync.dma_start(first_list[:], pos1)
+                nc.sync.dma_start(second_list[:], pos2)
+
         def quantise_pieces(n):
-            for e0, e1 in EXPERT_GROUPS:
+            for e0, e1 in GROUPS[n]:
                 nc.vector.quantize_mx(
                     out=w2_codes[n][:, e0 * P : e1 * P].bitcast(FP8X4),
                     scales=w2_scales[n][:, e0 * P : e1 * P],
@@ -275,93 +350,87 @@ def tile_moe_pkd_glu_sigmoid_kernel(
             nc.scalar.copy(y[:, first_slot : first_slot + (e1 - e0) * width], bank[:, : (e1 - e0) * width])
             return tag
 
-        round_pieces(range(E))
-        sig.append(sigmoid_onto(pieces[VECTOR_PIECES[0]], pre[1]))
+        for number in range(E):
+            round_pieces([number])
+            after(LAST_CHUNK + 2 + number)
         quantise_pieces(0)
         y = tile_on("y0", [P, S], F32)
-        for e0, e1 in EXPERT_GROUPS[:-1]:
+        for e0, e1 in GROUPS[0][:-1]:
             slot_results(0, y, e0, e1, all_slots)
         h_bf = keep.tile([P, C * PACK], BF16, name="h_last", align_bytes=ALIGN)
-        hidden_values(h_bf, lin, sig)
+        hidden_values(h_bf, lin[E - 1], [sig[E - 1, half] for half in halves])
         for half in halves:
             quantise_hidden(E - 1, half_slots(half), h_bf)
-        for half in halves:
-            slot_results(0, y, E - 1, E, half_slots(half))
-
-        def entries(inverse_list, cols):
-            return inverse_list[:, cols.start // LIST_COLUMN : cols.stop // LIST_COLUMN]
+        for slots in [all_slots] if LAST_WHOLE else [half_slots(half) for half in halves]:
+            slot_results(0, y, E - 1, E, slots)
 
         def gated(result, y, inverse_list, gate_tile, cols):
-            nc.vector.tensor_tensor(result[:, cols], y[:].indirect(entries(inverse_list, cols)), gate_tile[:, cols], MULT)
+            entries = inverse_list[:, cols.start // LIST_COLUMN : cols.stop // LIST_COLUMN]
+            nc.vector.tensor_tensor(result[:, cols], y[:].indirect(entries), gate_tile[:, cols], MULT)
 
         def add_and_store(n, total, first, second, cols):
             nc.vector.tensor_tensor(total[:, cols], first[:, cols], second[:, cols], ADD)
             nc.sync.dma_start(out[n * P : (n + 1) * P, cols], total[:, cols])
 
+        ends = (E, max(Y_AFTER[0] + 1, 2 * E), N_TILES * E)
+
         def make_y(n):
             round_pieces(range(ends[n - 1], ends[n]))
             quantise_pieces(n)
-            y = tile_on(piece_tags[n], [P, S], F32)
-            return y, [slot_results(n, y, e0, e1, all_slots) for e0, e1 in EXPERT_GROUPS]
-
-        def token_block(tile, b):
-            return tile[:, b * P : (b + 1) * P]
+            y = tile_at("y%d" % n, y_at[n], S)
+            return y, [slot_results(n, y, e0, e1, all_slots) for e0, e1 in GROUPS[n]]
 
         all_tokens = slice(0, T)
-        firsts = [tile_on("first0", [P, T], F32)]
-        totals = [tile_on("total0", [P, T], F32)]
+        terms, banks = [], []
+        for n in range(N_TILES - 1):
+            first = tile_on("first%d" % n, [P, T], F32)
+            gated(first, y, first_list, gates[0], all_tokens)
+            next_y, next_banks = make_y(n + 1)
+            second = tile_at("second%d" % n, second_at[n], T)
+            parts = [slice(0, SPLIT_ADD), slice(SPLIT_ADD, T)] if SPLIT_ADD and n not in PE_ADD else [all_tokens]
+            for cols in parts:
+                gated(second, y, second_list, gates[1], cols)
+            terms.append((first, second))
+            banks.append(next_banks)
+            if n not in PE_ADD:
+                total = tile_on("total%d" % n, [P, T], F32)
+                for cols in parts:
+                    nc.vector.tensor_tensor(total[:, cols], first[:, cols], second[:, cols], ADD)
+                nc.sync.dma_start(out[n * P : (n + 1) * P, :], total[:])
+            y = next_y
 
-        nc.vector.tensor_copy(firsts[0][:], y[:].indirect(first_list[:]))
-        middle_y, middle_banks = make_y(1)
-        second = tile_on("w2_rounded1", [P, T], F32)
-        nc.vector.tensor_copy(second[:], y[:].indirect(second_list[:]))
-        turned = []
-        for term in (firsts[0], second):
-            for b in range(TOKEN_BLOCKS):
-                place = len(turned) % (BANK // P)
-                if place == 0:
-                    bank = bank_on(middle_banks[len(turned) // (BANK // P)])
-                turned.append(token_block(bank, place))
-                nc.tensor.transpose(turned[-1], token_block(term, b), identity[:])
-
-        firsts.append(tile_on("first1", [P, T], F32))
-        totals.append(tile_on("total1", [P, T], F32))
-        gated(firsts[1], middle_y, first_list, gates[0], all_tokens)
-        last_y, last_banks = make_y(2)
-        second = tile_on("second1", [P, T], F32)
-        gated(second, middle_y, second_list, gates[1], all_tokens)
-        add_and_store(1, totals[1], firsts[1], second, all_tokens)
-
-        gate_cols = keep.tile([P, 2 * TOKEN_BLOCKS], F32, name="gate_cols")
-        for r in range(2):
-            bank = bank_tile()
-            for b in range(TOKEN_BLOCKS):
-                nc.tensor.transpose(bank[:, 32 * b : 32 * b + P], token_block(gates[r], b), identity[:])
-            nc.scalar.copy(gate_cols[:, r * TOKEN_BLOCKS : (r + 1) * TOKEN_BLOCKS], bank[:, 0 : 32 * TOKEN_BLOCKS : 32])
-        scaled = tile_on("w2_codes2", [P, 2 * T], F32)
-        for b in range(TOKEN_BLOCKS):
-            for i in (b, TOKEN_BLOCKS + b):
-                nc.scalar.activation(token_block(scaled, i), turned[i], COPY, scale=gate_cols[:, i : i + 1])
-        for c0 in range(0, T, BANK):
-            c1 = min(c0 + BANK, T)
-            bank = bank_on(last_banks[c0 // BANK])
-            for b in range(c0 // P, c1 // P):
-                for r in range(2):
-                    nc.tensor.matmul(
-                        token_block(bank, b - c0 // P),
-                        token_block(scaled, r * TOKEN_BLOCKS + b),
-                        identity[:],
-                        start=(r == 0),
-                        stop=(r == 1),
-                        is_transpose=True,
-                    )
-            nc.scalar.copy(totals[0][:, c0:c1], bank[:, : c1 - c0])
-        nc.sync.dma_start(out[:P, :], totals[0][:])
+        for n in PE_ADD:
+            turned = tile_on("w2_codes2" if n == 0 else "turned", [P, T], F32)
+            total = tile_on("total%d" % n, [P, T], F32)
+            for k, c0 in enumerate(range(0, T, BANK)):
+                c1 = min(c0 + BANK, T)
+                bank = bank_on(banks[0][k]) if n == 0 else bank_tile()
+                for b in range(c0 // P, c1 // P):
+                    for r in range(2):
+                        nc.tensor.matmul(
+                            token_block(bank, b - c0 // P),
+                            token_block(terms[n][r], b),
+                            identity[:],
+                            start=(r == 0),
+                            stop=(r == 1),
+                            is_transpose=True,
+                        )
+                nc.scalar.copy(turned[:, c0:c1], bank[:, : c1 - c0])
+            for k, c0 in enumerate(range(0, T, BANK)):
+                c1 = min(c0 + BANK, T)
+                bank = bank_on(banks[1][k]) if n == 0 else bank_tile()
+                for b in range(c0 // P, c1 // P):
+                    nc.tensor.transpose(token_block(bank, b - c0 // P), token_block(turned, b), identity[:])
+                nc.scalar.copy(total[:, c0:c1], bank[:, : c1 - c0])
+            nc.sync.dma_start(out[n * P : (n + 1) * P, :], total[:])
 
         first = tile_on("first2", [P, T], F32)
         total = tile_on("total2", [P, T], F32)
         second = tile_on("second2", [P, T], F32)
-        for cols in (slice(0, LAST_CUT), slice(LAST_CUT, T)):
-            gated(first, last_y, first_list, gates[0], cols)
-            gated(second, last_y, second_list, gates[1], cols)
+        if WHOLE_FIRST:
+            gated(first, y, first_list, gates[0], all_tokens)
+        for cols in [slice(c0, c1) for c0, c1 in zip(CUTS, CUTS[1:])]:
+            if not WHOLE_FIRST:
+                gated(first, y, first_list, gates[0], cols)
+            gated(second, y, second_list, gates[1], cols)
             add_and_store(2, total, first, second, cols)

@@ -37,31 +37,42 @@ TOKEN_BLOCKS = T // P
 BANKS = 8
 
 PAIRS_FROM = 2
-PAIRS_TO = 12
+PAIRS_TO = 2
 EARLY_PIECES = 0
 PE_ADD = ()
-SIG_TIE = (20, 21)
-SHARED_FROM = 14
-HEAD_V = 4
-SIG_EARLY = (3, 3)
-SIG_3 = (3, 4)
-H_EARLY = (4, False)
-H_3 = (5, False)
 
 SLOTS = 12
 SLOT = RAW * 4
-V_PIECES = (0, 1, 2, 5, 6)
+V_PIECES = (4, 5, 6, 7)
 Y_AFTER = (10, 14)
 SECOND_AFTER = (9, 14)
-LISTS_AFTER = 6
-CUTS = (0, 320, 512, 640)
+LISTS_AFTER = 7
+CUTS = (0, 384, 640)
 WHOLE_FIRST = False
-GROUPS = (((0, 2), (2, 3), (3, 4), (4, 5)), ((0, 2), (2, 4), (4, 5)), ((0, 2), (2, 4), (4, 5)))
+GROUPS = (((0, 2), (2, 3), (3, 4), (4, 5)), ((0, 1), (1, 3), (3, 4), (4, 5)), ((0, 2), (2, 4), (4, 5)))
 SPLIT_ADD = 320
-SMALL_ON_SYNC = False
+SMALL_ON_SYNC = True
 LAST_WHOLE = False
-ROUNDED_BUFS = 5
-CODE_BUFS = 6
+V_COLUMNS = 256
+V_COLUMNS_LAST = 128
+S_ALONE = 1
+LATE = {0: 2, 1: 3, 2: 4}
+SPREAD = False
+GATE_AFTER = (11, 14)
+SCALED = (0,)
+TURN_ON_V = False
+H_FIRST = True
+SIG_AT = ((3, 4), (3, 4), (3, 4), (3, 4), (2, 4))
+TT_AT = ((4, 5), (4, 5), (4, 5), (4, 4))
+TURN_AT = (6, 6, 6, 5)
+Y_LAST_ON_V = False
+V_HEAD = 128
+HEAD_TO = 4
+TURNS_TO = 4
+TURN_V = 512
+TURN_S = 0
+ROUNDED_BUFS = 4
+CODE_BUFS = 3
 
 
 def tile_moe_pkd_glu_sigmoid_kernel(
@@ -109,9 +120,10 @@ def tile_moe_pkd_glu_sigmoid_kernel(
             small.dma_start(
                 token_scales[32 * q : 32 * q + 4 * PASSES, :], x_scales[:, 4 * q : 4 * q + 4, :].bitcast(I32)
             )
-        gate_rows = keep.tile([P, T], F32, name="gate_rows", align_bytes=ALIGN)
-        nc.gpsimd.memset(gate_rows[:], 0.0)
-        small.dma_start(gate_rows[0:2, :], gate[:, 0, :])
+        if SPREAD:
+            gate_rows = keep.tile([P, T], F32, name="gate_rows", align_bytes=ALIGN)
+            nc.gpsimd.memset(gate_rows[:], 0.0)
+            small.dma_start(gate_rows[0:2, :], gate[:, 0, :])
         identity = keep.tile([P, P], F32, name="identity")
         make_identity(nc, identity[:])
 
@@ -121,40 +133,40 @@ def tile_moe_pkd_glu_sigmoid_kernel(
 
         gates = [keep.tile([P, T], F32, name="gate%d" % r, align_bytes=ALIGN) for r in range(2)]
         gate_cols = keep.tile([P, 2 * TOKEN_BLOCKS], F32, name="gate_cols")
-        bank = bank_tile()
-        for b in range(TOKEN_BLOCKS):
-            nc.tensor.transpose(bank[:, 32 * b : 32 * b + P], token_block(gate_rows, b), identity[:])
-        nc.scalar.copy(
-            gate_cols[:].rearrange("p (b r) -> p b r", r=2),
-            bank[:, : 32 * TOKEN_BLOCKS].rearrange("p (b c) -> p b c", c=32)[:, :, 0:2],
-        )
-        for r in range(2):
-            for c0 in range(0, T, BANK):
-                c1 = min(c0 + BANK, T)
-                bank = bank_tile()
-                for b in range(c0 // P, c1 // P):
-                    column = gate_cols[:, 2 * b + r : 2 * b + r + 1].to_broadcast([P, P])
-                    nc.tensor.transpose(token_block(bank, b - c0 // P), column, identity[:])
-                nc.scalar.copy(gates[r][:, c0:c1], bank[:, : c1 - c0])
+        if SPREAD:
+            bank = bank_tile()
+            for b in range(TOKEN_BLOCKS):
+                nc.tensor.transpose(bank[:, 32 * b : 32 * b + P], token_block(gate_rows, b), identity[:])
+            nc.scalar.copy(
+                gate_cols[:].rearrange("p (b r) -> p b r", r=2),
+                bank[:, : 32 * TOKEN_BLOCKS].rearrange("p (b c) -> p b c", c=32)[:, :, 0:2],
+            )
+            for r in range(2):
+                for c0 in range(0, T, BANK):
+                    c1 = min(c0 + BANK, T)
+                    bank = bank_tile()
+                    for b in range(c0 // P, c1 // P):
+                        column = gate_cols[:, 2 * b + r : 2 * b + r + 1].to_broadcast([P, P])
+                        nc.tensor.transpose(token_block(bank, b - c0 // P), column, identity[:])
+                    nc.scalar.copy(gates[r][:, c0:c1], bank[:, : c1 - c0])
 
         slot_words, slot_scales = {}, {}
-        for e in range(E):
-            offsets = slot_list[:, e * C // LIST_COLUMN : (e + 1) * C // LIST_COLUMN]
-            slot_words[e] = keep.tile([P, PASSES * C], U32, name="slot_words%d" % e, align_bytes=ALIGN)
+
+        def expert_offsets(e):
+            return slot_list[:, e * C // LIST_COLUMN : (e + 1) * C // LIST_COLUMN]
+
+        def gather_words(e):
+            slot_words[e] = tile_on("words%d" % e, [P, PASSES * C], U32)
             for o in range(PASSES):
                 window = token_words[:, o * T : (o + 1) * T].bitcast(U32)
-                nc.vector.tensor_copy(slot_words[e][:, o * C : (o + 1) * C], window.indirect(offsets))
-            slot_scales[e] = keep.tile([P, C], U8, name="slot_scales%d" % e, align_bytes=ALIGN)
-            nc.vector.tensor_copy(slot_scales[e][:], token_scales[:].bitcast(U8).indirect(offsets))
+                nc.vector.tensor_copy(slot_words[e][:, o * C : (o + 1) * C], window.indirect(expert_offsets(e)))
 
-        def vector_planes(chunk):
-            if chunk >= SHARED_FROM:
-                return PACK // 2
-            if chunk < PASSES or chunk % PASSES > 0:
-                return 0
-            if chunk == PASSES:
-                return HEAD_V
-            return PACK
+        for e in range(E):
+            if e not in LATE.values():
+                gather_words(e)
+        for e in range(E):
+            slot_scales[e] = keep.tile([P, C], U8, name="slot_scales%d" % e, align_bytes=ALIGN)
+            nc.vector.tensor_copy(slot_scales[e][:], token_scales[:].bitcast(U8).indirect(expert_offsets(e)))
 
         loaded, rounded_tags = {}, {}
 
@@ -180,17 +192,23 @@ def tile_moe_pkd_glu_sigmoid_kernel(
                 nc.sync.dma_start(parts[-1].rearrange("p (j c) -> p j c", j=PACK), rows[:, :, c0 : c0 + width])
             loaded[chunk] = parts
 
+        def interleave(copy, dst, src):
+            copy(dst.rearrange("p (c i) j -> p c j i", i=4), src.rearrange("p j (c i) -> p c j i", i=4))
+
         def quantise_chunk(chunk):
-            rounded_tags[chunk] = next_tag("rounded", ROUNDED_BUFS)
+            rounded_tags[chunk] = "words%d" % LATE[chunk] if chunk in LATE else next_tag("rounded", ROUNDED_BUFS)
             rounded = tile_on(rounded_tags[chunk], [P, RAW], BF16)
             parts = loaded[chunk]
-            dst = rounded[:].rearrange("p (t m j) -> p m j t", t=PACK, j=PACK)
+            dst = rounded[:].rearrange("p (c j) -> p c j", j=PACK)
+            width = H // len(parts)
+            cut = V_COLUMNS_LAST if chunk == LAST_CHUNK else (0 if chunk < S_ALONE else (V_HEAD if chunk < HEAD_TO else V_COLUMNS))
+            if HEAD_TO <= chunk < TURNS_TO:
+                cut = TURN_V if chunk % PASSES == 0 else TURN_S
             for n_part, part in enumerate(parts):
-                src = part.rearrange("p (j m t) -> p m j t", j=PACK, t=PACK)
-                ms = slice(n_part * P // len(parts), (n_part + 1) * P // len(parts))
-                for t0 in range(0, PACK, 2):
-                    copy = nc.vector.tensor_copy if t0 < vector_planes(chunk) else nc.scalar.copy
-                    copy(dst[:, ms, :, t0 : t0 + 2], src[:, :, :, t0 : t0 + 2])
+                src = part.rearrange("p (j c) -> p j c", j=PACK)
+                for copy, c0, c1 in ((nc.vector.tensor_copy, 0, cut), (nc.scalar.copy, cut, width)):
+                    if c1 > c0:
+                        interleave(copy, dst[:, n_part * width + c0 : n_part * width + c1, :], src[:, :, c0:c1])
             codes = tile_on(next_tag("codes", CODE_BUFS), [P, H], U32)
             scales = tile_on(next_tag("scales", CODE_BUFS), [P, H], U8)
             step = H // len(parts)
@@ -200,6 +218,8 @@ def tile_moe_pkd_glu_sigmoid_kernel(
                     scales=scales[:, w0 : w0 + step],
                     in_=rounded[:, w0 * PACK : (w0 + step) * PACK],
                 )
+            if chunk in LATE:
+                gather_words(LATE[chunk])
             return codes, scales
 
         halves = range(C // HALF)
@@ -207,40 +227,35 @@ def tile_moe_pkd_glu_sigmoid_kernel(
         def half_slots(half):
             return slice(half * HALF, (half + 1) * HALF)
 
-        def first_layer_product(passes, e, half):
-            bank = bank_tile()
-            for t in range(PACK):
-                cols = slice(t * P, (t + 1) * P)
-                for o, (codes, scales) in enumerate(passes):
-                    nc.tensor.matmul_mx(
-                        out=bank[:, t * HALF : (t + 1) * HALF],
-                        lhsT=codes[:, cols].bitcast(FP8X4),
-                        lhsT_scale=scales[:, cols],
-                        rhs=slot_words[e][:, o * C + half * HALF : o * C + (half + 1) * HALF].bitcast(FP8X4),
-                        rhs_scale=slot_scales[e][4 * o :, half_slots(half)],
-                        start=(o == 0),
-                        stop=(o == PASSES - 1),
-                    )
-            return bank[:].rearrange("p (t s) -> p s t", t=PACK)
+        def first_layer_pass(bank, e, half, o, codes, scales):
+            nc.tensor.matmul_mx(
+                out=bank[:],
+                lhsT=slot_words[e][:, o * C + half * HALF : o * C + (half + 1) * HALF].bitcast(FP8X4),
+                lhsT_scale=slot_scales[e][4 * o :, half_slots(half)],
+                rhs=codes[:].bitcast(FP8X4),
+                rhs_scale=scales[:],
+                start=(o == 0),
+                stop=(o == PASSES - 1),
+            )
 
         def sigmoid_onto(spent, pre):
-            sig = spent.rearrange("p (s t) -> p s t", t=PACK)
-            nc.scalar.activation(sig, pre, SIGMOID)
-            return sig
+            nc.scalar.activation(spent, pre[:].rearrange("p (r c) -> p r c", r=2), SIGMOID)
+            return spent
 
         h_codes = [keep.tile([P, C], U32, name="h_codes%d" % e, align_bytes=ALIGN) for e in range(E)]
         h_scales = [keep.tile([P, C], U8, name="h_scales%d" % e, align_bytes=ALIGN) for e in range(E)]
 
-        def hidden_values(h_bf, lin, sig):
-            for half in halves:
-                h_half = h_bf[:, half * BANK : (half + 1) * BANK].rearrange("p (s t) -> p s t", t=PACK)
-                nc.vector.tensor_tensor(h_half, lin[half], sig[half], MULT)
+        def hidden_rows(h_rows, lin, sig, bank):
+            nc.vector.tensor_tensor(h_rows.rearrange("p (r c) -> p r c", r=2), lin[:].rearrange("p (r c) -> p r c", r=2), sig, MULT)
+            words = h_rows.bitcast(F32)
+            for u in range(2):
+                nc.tensor.transpose(token_block(bank, u), words[:, u : H // 2 : 2], identity[:])
 
-        def quantise_hidden(e, slots, h_bf):
+        def quantise_hidden(e, slots, h_words):
             nc.vector.quantize_mx(
                 out=h_codes[e][:, slots].bitcast(FP8X4),
                 scales=h_scales[e][:, slots],
-                in_=h_bf[:, slots.start * PACK : slots.stop * PACK],
+                in_=h_words.bitcast(BF16),
             )
 
         first_list = keep.tile([P, T // LIST_COLUMN], U16, name="first_list")
@@ -281,41 +296,58 @@ def tile_moe_pkd_glu_sigmoid_kernel(
                 copy(dst, src)
 
         all_slots = slice(0, C)
-        pre, lin, sig = {}, {}, {}
+        pre, lin, sig, turned_h = {}, {}, {}, {}
 
-        def spent(place, half):
+        def spent_rows(place):
             if place < LAST_CHUNK:
-                return loaded[place][0][:, half * BANK : (half + 1) * BANK]
+                return loaded[place][0].rearrange("p (j c) -> p j c", j=PACK)
             if place < LAST_CHUNK + 2:
-                return loaded[LAST_CHUNK][place - LAST_CHUNK][:, half * BANK : (half + 1) * BANK]
-            return pieces[place - LAST_CHUNK - 2]
+                return loaded[LAST_CHUNK][place - LAST_CHUNK].rearrange("p (j c) -> p j c", j=2)
+            return pieces[place - LAST_CHUNK - 2].rearrange("p (j c) -> p j c", j=1)
+
+        def turn_out(copy, h_words, bank):
+            n = h_words.shape[1]
+            copy(h_words.rearrange("p k (s u) -> p k s u", u=2), bank[:, : n * 2 * P].rearrange("p (k u s) -> p k s u", k=n, u=2))
 
         def after(place):
             for e in range(E):
-                ties = SIG_TIE if e == E - 1 else [e * CHUNKS + k for k in (SIG_3 if e == E - 2 else SIG_EARLY)]
                 for half in halves:
-                    if ties[half] == place:
-                        sig[e, half] = sigmoid_onto(spent(place, half), pre[e][half])
+                    if e * CHUNKS + SIG_AT[e][half] == place:
+                        rows = spent_rows(place)
+                        if place < LAST_CHUNK:
+                            onto = rows[:, 0:2, C:] if (half == 0 or SIG_AT[e][0] != SIG_AT[e][1]) else rows[:, 2:4, C:]
+                        elif place < LAST_CHUNK + 2:
+                            onto = rows[:, half, :].rearrange("p (r c) -> p r c", r=2)
+                        else:
+                            onto = rows[:, 0, :].rearrange("p (r c) -> p r c", r=2)
+                        sig[e, half] = sigmoid_onto(onto, pre[e][half])
             for e in range(E - 1):
-                offset, tied = H_3 if e == E - 2 else H_EARLY
-                if e * CHUNKS + offset == place:
-                    h_bf = tile_on(rounded_tags[place] if tied else next_tag("h_bf", 2), [P, C * PACK], BF16)
-                    hidden_values(h_bf, lin[e], [sig[e, half] for half in halves])
-                    quantise_hidden(e, all_slots, h_bf)
+                for half in halves:
+                    if e * CHUNKS + TT_AT[e][half] == place:
+                        if half == 0:
+                            turned_h[e] = bank_tile()
+                        h_rows = spent_rows(place)[:, half, :C].bitcast(BF16)
+                        hidden_rows(h_rows, lin[e][half], sig[e, half], turned_h[e][:, half * C : (half + 1) * C])
+                if e * CHUNKS + TURN_AT[e] == place:
+                    h_words = spent_rows(place)[:, 2:4, C:]
+                    turn_out(nc.scalar.copy, h_words, turned_h[e])
+                    for half in halves:
+                        quantise_hidden(e, half_slots(half), h_words[:, half, :])
 
         for e in range(E):
-            done = []
             for c in range(CHUNKS):
                 chunk = e * CHUNKS + c
                 if chunk == LAST_CHUNK:
                     for number in range(EARLY_PIECES):
                         load_piece(number)
                 load_chunk(chunk)
-                done.append(quantise_chunk(chunk))
-                if c == PASSES - 1:
-                    pre[e] = [first_layer_product(done[:PASSES], e, half) for half in halves]
+                codes, scales = quantise_chunk(chunk)
+                sums = (pre, lin)[c // PASSES]
+                if c % PASSES == 0:
+                    sums[e] = [bank_tile() for half in halves]
+                for half in halves:
+                    first_layer_pass(sums[e][half], e, half, c % PASSES, codes, scales)
                 after(chunk)
-            lin[e] = [first_layer_product(done[PASSES:], e, half) for half in halves]
         after(LAST_CHUNK + 1)
 
         for number in range(EARLY_PIECES, N_TILES * E):
@@ -323,6 +355,10 @@ def tile_moe_pkd_glu_sigmoid_kernel(
             if number == LISTS_AFTER:
                 nc.sync.dma_start(first_list[:], pos1)
                 nc.sync.dma_start(second_list[:], pos2)
+            if not SPREAD and number in GATE_AFTER:
+                for r in range(2):
+                    if GATE_AFTER[r] == number:
+                        nc.sync.dma_start(gates[r][:], gate[r, :P, :])
 
         def quantise_pieces(n):
             for e0, e1 in GROUPS[n]:
@@ -332,7 +368,7 @@ def tile_moe_pkd_glu_sigmoid_kernel(
                     in_=w2_rounded[n][:, e0 * PIECE : e1 * PIECE],
                 )
 
-        def slot_results(n, y, e0, e1, slots):
+        def slot_results(n, y, e0, e1, slots, on_vector=False):
             tag = next_tag("bank", BANKS)
             bank = bank_on(tag)
             width = slots.stop - slots.start
@@ -347,22 +383,33 @@ def tile_moe_pkd_glu_sigmoid_kernel(
                     stop=True,
                 )
             first_slot = e0 * C + slots.start
-            nc.scalar.copy(y[:, first_slot : first_slot + (e1 - e0) * width], bank[:, : (e1 - e0) * width])
+            (nc.vector.tensor_copy if on_vector else nc.scalar.copy)(y[:, first_slot : first_slot + (e1 - e0) * width], bank[:, : (e1 - e0) * width])
             return tag
 
         for number in range(E):
             round_pieces([number])
             after(LAST_CHUNK + 2 + number)
+        def last_hidden():
+            h_rows = keep.tile([P, C // HALF * H], BF16, name="h_rows_last", align_bytes=ALIGN)
+            h_words = keep.tile([P, BANK], F32, name="h_last", align_bytes=ALIGN)
+            for half in halves:
+                bank = bank_tile()
+                hidden_rows(h_rows[:, half * H : (half + 1) * H], lin[E - 1][half], sig[E - 1, half], bank)
+                words = h_words[:, half * C : (half + 1) * C]
+                copy = nc.vector.tensor_copy if TURN_ON_V else nc.scalar.copy
+                turn_out(copy, words.rearrange("p (k c) -> p k c", k=1), bank)
+                quantise_hidden(E - 1, half_slots(half), words)
+
+        if H_FIRST:
+            last_hidden()
         quantise_pieces(0)
         y = tile_on("y0", [P, S], F32)
         for e0, e1 in GROUPS[0][:-1]:
             slot_results(0, y, e0, e1, all_slots)
-        h_bf = keep.tile([P, C * PACK], BF16, name="h_last", align_bytes=ALIGN)
-        hidden_values(h_bf, lin[E - 1], [sig[E - 1, half] for half in halves])
-        for half in halves:
-            quantise_hidden(E - 1, half_slots(half), h_bf)
+        if not H_FIRST:
+            last_hidden()
         for slots in [all_slots] if LAST_WHOLE else [half_slots(half) for half in halves]:
-            slot_results(0, y, E - 1, E, slots)
+            slot_results(0, y, E - 1, E, slots, Y_LAST_ON_V)
 
         def gated(result, y, inverse_list, gate_tile, cols):
             entries = inverse_list[:, cols.start // LIST_COLUMN : cols.stop // LIST_COLUMN]
@@ -384,20 +431,63 @@ def tile_moe_pkd_glu_sigmoid_kernel(
         terms, banks = [], []
         for n in range(N_TILES - 1):
             first = tile_on("first%d" % n, [P, T], F32)
-            gated(first, y, first_list, gates[0], all_tokens)
+            if n in SCALED:
+                nc.vector.tensor_copy(first[:], y[:].indirect(first_list[:]))
+            else:
+                gated(first, y, first_list, gates[0], all_tokens)
             next_y, next_banks = make_y(n + 1)
             second = tile_at("second%d" % n, second_at[n], T)
             parts = [slice(0, SPLIT_ADD), slice(SPLIT_ADD, T)] if SPLIT_ADD and n not in PE_ADD else [all_tokens]
-            for cols in parts:
-                gated(second, y, second_list, gates[1], cols)
+            if n in SCALED:
+                nc.vector.tensor_copy(second[:], y[:].indirect(second_list[:]))
+                turned = []
+                for term in (first, second):
+                    for b in range(TOKEN_BLOCKS):
+                        place = len(turned) % (BANK // P)
+                        if place == 0:
+                            bank = bank_on(next_banks[len(turned) // (BANK // P)])
+                        turned.append(token_block(bank, place))
+                        nc.tensor.transpose(turned[-1], token_block(term, b), identity[:])
+            else:
+                for cols in parts:
+                    gated(second, y, second_list, gates[1], cols)
             terms.append((first, second))
             banks.append(next_banks)
-            if n not in PE_ADD:
+            if n not in PE_ADD and n not in SCALED:
                 total = tile_on("total%d" % n, [P, T], F32)
                 for cols in parts:
                     nc.vector.tensor_tensor(total[:, cols], first[:, cols], second[:, cols], ADD)
                 nc.sync.dma_start(out[n * P : (n + 1) * P, :], total[:])
             y = next_y
+
+        for n in SCALED:
+            if not SPREAD:
+                for r in range(2):
+                    bank = bank_tile()
+                    for b in range(TOKEN_BLOCKS):
+                        nc.tensor.transpose(bank[:, 32 * b : 32 * b + P], token_block(gates[r], b), identity[:])
+                    nc.scalar.copy(gate_cols[:, r : 2 * TOKEN_BLOCKS : 2], bank[:, 0 : 32 * TOKEN_BLOCKS : 32])
+            scaled = tile_on("w2_codes2", [P, 2 * T], F32)
+            total = tile_on("total%d" % n, [P, T], F32)
+            for b in range(TOKEN_BLOCKS):
+                for r in range(2):
+                    i = r * TOKEN_BLOCKS + b
+                    nc.scalar.activation(token_block(scaled, i), turned[i], COPY, scale=gate_cols[:, 2 * b + r : 2 * b + r + 1])
+            for c0 in range(0, T, BANK):
+                c1 = min(c0 + BANK, T)
+                bank = bank_on(banks[1][c0 // BANK])
+                for b in range(c0 // P, c1 // P):
+                    for r in range(2):
+                        nc.tensor.matmul(
+                            token_block(bank, b - c0 // P),
+                            token_block(scaled, r * TOKEN_BLOCKS + b),
+                            identity[:],
+                            start=(r == 0),
+                            stop=(r == 1),
+                            is_transpose=True,
+                        )
+                nc.scalar.copy(total[:, c0:c1], bank[:, : c1 - c0])
+            nc.scalar.dma_start(out[n * P : (n + 1) * P, :], total[:])
 
         for n in PE_ADD:
             turned = tile_on("w2_codes2" if n == 0 else "turned", [P, T], F32)

@@ -43,36 +43,35 @@ PE_ADD = ()
 
 SLOTS = 12
 SLOT = RAW * 4
-V_PIECES = (4, 5, 6, 7)
+V_PIECES = (1, 5, 6, 7)
 Y_AFTER = (10, 14)
 SECOND_AFTER = (9, 14)
 LISTS_AFTER = 7
-CUTS = (0, 384, 640)
+CUTS = (0, 320, 512, 640)
 WHOLE_FIRST = False
-GROUPS = (((0, 2), (2, 3), (3, 4), (4, 5)), ((0, 1), (1, 3), (3, 4), (4, 5)), ((0, 2), (2, 4), (4, 5)))
+GROUPS = (((0, 2), (2, 4), (4, 5)), ((0, 1), (1, 3), (3, 4), (4, 5)), ((0, 2), (2, 4), (4, 5)))
 SPLIT_ADD = 320
 SMALL_ON_SYNC = True
 LAST_WHOLE = False
-V_COLUMNS = 256
-V_COLUMNS_LAST = 128
 S_ALONE = 1
 LATE = {0: 2, 1: 3, 2: 4}
 SPREAD = False
 GATE_AFTER = (11, 14)
 SCALED = (0,)
-TURN_ON_V = False
+Q_SPLIT = False
+SCALED_ON = ("w2_rounded1", "w2_codes2")
+END_PLANES = (4, 0, 2, 2, 2, 2, 2)
+HEAD_PLANES = (0, 0, 2, 0)
+TURN_PLANES = (4, 0, 2, 2)
+H_AT = ((4, False), (4, False), (4, False), (4, False))
+STORE_SPLIT = True
 H_FIRST = True
-SIG_AT = ((3, 4), (3, 4), (3, 4), (3, 4), (2, 4))
-TT_AT = ((4, 5), (4, 5), (4, 5), (4, 4))
-TURN_AT = (6, 6, 6, 5)
+SIG_AT = ((3, 3), (3, 3), (3, 3), (3, 4), (4, 7))
 Y_LAST_ON_V = False
-V_HEAD = 128
 HEAD_TO = 4
-TURNS_TO = 4
-TURN_V = 512
-TURN_S = 0
+TURNS_TO = 14
 ROUNDED_BUFS = 4
-CODE_BUFS = 3
+CODE_BUFS = 5
 
 
 def tile_moe_pkd_glu_sigmoid_kernel(
@@ -108,6 +107,10 @@ def tile_moe_pkd_glu_sigmoid_kernel(
 
         slot_list = keep.tile([P, S // LIST_COLUMN], U16, name="slot_list")
         nc.sync.dma_start(slot_list[:], offs)
+        if SPREAD:
+            gate_rows = keep.tile([P, T], F32, name="gate_rows", align_bytes=ALIGN)
+            nc.vector.memset(gate_rows[:], 0.0)
+            nc.sync.dma_start(gate_rows[0:2, :], gate[:, 0, :])
         token_scales = keep.tile([P, T // 4], I32, name="token_scales", align_bytes=ALIGN)
         nc.vector.memset(token_scales[:], 0)
         token_words = keep.tile([P, PASSES * T], I32, name="token_words", align_bytes=ALIGN)
@@ -120,10 +123,6 @@ def tile_moe_pkd_glu_sigmoid_kernel(
             small.dma_start(
                 token_scales[32 * q : 32 * q + 4 * PASSES, :], x_scales[:, 4 * q : 4 * q + 4, :].bitcast(I32)
             )
-        if SPREAD:
-            gate_rows = keep.tile([P, T], F32, name="gate_rows", align_bytes=ALIGN)
-            nc.gpsimd.memset(gate_rows[:], 0.0)
-            small.dma_start(gate_rows[0:2, :], gate[:, 0, :])
         identity = keep.tile([P, P], F32, name="identity")
         make_identity(nc, identity[:])
 
@@ -192,27 +191,34 @@ def tile_moe_pkd_glu_sigmoid_kernel(
                 nc.sync.dma_start(parts[-1].rearrange("p (j c) -> p j c", j=PACK), rows[:, :, c0 : c0 + width])
             loaded[chunk] = parts
 
-        def interleave(copy, dst, src):
-            copy(dst.rearrange("p (c i) j -> p c j i", i=4), src.rearrange("p j (c i) -> p c j i", i=4))
+        def vector_planes(chunk):
+            if chunk < HEAD_TO:
+                return HEAD_PLANES[chunk]
+            if chunk >= 12 and chunk < LAST_CHUNK:
+                return END_PLANES[chunk - 12]
+            if chunk >= TURNS_TO:
+                return PACK // 2
+            return TURN_PLANES[chunk % CHUNKS]
 
         def quantise_chunk(chunk):
             rounded_tags[chunk] = "words%d" % LATE[chunk] if chunk in LATE else next_tag("rounded", ROUNDED_BUFS)
             rounded = tile_on(rounded_tags[chunk], [P, RAW], BF16)
             parts = loaded[chunk]
-            dst = rounded[:].rearrange("p (c j) -> p c j", j=PACK)
-            width = H // len(parts)
-            cut = V_COLUMNS_LAST if chunk == LAST_CHUNK else (0 if chunk < S_ALONE else (V_HEAD if chunk < HEAD_TO else V_COLUMNS))
-            if HEAD_TO <= chunk < TURNS_TO:
-                cut = TURN_V if chunk % PASSES == 0 else TURN_S
+            dst = rounded[:].rearrange("p (t m j) -> p m j t", t=PACK, j=PACK)
             for n_part, part in enumerate(parts):
-                src = part.rearrange("p (j c) -> p j c", j=PACK)
-                for copy, c0, c1 in ((nc.vector.tensor_copy, 0, cut), (nc.scalar.copy, cut, width)):
-                    if c1 > c0:
-                        interleave(copy, dst[:, n_part * width + c0 : n_part * width + c1, :], src[:, :, c0:c1])
+                src = part.rearrange("p (j m t) -> p m j t", j=PACK, t=PACK)
+                ms = slice(n_part * P // len(parts), (n_part + 1) * P // len(parts))
+                for t0 in range(0, PACK, 2):
+                    copy = nc.vector.tensor_copy if t0 < vector_planes(chunk) else nc.scalar.copy
+                    copy(dst[:, ms, :, t0 : t0 + 2], src[:, :, :, t0 : t0 + 2])
             codes = tile_on(next_tag("codes", CODE_BUFS), [P, H], U32)
             scales = tile_on(next_tag("scales", CODE_BUFS), [P, H], U8)
             step = H // len(parts)
-            for w0 in range(0, H, step):
+            starts = range(0, H, step)
+            if Q_SPLIT and chunk < LAST_CHUNK and chunk >= S_ALONE:
+                step = H // 2
+                starts = (step, 0)
+            for w0 in starts:
                 nc.vector.quantize_mx(
                     out=codes[:, w0 : w0 + step].bitcast(FP8X4),
                     scales=scales[:, w0 : w0 + step],
@@ -227,36 +233,35 @@ def tile_moe_pkd_glu_sigmoid_kernel(
         def half_slots(half):
             return slice(half * HALF, (half + 1) * HALF)
 
-        def first_layer_pass(bank, e, half, o, codes, scales):
-            nc.tensor.matmul_mx(
-                out=bank[:],
-                lhsT=slot_words[e][:, o * C + half * HALF : o * C + (half + 1) * HALF].bitcast(FP8X4),
-                lhsT_scale=slot_scales[e][4 * o :, half_slots(half)],
-                rhs=codes[:].bitcast(FP8X4),
-                rhs_scale=scales[:],
-                start=(o == 0),
-                stop=(o == PASSES - 1),
-            )
+        def first_layer_product(passes, e, half):
+            bank = bank_tile()
+            for t in range(PACK):
+                cols = slice(t * P, (t + 1) * P)
+                for o, (codes, scales) in enumerate(passes):
+                    nc.tensor.matmul_mx(
+                        out=bank[:, t * HALF : (t + 1) * HALF],
+                        lhsT=codes[:, cols].bitcast(FP8X4),
+                        lhsT_scale=scales[:, cols],
+                        rhs=slot_words[e][:, o * C + half * HALF : o * C + (half + 1) * HALF].bitcast(FP8X4),
+                        rhs_scale=slot_scales[e][4 * o :, half_slots(half)],
+                        start=(o == 0),
+                        stop=(o == PASSES - 1),
+                    )
+            return bank[:].rearrange("p (t s) -> p s t", t=PACK)
 
         def sigmoid_onto(spent, pre):
-            nc.scalar.activation(spent, pre[:].rearrange("p (r c) -> p r c", r=2), SIGMOID)
-            return spent
+            sig = spent.rearrange("p (s t) -> p s t", t=PACK)
+            nc.scalar.activation(sig, pre, SIGMOID)
+            return sig
 
         h_codes = [keep.tile([P, C], U32, name="h_codes%d" % e, align_bytes=ALIGN) for e in range(E)]
         h_scales = [keep.tile([P, C], U8, name="h_scales%d" % e, align_bytes=ALIGN) for e in range(E)]
 
-        def hidden_rows(h_rows, lin, sig, bank):
-            nc.vector.tensor_tensor(h_rows.rearrange("p (r c) -> p r c", r=2), lin[:].rearrange("p (r c) -> p r c", r=2), sig, MULT)
-            words = h_rows.bitcast(F32)
-            for u in range(2):
-                nc.tensor.transpose(token_block(bank, u), words[:, u : H // 2 : 2], identity[:])
+        def hidden_half(h_half, lin, sig):
+            nc.vector.tensor_tensor(h_half.rearrange("p (s t) -> p s t", t=PACK), lin, sig, MULT)
 
-        def quantise_hidden(e, slots, h_words):
-            nc.vector.quantize_mx(
-                out=h_codes[e][:, slots].bitcast(FP8X4),
-                scales=h_scales[e][:, slots],
-                in_=h_words.bitcast(BF16),
-            )
+        def quantise_hidden(e, slots, h_bf):
+            nc.vector.quantize_mx(out=h_codes[e][:, slots].bitcast(FP8X4), scales=h_scales[e][:, slots], in_=h_bf)
 
         first_list = keep.tile([P, T // LIST_COLUMN], U16, name="first_list")
         second_list = keep.tile([P, T // LIST_COLUMN], U16, name="second_list")
@@ -298,56 +303,42 @@ def tile_moe_pkd_glu_sigmoid_kernel(
         all_slots = slice(0, C)
         pre, lin, sig, turned_h = {}, {}, {}, {}
 
-        def spent_rows(place):
+        def spent(place, half):
             if place < LAST_CHUNK:
-                return loaded[place][0].rearrange("p (j c) -> p j c", j=PACK)
+                return loaded[place][0][:, half * BANK : (half + 1) * BANK]
             if place < LAST_CHUNK + 2:
-                return loaded[LAST_CHUNK][place - LAST_CHUNK].rearrange("p (j c) -> p j c", j=2)
-            return pieces[place - LAST_CHUNK - 2].rearrange("p (j c) -> p j c", j=1)
-
-        def turn_out(copy, h_words, bank):
-            n = h_words.shape[1]
-            copy(h_words.rearrange("p k (s u) -> p k s u", u=2), bank[:, : n * 2 * P].rearrange("p (k u s) -> p k s u", k=n, u=2))
+                return loaded[LAST_CHUNK][place - LAST_CHUNK][:, half * BANK : (half + 1) * BANK]
+            return pieces[place - LAST_CHUNK - 2]
 
         def after(place):
             for e in range(E):
                 for half in halves:
                     if e * CHUNKS + SIG_AT[e][half] == place:
-                        rows = spent_rows(place)
-                        if place < LAST_CHUNK:
-                            onto = rows[:, 0:2, C:] if (half == 0 or SIG_AT[e][0] != SIG_AT[e][1]) else rows[:, 2:4, C:]
-                        elif place < LAST_CHUNK + 2:
-                            onto = rows[:, half, :].rearrange("p (r c) -> p r c", r=2)
-                        else:
-                            onto = rows[:, 0, :].rearrange("p (r c) -> p r c", r=2)
-                        sig[e, half] = sigmoid_onto(onto, pre[e][half])
+                        sig[e, half] = sigmoid_onto(spent(place, half), pre[e][half])
             for e in range(E - 1):
-                for half in halves:
-                    if e * CHUNKS + TT_AT[e][half] == place:
-                        if half == 0:
-                            turned_h[e] = bank_tile()
-                        h_rows = spent_rows(place)[:, half, :C].bitcast(BF16)
-                        hidden_rows(h_rows, lin[e][half], sig[e, half], turned_h[e][:, half * C : (half + 1) * C])
-                if e * CHUNKS + TURN_AT[e] == place:
-                    h_words = spent_rows(place)[:, 2:4, C:]
-                    turn_out(nc.scalar.copy, h_words, turned_h[e])
+                offset, tied = H_AT[e]
+                if e * CHUNKS + offset == place:
+                    if tied:
+                        h_bf = loaded[place][0][:, 3 * BANK :].bitcast(BF16)
+                    else:
+                        h_bf = tile_on(next_tag("h_bf", 2), [P, C * PACK], BF16)[:]
                     for half in halves:
-                        quantise_hidden(e, half_slots(half), h_words[:, half, :])
+                        hidden_half(h_bf[:, half * BANK : (half + 1) * BANK], lin[e][half], sig[e, half])
+                    quantise_hidden(e, all_slots, h_bf)
 
         for e in range(E):
+            done = []
             for c in range(CHUNKS):
                 chunk = e * CHUNKS + c
                 if chunk == LAST_CHUNK:
                     for number in range(EARLY_PIECES):
                         load_piece(number)
                 load_chunk(chunk)
-                codes, scales = quantise_chunk(chunk)
-                sums = (pre, lin)[c // PASSES]
-                if c % PASSES == 0:
-                    sums[e] = [bank_tile() for half in halves]
-                for half in halves:
-                    first_layer_pass(sums[e][half], e, half, c % PASSES, codes, scales)
+                done.append(quantise_chunk(chunk))
+                if c == PASSES - 1:
+                    pre[e] = [first_layer_product(done[:PASSES], e, half) for half in halves]
                 after(chunk)
+            lin[e] = [first_layer_product(done[PASSES:], e, half) for half in halves]
         after(LAST_CHUNK + 1)
 
         for number in range(EARLY_PIECES, N_TILES * E):
@@ -390,15 +381,11 @@ def tile_moe_pkd_glu_sigmoid_kernel(
             round_pieces([number])
             after(LAST_CHUNK + 2 + number)
         def last_hidden():
-            h_rows = keep.tile([P, C // HALF * H], BF16, name="h_rows_last", align_bytes=ALIGN)
-            h_words = keep.tile([P, BANK], F32, name="h_last", align_bytes=ALIGN)
+            h_bf = keep.tile([P, C * PACK], BF16, name="h_last", align_bytes=ALIGN)
             for half in halves:
-                bank = bank_tile()
-                hidden_rows(h_rows[:, half * H : (half + 1) * H], lin[E - 1][half], sig[E - 1, half], bank)
-                words = h_words[:, half * C : (half + 1) * C]
-                copy = nc.vector.tensor_copy if TURN_ON_V else nc.scalar.copy
-                turn_out(copy, words.rearrange("p (k c) -> p k c", k=1), bank)
-                quantise_hidden(E - 1, half_slots(half), words)
+                hidden_half(h_bf[:, half * BANK : (half + 1) * BANK], lin[E - 1][half], sig[E - 1, half])
+            for half in halves:
+                quantise_hidden(E - 1, half_slots(half), h_bf[:, half * BANK : (half + 1) * BANK])
 
         if H_FIRST:
             last_hidden()
@@ -462,17 +449,19 @@ def tile_moe_pkd_glu_sigmoid_kernel(
 
         for n in SCALED:
             if not SPREAD:
-                for r in range(2):
-                    bank = bank_tile()
+                gate_banks = [bank_tile(), bank_on(banks[0][-1])]
+                for r, bank in enumerate(gate_banks):
                     for b in range(TOKEN_BLOCKS):
                         nc.tensor.transpose(bank[:, 32 * b : 32 * b + P], token_block(gates[r], b), identity[:])
                     nc.scalar.copy(gate_cols[:, r : 2 * TOKEN_BLOCKS : 2], bank[:, 0 : 32 * TOKEN_BLOCKS : 32])
-            scaled = tile_on("w2_codes2", [P, 2 * T], F32)
+            scaled = [tile_on(SCALED_ON[r], [P, T], F32) for r in range(2)]
             total = tile_on("total%d" % n, [P, T], F32)
-            for b in range(TOKEN_BLOCKS):
-                for r in range(2):
-                    i = r * TOKEN_BLOCKS + b
-                    nc.scalar.activation(token_block(scaled, i), turned[i], COPY, scale=gate_cols[:, 2 * b + r : 2 * b + r + 1])
+            order = [(b, r) for b in range(TOKEN_BLOCKS) for r in range(2)]
+            if SCALED_ON[0] != SCALED_ON[1][:-1]:
+                order.sort(key=lambda br: br[1])
+            for b, r in order:
+                i = r * TOKEN_BLOCKS + b
+                nc.scalar.activation(token_block(scaled[r], b), turned[i], COPY, scale=gate_cols[:, 2 * b + r : 2 * b + r + 1])
             for c0 in range(0, T, BANK):
                 c1 = min(c0 + BANK, T)
                 bank = bank_on(banks[1][c0 // BANK])
@@ -480,14 +469,17 @@ def tile_moe_pkd_glu_sigmoid_kernel(
                     for r in range(2):
                         nc.tensor.matmul(
                             token_block(bank, b - c0 // P),
-                            token_block(scaled, r * TOKEN_BLOCKS + b),
+                            token_block(scaled[r], b),
                             identity[:],
                             start=(r == 0),
                             stop=(r == 1),
                             is_transpose=True,
                         )
                 nc.scalar.copy(total[:, c0:c1], bank[:, : c1 - c0])
-            nc.scalar.dma_start(out[n * P : (n + 1) * P, :], total[:])
+                if STORE_SPLIT:
+                    nc.scalar.dma_start(out[n * P : (n + 1) * P, c0:c1], total[:, c0:c1])
+            if not STORE_SPLIT:
+                nc.scalar.dma_start(out[n * P : (n + 1) * P, :], total[:])
 
         for n in PE_ADD:
             turned = tile_on("w2_codes2" if n == 0 else "turned", [P, T], F32)
@@ -512,7 +504,7 @@ def tile_moe_pkd_glu_sigmoid_kernel(
                 for b in range(c0 // P, c1 // P):
                     nc.tensor.transpose(token_block(bank, b - c0 // P), token_block(turned, b), identity[:])
                 nc.scalar.copy(total[:, c0:c1], bank[:, : c1 - c0])
-            nc.sync.dma_start(out[n * P : (n + 1) * P, :], total[:])
+            nc.scalar.dma_start(out[n * P : (n + 1) * P, :], total[:])
 
         first = tile_on("first2", [P, T], F32)
         total = tile_on("total2", [P, T], F32)

@@ -54,7 +54,11 @@ SPLIT_ADD = 320
 SMALL_ON_SYNC = True
 LAST_WHOLE = False
 S_ALONE = 1
-LATE = {0: 2, 1: 3, 2: 4}
+LATE = {0: (2, 4), 2: (4, 5)}
+EARLY = ((0, 2),)
+SCALE_GROUPS = ((0, 2), (2, 4), (4, 5))
+WINDOW = 704
+S_WHOLE = False
 SPREAD = False
 GATE_AFTER = (11, 14)
 SCALED = (0,)
@@ -62,7 +66,7 @@ Q_SPLIT = False
 SCALED_ON = ("w2_rounded1", "w2_codes2")
 END_PLANES = (4, 0, 2, 2, 2, 2, 2)
 HEAD_PLANES = (0, 0, 2, 0)
-TURN_PLANES = (4, 0, 2, 2)
+TURN_PLANES = (4, 0, 2, 0)
 H_AT = ((4, False), (4, False), (4, False), (4, False))
 STORE_SPLIT = True
 H_FIRST = True
@@ -111,17 +115,19 @@ def tile_moe_pkd_glu_sigmoid_kernel(
             gate_rows = keep.tile([P, T], F32, name="gate_rows", align_bytes=ALIGN)
             nc.vector.memset(gate_rows[:], 0.0)
             nc.sync.dma_start(gate_rows[0:2, :], gate[:, 0, :])
-        token_scales = keep.tile([P, T // 4], I32, name="token_scales", align_bytes=ALIGN)
+        token_scales = keep.tile([P, WINDOW // 4], I32, name="token_scales", align_bytes=ALIGN)
         nc.vector.memset(token_scales[:], 0)
-        token_words = keep.tile([P, PASSES * T], I32, name="token_words", align_bytes=ALIGN)
+        token_words = keep.tile([P, T + WINDOW], I32, name="token_words", align_bytes=ALIGN)
+        if WINDOW > T:
+            nc.vector.memset(token_words[:, PASSES * T :], 0)
         nc.sync.dma_start(
-            token_words[:].rearrange("p (o t) -> p o t", o=PASSES),
+            token_words[:, : PASSES * T].rearrange("p (o t) -> p o t", o=PASSES),
             x_words.rearrange("o p t r -> p o (t r)").bitcast(I32),
         )
         small = nc.sync if SMALL_ON_SYNC else nc.scalar
         for q in range(4):
             small.dma_start(
-                token_scales[32 * q : 32 * q + 4 * PASSES, :], x_scales[:, 4 * q : 4 * q + 4, :].bitcast(I32)
+                token_scales[32 * q : 32 * q + 4 * PASSES, : T // 4], x_scales[:, 4 * q : 4 * q + 4, :].bitcast(I32)
             )
         identity = keep.tile([P, P], F32, name="identity")
         make_identity(nc, identity[:])
@@ -151,21 +157,25 @@ def tile_moe_pkd_glu_sigmoid_kernel(
 
         slot_words, slot_scales = {}, {}
 
-        def expert_offsets(e):
-            return slot_list[:, e * C // LIST_COLUMN : (e + 1) * C // LIST_COLUMN]
+        def expert_offsets(e0, e1):
+            return slot_list[:, e0 * C // LIST_COLUMN : e1 * C // LIST_COLUMN]
 
-        def gather_words(e):
-            slot_words[e] = tile_on("words%d" % e, [P, PASSES * C], U32)
+        def gather_words(e0, e1):
+            width = (e1 - e0) * C
+            words = tile_on("words%d" % e0, [P, PASSES * width], U32)
             for o in range(PASSES):
-                window = token_words[:, o * T : (o + 1) * T].bitcast(U32)
-                nc.vector.tensor_copy(slot_words[e][:, o * C : (o + 1) * C], window.indirect(expert_offsets(e)))
+                window = token_words[:, o * T : o * T + WINDOW].bitcast(U32)
+                nc.vector.tensor_copy(words[:, o * width : (o + 1) * width], window.indirect(expert_offsets(e0, e1)))
+            for e in range(e0, e1):
+                slot_words[e] = [words[:, o * width + (e - e0) * C : o * width + (e - e0 + 1) * C] for o in range(PASSES)]
 
-        for e in range(E):
-            if e not in LATE.values():
-                gather_words(e)
-        for e in range(E):
-            slot_scales[e] = keep.tile([P, C], U8, name="slot_scales%d" % e, align_bytes=ALIGN)
-            nc.vector.tensor_copy(slot_scales[e][:], token_scales[:].bitcast(U8).indirect(expert_offsets(e)))
+        for e0, e1 in EARLY:
+            gather_words(e0, e1)
+        for e0, e1 in SCALE_GROUPS:
+            gathered = keep.tile([P, (e1 - e0) * C], U8, name="slot_scales%d" % e0, align_bytes=ALIGN)
+            nc.vector.tensor_copy(gathered[:], token_scales[:].bitcast(U8).indirect(expert_offsets(e0, e1)))
+            for e in range(e0, e1):
+                slot_scales[e] = gathered[:, (e - e0) * C : (e - e0 + 1) * C]
 
         loaded, rounded_tags = {}, {}
 
@@ -201,13 +211,16 @@ def tile_moe_pkd_glu_sigmoid_kernel(
             return TURN_PLANES[chunk % CHUNKS]
 
         def quantise_chunk(chunk):
-            rounded_tags[chunk] = "words%d" % LATE[chunk] if chunk in LATE else next_tag("rounded", ROUNDED_BUFS)
+            rounded_tags[chunk] = "words%d" % LATE[chunk][0] if chunk in LATE else next_tag("rounded", ROUNDED_BUFS)
             rounded = tile_on(rounded_tags[chunk], [P, RAW], BF16)
             parts = loaded[chunk]
             dst = rounded[:].rearrange("p (t m j) -> p m j t", t=PACK, j=PACK)
             for n_part, part in enumerate(parts):
                 src = part.rearrange("p (j m t) -> p m j t", j=PACK, t=PACK)
                 ms = slice(n_part * P // len(parts), (n_part + 1) * P // len(parts))
+                if S_WHOLE and vector_planes(chunk) == 0:
+                    nc.scalar.copy(dst.rearrange("p m j (h t) -> p h m j t", h=2), src.rearrange("p m j (h t) -> p h m j t", h=2))
+                    continue
                 for t0 in range(0, PACK, 2):
                     copy = nc.vector.tensor_copy if t0 < vector_planes(chunk) else nc.scalar.copy
                     copy(dst[:, ms, :, t0 : t0 + 2], src[:, :, :, t0 : t0 + 2])
@@ -225,7 +238,7 @@ def tile_moe_pkd_glu_sigmoid_kernel(
                     in_=rounded[:, w0 * PACK : (w0 + step) * PACK],
                 )
             if chunk in LATE:
-                gather_words(LATE[chunk])
+                gather_words(*LATE[chunk])
             return codes, scales
 
         halves = range(C // HALF)
@@ -242,7 +255,7 @@ def tile_moe_pkd_glu_sigmoid_kernel(
                         out=bank[:, t * HALF : (t + 1) * HALF],
                         lhsT=codes[:, cols].bitcast(FP8X4),
                         lhsT_scale=scales[:, cols],
-                        rhs=slot_words[e][:, o * C + half * HALF : o * C + (half + 1) * HALF].bitcast(FP8X4),
+                        rhs=slot_words[e][o][:, half_slots(half)].bitcast(FP8X4),
                         rhs_scale=slot_scales[e][4 * o :, half_slots(half)],
                         start=(o == 0),
                         stop=(o == PASSES - 1),

@@ -54,15 +54,13 @@ SPLIT_ADD = 320
 SMALL_ON_SYNC = True
 LAST_WHOLE = False
 S_ALONE = 1
-LATE = {0: (2, 4), 2: (4, 5)}
-EARLY = ((0, 2),)
-SCALE_GROUPS = ((0, 2), (2, 4), (4, 5))
-WINDOW = 704
-S_WHOLE = False
+LATE = {0: 2, 1: 3, 2: 4}
 SPREAD = False
 GATE_AFTER = (11, 14)
 SCALED = (0,)
 Q_SPLIT = False
+S_EXTRA = 16
+EXTRA_AT = (14, 15, 16, 17, 18)
 SCALED_ON = ("w2_rounded1", "w2_codes2")
 END_PLANES = (4, 0, 2, 2, 2, 2, 2)
 HEAD_PLANES = (0, 0, 2, 0)
@@ -115,19 +113,17 @@ def tile_moe_pkd_glu_sigmoid_kernel(
             gate_rows = keep.tile([P, T], F32, name="gate_rows", align_bytes=ALIGN)
             nc.vector.memset(gate_rows[:], 0.0)
             nc.sync.dma_start(gate_rows[0:2, :], gate[:, 0, :])
-        token_scales = keep.tile([P, WINDOW // 4], I32, name="token_scales", align_bytes=ALIGN)
+        token_scales = keep.tile([P, T // 4], I32, name="token_scales", align_bytes=ALIGN)
         nc.vector.memset(token_scales[:], 0)
-        token_words = keep.tile([P, T + WINDOW], I32, name="token_words", align_bytes=ALIGN)
-        if WINDOW > T:
-            nc.vector.memset(token_words[:, PASSES * T :], 0)
+        token_words = keep.tile([P, PASSES * T], I32, name="token_words", align_bytes=ALIGN)
         nc.sync.dma_start(
-            token_words[:, : PASSES * T].rearrange("p (o t) -> p o t", o=PASSES),
+            token_words[:].rearrange("p (o t) -> p o t", o=PASSES),
             x_words.rearrange("o p t r -> p o (t r)").bitcast(I32),
         )
         small = nc.sync if SMALL_ON_SYNC else nc.scalar
         for q in range(4):
             small.dma_start(
-                token_scales[32 * q : 32 * q + 4 * PASSES, : T // 4], x_scales[:, 4 * q : 4 * q + 4, :].bitcast(I32)
+                token_scales[32 * q : 32 * q + 4 * PASSES, :], x_scales[:, 4 * q : 4 * q + 4, :].bitcast(I32)
             )
         identity = keep.tile([P, P], F32, name="identity")
         make_identity(nc, identity[:])
@@ -157,25 +153,21 @@ def tile_moe_pkd_glu_sigmoid_kernel(
 
         slot_words, slot_scales = {}, {}
 
-        def expert_offsets(e0, e1):
-            return slot_list[:, e0 * C // LIST_COLUMN : e1 * C // LIST_COLUMN]
+        def expert_offsets(e):
+            return slot_list[:, e * C // LIST_COLUMN : (e + 1) * C // LIST_COLUMN]
 
-        def gather_words(e0, e1):
-            width = (e1 - e0) * C
-            words = tile_on("words%d" % e0, [P, PASSES * width], U32)
+        def gather_words(e):
+            slot_words[e] = tile_on("words%d" % e, [P, PASSES * C], U32)
             for o in range(PASSES):
-                window = token_words[:, o * T : o * T + WINDOW].bitcast(U32)
-                nc.vector.tensor_copy(words[:, o * width : (o + 1) * width], window.indirect(expert_offsets(e0, e1)))
-            for e in range(e0, e1):
-                slot_words[e] = [words[:, o * width + (e - e0) * C : o * width + (e - e0 + 1) * C] for o in range(PASSES)]
+                window = token_words[:, o * T : (o + 1) * T].bitcast(U32)
+                nc.vector.tensor_copy(slot_words[e][:, o * C : (o + 1) * C], window.indirect(expert_offsets(e)))
 
-        for e0, e1 in EARLY:
-            gather_words(e0, e1)
-        for e0, e1 in SCALE_GROUPS:
-            gathered = keep.tile([P, (e1 - e0) * C], U8, name="slot_scales%d" % e0, align_bytes=ALIGN)
-            nc.vector.tensor_copy(gathered[:], token_scales[:].bitcast(U8).indirect(expert_offsets(e0, e1)))
-            for e in range(e0, e1):
-                slot_scales[e] = gathered[:, (e - e0) * C : (e - e0 + 1) * C]
+        for e in range(E):
+            if e not in LATE.values():
+                gather_words(e)
+        for e in range(E):
+            slot_scales[e] = keep.tile([P, C], U8, name="slot_scales%d" % e, align_bytes=ALIGN)
+            nc.vector.tensor_copy(slot_scales[e][:], token_scales[:].bitcast(U8).indirect(expert_offsets(e)))
 
         loaded, rounded_tags = {}, {}
 
@@ -211,15 +203,18 @@ def tile_moe_pkd_glu_sigmoid_kernel(
             return TURN_PLANES[chunk % CHUNKS]
 
         def quantise_chunk(chunk):
-            rounded_tags[chunk] = "words%d" % LATE[chunk][0] if chunk in LATE else next_tag("rounded", ROUNDED_BUFS)
+            rounded_tags[chunk] = "words%d" % LATE[chunk] if chunk in LATE else next_tag("rounded", ROUNDED_BUFS)
             rounded = tile_on(rounded_tags[chunk], [P, RAW], BF16)
             parts = loaded[chunk]
             dst = rounded[:].rearrange("p (t m j) -> p m j t", t=PACK, j=PACK)
             for n_part, part in enumerate(parts):
                 src = part.rearrange("p (j m t) -> p m j t", j=PACK, t=PACK)
                 ms = slice(n_part * P // len(parts), (n_part + 1) * P // len(parts))
-                if S_WHOLE and vector_planes(chunk) == 0:
-                    nc.scalar.copy(dst.rearrange("p m j (h t) -> p h m j t", h=2), src.rearrange("p m j (h t) -> p h m j t", h=2))
+                if chunk in EXTRA_AT:
+                    cut = P - S_EXTRA
+                    nc.vector.tensor_copy(dst[:, :cut, :, 0:2], src[:, :cut, :, 0:2])
+                    nc.scalar.copy(dst[:, :, :, 2:4], src[:, :, :, 2:4])
+                    nc.scalar.copy(dst[:, cut:, :, 0:2], src[:, cut:, :, 0:2])
                     continue
                 for t0 in range(0, PACK, 2):
                     copy = nc.vector.tensor_copy if t0 < vector_planes(chunk) else nc.scalar.copy
@@ -238,7 +233,7 @@ def tile_moe_pkd_glu_sigmoid_kernel(
                     in_=rounded[:, w0 * PACK : (w0 + step) * PACK],
                 )
             if chunk in LATE:
-                gather_words(*LATE[chunk])
+                gather_words(LATE[chunk])
             return codes, scales
 
         halves = range(C // HALF)
@@ -255,7 +250,7 @@ def tile_moe_pkd_glu_sigmoid_kernel(
                         out=bank[:, t * HALF : (t + 1) * HALF],
                         lhsT=codes[:, cols].bitcast(FP8X4),
                         lhsT_scale=scales[:, cols],
-                        rhs=slot_words[e][o][:, half_slots(half)].bitcast(FP8X4),
+                        rhs=slot_words[e][:, o * C + half * HALF : o * C + (half + 1) * HALF].bitcast(FP8X4),
                         rhs_scale=slot_scales[e][4 * o :, half_slots(half)],
                         start=(o == 0),
                         stop=(o == PASSES - 1),

@@ -27,53 +27,34 @@ CHUNKS = 2 * PASSES
 LAST_CHUNK = E * CHUNKS - 1
 RAW = PACK * H
 PIECE = PACK * P
+N_TILES = N // P
+PIECES = N_TILES * E
 HALF = C // 2
 BANK = 512
-N_TILES = N // P
+BANKS = 8
+TOKEN_BLOCKS = T // P
 LIST_COLUMN = 16
+SCALE_ROWS = 4
 ALIGN = 256
 
-TOKEN_BLOCKS = T // P
-BANKS = 8
-
-PAIRS_FROM = 2
-PAIRS_TO = 2
-EARLY_PIECES = 0
-PE_ADD = ()
-
-SLOTS = 12
-SLOT = RAW * 4
-V_PIECES = (1, 5, 6, 7)
-Y_AFTER = (10, 14)
-SECOND_AFTER = (9, 14)
-LISTS_AFTER = 7
-CUTS = (0, 320, 512, 640)
-WHOLE_FIRST = False
-GROUPS = (((0, 2), (2, 4), (4, 5)), ((0, 1), (1, 3), (3, 4), (4, 5)), ((0, 2), (2, 4), (4, 5)))
-SPLIT_ADD = 320
-SMALL_ON_SYNC = True
-LAST_WHOLE = False
-S_ALONE = 1
-LATE = {0: 2, 1: 3, 2: 4}
-SPREAD = False
-GATE_AFTER = (11, 14)
-SCALED = (0,)
-Q_SPLIT = False
-S_EXTRA = 16
-EXTRA_AT = (14, 15, 16, 17, 18)
-SCALED_ON = ("w2_rounded1", "w2_codes2")
-END_PLANES = (4, 0, 2, 2, 2, 2, 2)
-HEAD_PLANES = (0, 0, 2, 0)
-TURN_PLANES = (4, 0, 2, 0)
-H_AT = ((4, False), (4, False), (4, False), (4, False))
-STORE_SPLIT = True
-H_FIRST = True
-SIG_AT = ((3, 3), (3, 3), (3, 3), (3, 4), (4, 7))
-Y_LAST_ON_V = False
-HEAD_TO = 4
-TURNS_TO = 14
+RAW_PLACES = 12
+RAW_BYTES = 4 * RAW
 ROUNDED_BUFS = 4
 CODE_BUFS = 5
+HIDDEN_BUFS = 2
+
+HEAD_EXPERTS = 2
+SHARED_FROM = 14
+SCALAR_EXTRA = 16
+VECTOR_PIECES = (1, E, E + 1, E + 2)
+PAIRS = ((0, 2), (2, 4), (4, 5))
+GROUPS = (PAIRS, ((0, 1), (1, 3), (3, 4), (4, 5)), PAIRS)
+LISTS_AFTER = VECTOR_PIECES[-1]
+GATES_AFTER = (PIECES - 4, PIECES - 1)
+Y_AFTER = {1: 2 * E, 2: PIECES - 1}
+SECOND_AFTER = {0: 2 * E - 1, 1: PIECES - 1}
+MIDDLE_CUTS = (0, T // 2, T)
+LAST_CUTS = (0, T // 2, T - P, T)
 
 
 def tile_moe_pkd_glu_sigmoid_kernel(
@@ -101,18 +82,20 @@ def tile_moe_pkd_glu_sigmoid_kernel(
         def bank_on(tag):
             return psum.tile([P, BANK], F32, name="bank", tag=tag)
 
-        def bank_tile():
-            return bank_on(next_tag("bank", BANKS))
-
         def token_block(tile, b):
             return tile[:, b * P : (b + 1) * P]
 
+        def entries(list_tile, start, stop):
+            return list_tile[:, start // LIST_COLUMN : stop // LIST_COLUMN]
+
+        def cuts(edges):
+            return [slice(c0, c1) for c0, c1 in zip(edges, edges[1:])]
+
+        def quantise(codes, scales, values):
+            nc.vector.quantize_mx(out=codes.bitcast(FP8X4), scales=scales, in_=values)
+
         slot_list = keep.tile([P, S // LIST_COLUMN], U16, name="slot_list")
         nc.sync.dma_start(slot_list[:], offs)
-        if SPREAD:
-            gate_rows = keep.tile([P, T], F32, name="gate_rows", align_bytes=ALIGN)
-            nc.vector.memset(gate_rows[:], 0.0)
-            nc.sync.dma_start(gate_rows[0:2, :], gate[:, 0, :])
         token_scales = keep.tile([P, T // 4], I32, name="token_scales", align_bytes=ALIGN)
         nc.vector.memset(token_scales[:], 0)
         token_words = keep.tile([P, PASSES * T], I32, name="token_words", align_bytes=ALIGN)
@@ -120,120 +103,78 @@ def tile_moe_pkd_glu_sigmoid_kernel(
             token_words[:].rearrange("p (o t) -> p o t", o=PASSES),
             x_words.rearrange("o p t r -> p o (t r)").bitcast(I32),
         )
-        small = nc.sync if SMALL_ON_SYNC else nc.scalar
-        for q in range(4):
-            small.dma_start(
-                token_scales[32 * q : 32 * q + 4 * PASSES, :], x_scales[:, 4 * q : 4 * q + 4, :].bitcast(I32)
+        for q in range(P // 32):
+            nc.sync.dma_start(
+                token_scales[32 * q : 32 * q + SCALE_ROWS * PASSES, :],
+                x_scales[:, SCALE_ROWS * q : SCALE_ROWS * (q + 1), :].bitcast(I32),
             )
         identity = keep.tile([P, P], F32, name="identity")
         make_identity(nc, identity[:])
 
-        warm = keep.tile([P, 8], F32, name="warm")
-        nc.vector.memset(warm[:], 0.0)
-        nc.scalar.activation(warm[:], warm[:], SIGMOID)
-
         gates = [keep.tile([P, T], F32, name="gate%d" % r, align_bytes=ALIGN) for r in range(2)]
-        gate_cols = keep.tile([P, 2 * TOKEN_BLOCKS], F32, name="gate_cols")
-        if SPREAD:
-            bank = bank_tile()
-            for b in range(TOKEN_BLOCKS):
-                nc.tensor.transpose(bank[:, 32 * b : 32 * b + P], token_block(gate_rows, b), identity[:])
-            nc.scalar.copy(
-                gate_cols[:].rearrange("p (b r) -> p b r", r=2),
-                bank[:, : 32 * TOKEN_BLOCKS].rearrange("p (b c) -> p b c", c=32)[:, :, 0:2],
-            )
-            for r in range(2):
-                for c0 in range(0, T, BANK):
-                    c1 = min(c0 + BANK, T)
-                    bank = bank_tile()
-                    for b in range(c0 // P, c1 // P):
-                        column = gate_cols[:, 2 * b + r : 2 * b + r + 1].to_broadcast([P, P])
-                        nc.tensor.transpose(token_block(bank, b - c0 // P), column, identity[:])
-                    nc.scalar.copy(gates[r][:, c0:c1], bank[:, : c1 - c0])
+        gate_columns = keep.tile([P, 2 * TOKEN_BLOCKS], F32, name="gate_columns")
 
         slot_words, slot_scales = {}, {}
-
-        def expert_offsets(e):
-            return slot_list[:, e * C // LIST_COLUMN : (e + 1) * C // LIST_COLUMN]
 
         def gather_words(e):
             slot_words[e] = tile_on("words%d" % e, [P, PASSES * C], U32)
             for o in range(PASSES):
                 window = token_words[:, o * T : (o + 1) * T].bitcast(U32)
-                nc.vector.tensor_copy(slot_words[e][:, o * C : (o + 1) * C], window.indirect(expert_offsets(e)))
+                offsets = entries(slot_list, e * C, (e + 1) * C)
+                nc.vector.tensor_copy(slot_words[e][:, o * C : (o + 1) * C], window.indirect(offsets))
 
-        for e in range(E):
-            if e not in LATE.values():
-                gather_words(e)
+        for e in range(HEAD_EXPERTS):
+            gather_words(e)
         for e in range(E):
             slot_scales[e] = keep.tile([P, C], U8, name="slot_scales%d" % e, align_bytes=ALIGN)
-            nc.vector.tensor_copy(slot_scales[e][:], token_scales[:].bitcast(U8).indirect(expert_offsets(e)))
+            offsets = entries(slot_list, e * C, (e + 1) * C)
+            nc.vector.tensor_copy(slot_scales[e][:], token_scales[:].bitcast(U8).indirect(offsets))
 
-        loaded, rounded_tags = {}, {}
+        raw = {}
 
         def load_chunk(chunk):
             e, c = divmod(chunk, CHUNKS)
             w, o = (w1, w3)[c // PASSES], c % PASSES
-            if PAIRS_FROM <= chunk < PAIRS_TO:
-                if o == 0:
-                    pair = tile_at("pair%d" % chunk, chunk % SLOTS * SLOT, PASSES * RAW)
-                    nc.sync.dma_start(
-                        pair[:].rearrange("p (o x) -> p o x", o=PASSES),
-                        w[e].rearrange("(o p j) c -> p o (j c)", o=PASSES, j=PACK),
-                    )
-                    for k in range(PASSES):
-                        loaded[chunk + k] = [pair[:, k * RAW : (k + 1) * RAW]]
-                return
             rows = w[e, o * P * PACK : (o + 1) * P * PACK, :].rearrange("(p j) c -> p j c", j=PACK)
             width = H // 2 if chunk == LAST_CHUNK else H
-            parts = []
+            raw[chunk] = []
             for c0 in range(0, H, width):
-                offset = chunk % SLOTS * SLOT + c0 * PACK * 4
-                parts.append(tile_at("part%d_%d" % (chunk, c0), offset, PACK * width)[:])
-                nc.sync.dma_start(parts[-1].rearrange("p (j c) -> p j c", j=PACK), rows[:, :, c0 : c0 + width])
-            loaded[chunk] = parts
+                offset = chunk % RAW_PLACES * RAW_BYTES + 4 * PACK * c0
+                part = tile_at("part%d_%d" % (chunk, c0), offset, PACK * width)[:]
+                nc.sync.dma_start(part.rearrange("p (j c) -> p j c", j=PACK), rows[:, :, c0 : c0 + width])
+                raw[chunk].append(part)
 
         def vector_planes(chunk):
-            if chunk < HEAD_TO:
-                return HEAD_PLANES[chunk]
-            if chunk >= 12 and chunk < LAST_CHUNK:
-                return END_PLANES[chunk - 12]
-            if chunk >= TURNS_TO:
+            e, c = divmod(chunk, CHUNKS)
+            if chunk == LAST_CHUNK or c == PASSES:
                 return PACK // 2
-            return TURN_PLANES[chunk % CHUNKS]
+            return PACK if c == 0 and e > 0 else 0
 
         def quantise_chunk(chunk):
-            rounded_tags[chunk] = "words%d" % LATE[chunk] if chunk in LATE else next_tag("rounded", ROUNDED_BUFS)
-            rounded = tile_on(rounded_tags[chunk], [P, RAW], BF16)
-            parts = loaded[chunk]
+            late_expert = HEAD_EXPERTS + chunk
+            tag = "words%d" % late_expert if late_expert < E else next_tag("rounded", ROUNDED_BUFS)
+            rounded = tile_on(tag, [P, RAW], BF16)
+            parts = raw[chunk]
             dst = rounded[:].rearrange("p (t m j) -> p m j t", t=PACK, j=PACK)
             for n_part, part in enumerate(parts):
                 src = part.rearrange("p (j m t) -> p m j t", j=PACK, t=PACK)
-                ms = slice(n_part * P // len(parts), (n_part + 1) * P // len(parts))
-                if chunk in EXTRA_AT:
-                    cut = P - S_EXTRA
+                if SHARED_FROM <= chunk < LAST_CHUNK:
+                    cut = P - SCALAR_EXTRA
                     nc.vector.tensor_copy(dst[:, :cut, :, 0:2], src[:, :cut, :, 0:2])
                     nc.scalar.copy(dst[:, :, :, 2:4], src[:, :, :, 2:4])
                     nc.scalar.copy(dst[:, cut:, :, 0:2], src[:, cut:, :, 0:2])
-                    continue
-                for t0 in range(0, PACK, 2):
-                    copy = nc.vector.tensor_copy if t0 < vector_planes(chunk) else nc.scalar.copy
-                    copy(dst[:, ms, :, t0 : t0 + 2], src[:, :, :, t0 : t0 + 2])
+                else:
+                    words = slice(n_part * P // len(parts), (n_part + 1) * P // len(parts))
+                    for t0 in range(0, PACK, 2):
+                        copy = nc.vector.tensor_copy if t0 < vector_planes(chunk) else nc.scalar.copy
+                        copy(dst[:, words, :, t0 : t0 + 2], src[:, :, :, t0 : t0 + 2])
             codes = tile_on(next_tag("codes", CODE_BUFS), [P, H], U32)
             scales = tile_on(next_tag("scales", CODE_BUFS), [P, H], U8)
             step = H // len(parts)
-            starts = range(0, H, step)
-            if Q_SPLIT and chunk < LAST_CHUNK and chunk >= S_ALONE:
-                step = H // 2
-                starts = (step, 0)
-            for w0 in starts:
-                nc.vector.quantize_mx(
-                    out=codes[:, w0 : w0 + step].bitcast(FP8X4),
-                    scales=scales[:, w0 : w0 + step],
-                    in_=rounded[:, w0 * PACK : (w0 + step) * PACK],
-                )
-            if chunk in LATE:
-                gather_words(LATE[chunk])
+            for w0 in range(0, H, step):
+                quantise(codes[:, w0 : w0 + step], scales[:, w0 : w0 + step], rounded[:, w0 * PACK : (w0 + step) * PACK])
+            if late_expert < E:
+                gather_words(late_expert)
             return codes, scales
 
         halves = range(C // HALF)
@@ -241,133 +182,103 @@ def tile_moe_pkd_glu_sigmoid_kernel(
         def half_slots(half):
             return slice(half * HALF, (half + 1) * HALF)
 
+        def half_values(tile, half):
+            return tile[:, half * BANK : (half + 1) * BANK]
+
         def first_layer_product(passes, e, half):
-            bank = bank_tile()
+            bank = bank_on(next_tag("bank", BANKS))
             for t in range(PACK):
-                cols = slice(t * P, (t + 1) * P)
+                plane = slice(t * P, (t + 1) * P)
                 for o, (codes, scales) in enumerate(passes):
                     nc.tensor.matmul_mx(
                         out=bank[:, t * HALF : (t + 1) * HALF],
-                        lhsT=codes[:, cols].bitcast(FP8X4),
-                        lhsT_scale=scales[:, cols],
+                        lhsT=codes[:, plane].bitcast(FP8X4),
+                        lhsT_scale=scales[:, plane],
                         rhs=slot_words[e][:, o * C + half * HALF : o * C + (half + 1) * HALF].bitcast(FP8X4),
-                        rhs_scale=slot_scales[e][4 * o :, half_slots(half)],
+                        rhs_scale=slot_scales[e][SCALE_ROWS * o :, half_slots(half)],
                         start=(o == 0),
                         stop=(o == PASSES - 1),
                     )
             return bank[:].rearrange("p (t s) -> p s t", t=PACK)
 
-        def sigmoid_onto(spent, pre):
-            sig = spent.rearrange("p (s t) -> p s t", t=PACK)
-            nc.scalar.activation(sig, pre, SIGMOID)
-            return sig
-
         h_codes = [keep.tile([P, C], U32, name="h_codes%d" % e, align_bytes=ALIGN) for e in range(E)]
         h_scales = [keep.tile([P, C], U8, name="h_scales%d" % e, align_bytes=ALIGN) for e in range(E)]
+        pre, lin, sig = {}, {}, {}
 
-        def hidden_half(h_half, lin, sig):
-            nc.vector.tensor_tensor(h_half.rearrange("p (s t) -> p s t", t=PACK), lin, sig, MULT)
+        def sigmoid_onto(spent, e, half):
+            sig[e, half] = spent.rearrange("p (s t) -> p s t", t=PACK)
+            nc.scalar.activation(sig[e, half], pre[e][half], SIGMOID)
 
-        def quantise_hidden(e, slots, h_bf):
-            nc.vector.quantize_mx(out=h_codes[e][:, slots].bitcast(FP8X4), scales=h_scales[e][:, slots], in_=h_bf)
+        def hidden(h_values, e):
+            for half in halves:
+                by_slot = half_values(h_values, half).rearrange("p (s t) -> p s t", t=PACK)
+                nc.vector.tensor_tensor(by_slot, lin[e][half], sig[e, half], MULT)
 
-        first_list = keep.tile([P, T // LIST_COLUMN], U16, name="first_list")
-        second_list = keep.tile([P, T // LIST_COLUMN], U16, name="second_list")
+        inverse_lists = [keep.tile([P, T // LIST_COLUMN], U16, name="inverse_list%d" % r) for r in range(2)]
         w2_rounded = [tile_on("w2_rounded%d" % n, [P, E * PIECE], BF16) for n in range(N_TILES)]
         w2_codes = [tile_on("w2_codes%d" % n, [P, E * P], U32) for n in range(N_TILES)]
         w2_scales = [tile_on("w2_scales%d" % n, [P, E * P], U8) for n in range(N_TILES)]
-
-        pieces, y_at, second_at = [], {}, {}
-        piece_at = []
-        offset = (LAST_CHUNK + 1) % SLOTS * SLOT
-        for number in range(N_TILES * E):
-            if offset + 4 * (S + PIECE + T) > SLOTS * SLOT:
-                offset = 0
-            if number in Y_AFTER:
-                y_at[Y_AFTER.index(number) + 1] = offset
-                offset += 4 * S - ALIGN
-            piece_at.append(offset)
-            offset += 4 * PIECE
-            if number in SECOND_AFTER:
-                second_at[SECOND_AFTER.index(number)] = offset - ALIGN
-                offset += 4 * T - ALIGN
-
-        def load_piece(number):
-            tile_n, e = divmod(number, E)
-            pieces.append(tile_at("piece%d" % number, piece_at[number], PIECE)[:])
-            nc.sync.dma_start(
-                pieces[number].rearrange("p (j c) -> p j c", j=PACK),
-                w2[e, :, tile_n * P : (tile_n + 1) * P].rearrange("(p j) c -> p j c", j=PACK),
-            )
-
-        def round_pieces(numbers):
-            for number in numbers:
-                n, e = divmod(number, E)
-                dst = w2_rounded[n][:, e * PIECE : (e + 1) * PIECE].rearrange("p (c i j) -> p c j i", i=4, j=PACK)
-                src = pieces[number].rearrange("p (j c i) -> p c j i", i=4, j=PACK)
-                copy = nc.vector.tensor_copy if number in V_PIECES else nc.scalar.copy
-                copy(dst, src)
-
-        all_slots = slice(0, C)
-        pre, lin, sig, turned_h = {}, {}, {}, {}
-
-        def spent(place, half):
-            if place < LAST_CHUNK:
-                return loaded[place][0][:, half * BANK : (half + 1) * BANK]
-            if place < LAST_CHUNK + 2:
-                return loaded[LAST_CHUNK][place - LAST_CHUNK][:, half * BANK : (half + 1) * BANK]
-            return pieces[place - LAST_CHUNK - 2]
-
-        def after(place):
-            for e in range(E):
-                for half in halves:
-                    if e * CHUNKS + SIG_AT[e][half] == place:
-                        sig[e, half] = sigmoid_onto(spent(place, half), pre[e][half])
-            for e in range(E - 1):
-                offset, tied = H_AT[e]
-                if e * CHUNKS + offset == place:
-                    if tied:
-                        h_bf = loaded[place][0][:, 3 * BANK :].bitcast(BF16)
-                    else:
-                        h_bf = tile_on(next_tag("h_bf", 2), [P, C * PACK], BF16)[:]
-                    for half in halves:
-                        hidden_half(h_bf[:, half * BANK : (half + 1) * BANK], lin[e][half], sig[e, half])
-                    quantise_hidden(e, all_slots, h_bf)
 
         for e in range(E):
             done = []
             for c in range(CHUNKS):
                 chunk = e * CHUNKS + c
-                if chunk == LAST_CHUNK:
-                    for number in range(EARLY_PIECES):
-                        load_piece(number)
                 load_chunk(chunk)
                 done.append(quantise_chunk(chunk))
                 if c == PASSES - 1:
-                    pre[e] = [first_layer_product(done[:PASSES], e, half) for half in halves]
-                after(chunk)
+                    pre[e] = [first_layer_product(done, e, half) for half in halves]
+                if c == CHUNKS - 1 and e < E - 1:
+                    for half in halves if chunk < SHARED_FROM else halves[:1]:
+                        sigmoid_onto(half_values(raw[chunk][0], half), e, half)
+                if c == 0 and e > 0:
+                    if chunk > SHARED_FROM:
+                        sigmoid_onto(half_values(raw[chunk][0], 1), e - 1, 1)
+                    h_values = tile_on(next_tag("h_values", HIDDEN_BUFS), [P, C * PACK], BF16)[:]
+                    hidden(h_values, e - 1)
+                    quantise(h_codes[e - 1][:], h_scales[e - 1][:], h_values)
             lin[e] = [first_layer_product(done[PASSES:], e, half) for half in halves]
-        after(LAST_CHUNK + 1)
+        sigmoid_onto(half_values(raw[LAST_CHUNK][-1], 0), E - 1, 0)
 
-        for number in range(EARLY_PIECES, N_TILES * E):
-            load_piece(number)
+        pieces, y_at, second_at = [], {}, {}
+        offset = (LAST_CHUNK + 1) % RAW_PLACES * RAW_BYTES
+        for number in range(PIECES):
+            if offset + 4 * (S + PIECE + T) > RAW_PLACES * RAW_BYTES:
+                offset = 0
+            for n, after in Y_AFTER.items():
+                if after == number:
+                    y_at[n] = offset
+                    offset += 4 * S - ALIGN
+            n, e = divmod(number, E)
+            pieces.append(tile_at("piece%d" % number, offset, PIECE)[:])
+            nc.sync.dma_start(
+                pieces[number].rearrange("p (j c) -> p j c", j=PACK),
+                w2[e, :, n * P : (n + 1) * P].rearrange("(p j) c -> p j c", j=PACK),
+            )
+            offset += 4 * PIECE
+            for n, after in SECOND_AFTER.items():
+                if after == number:
+                    second_at[n] = offset - ALIGN
+                    offset += 4 * T - ALIGN
             if number == LISTS_AFTER:
-                nc.sync.dma_start(first_list[:], pos1)
-                nc.sync.dma_start(second_list[:], pos2)
-            if not SPREAD and number in GATE_AFTER:
-                for r in range(2):
-                    if GATE_AFTER[r] == number:
-                        nc.sync.dma_start(gates[r][:], gate[r, :P, :])
+                for list_tile, source in zip(inverse_lists, (pos1, pos2)):
+                    nc.sync.dma_start(list_tile[:], source)
+            for r, after in enumerate(GATES_AFTER):
+                if after == number:
+                    nc.sync.dma_start(gates[r][:], gate[r, :P, :])
+
+        def round_piece(number):
+            n, e = divmod(number, E)
+            dst = w2_rounded[n][:, e * PIECE : (e + 1) * PIECE].rearrange("p (c i j) -> p c j i", i=2, j=PACK)
+            src = pieces[number].rearrange("p (j c i) -> p c j i", i=2, j=PACK)
+            copy = nc.vector.tensor_copy if number in VECTOR_PIECES else nc.scalar.copy
+            copy(dst, src)
 
         def quantise_pieces(n):
             for e0, e1 in GROUPS[n]:
-                nc.vector.quantize_mx(
-                    out=w2_codes[n][:, e0 * P : e1 * P].bitcast(FP8X4),
-                    scales=w2_scales[n][:, e0 * P : e1 * P],
-                    in_=w2_rounded[n][:, e0 * PIECE : e1 * PIECE],
-                )
+                words = slice(e0 * P, e1 * P)
+                quantise(w2_codes[n][:, words], w2_scales[n][:, words], w2_rounded[n][:, e0 * PIECE : e1 * PIECE])
 
-        def slot_results(n, y, e0, e1, slots, on_vector=False):
+        def slot_results(n, y, e0, e1, slots):
             tag = next_tag("bank", BANKS)
             bank = bank_on(tag)
             width = slots.stop - slots.start
@@ -382,145 +293,95 @@ def tile_moe_pkd_glu_sigmoid_kernel(
                     stop=True,
                 )
             first_slot = e0 * C + slots.start
-            (nc.vector.tensor_copy if on_vector else nc.scalar.copy)(y[:, first_slot : first_slot + (e1 - e0) * width], bank[:, : (e1 - e0) * width])
+            nc.scalar.copy(y[:, first_slot : first_slot + (e1 - e0) * width], bank[:, : (e1 - e0) * width])
             return tag
 
+        all_slots = slice(0, C)
+        all_tokens = slice(0, T)
+
         for number in range(E):
-            round_pieces([number])
-            after(LAST_CHUNK + 2 + number)
-        def last_hidden():
-            h_bf = keep.tile([P, C * PACK], BF16, name="h_last", align_bytes=ALIGN)
-            for half in halves:
-                hidden_half(h_bf[:, half * BANK : (half + 1) * BANK], lin[E - 1][half], sig[E - 1, half])
-            for half in halves:
-                quantise_hidden(E - 1, half_slots(half), h_bf[:, half * BANK : (half + 1) * BANK])
-
-        if H_FIRST:
-            last_hidden()
+            round_piece(number)
+            if number == E // 2:
+                sigmoid_onto(pieces[number], E - 1, 1)
+        h_values = keep.tile([P, C * PACK], BF16, name="h_last", align_bytes=ALIGN)
+        hidden(h_values, E - 1)
+        for half in halves:
+            slots = half_slots(half)
+            quantise(h_codes[E - 1][:, slots], h_scales[E - 1][:, slots], half_values(h_values, half))
         quantise_pieces(0)
-        y = tile_on("y0", [P, S], F32)
+        y0 = tile_on("y0", [P, S], F32)
         for e0, e1 in GROUPS[0][:-1]:
-            slot_results(0, y, e0, e1, all_slots)
-        if not H_FIRST:
-            last_hidden()
-        for slots in [all_slots] if LAST_WHOLE else [half_slots(half) for half in halves]:
-            slot_results(0, y, E - 1, E, slots, Y_LAST_ON_V)
+            slot_results(0, y0, e0, e1, all_slots)
+        for half in halves:
+            slot_results(0, y0, E - 1, E, half_slots(half))
 
-        def gated(result, y, inverse_list, gate_tile, cols):
-            entries = inverse_list[:, cols.start // LIST_COLUMN : cols.stop // LIST_COLUMN]
-            nc.vector.tensor_tensor(result[:, cols], y[:].indirect(entries), gate_tile[:, cols], MULT)
-
-        def add_and_store(n, total, first, second, cols):
-            nc.vector.tensor_tensor(total[:, cols], first[:, cols], second[:, cols], ADD)
-            nc.sync.dma_start(out[n * P : (n + 1) * P, cols], total[:, cols])
-
-        ends = (E, max(Y_AFTER[0] + 1, 2 * E), N_TILES * E)
-
-        def make_y(n):
-            round_pieces(range(ends[n - 1], ends[n]))
+        def make_y(n, numbers):
+            for number in numbers:
+                round_piece(number)
             quantise_pieces(n)
             y = tile_at("y%d" % n, y_at[n], S)
             return y, [slot_results(n, y, e0, e1, all_slots) for e0, e1 in GROUPS[n]]
 
-        all_tokens = slice(0, T)
-        terms, banks = [], []
-        for n in range(N_TILES - 1):
-            first = tile_on("first%d" % n, [P, T], F32)
-            if n in SCALED:
-                nc.vector.tensor_copy(first[:], y[:].indirect(first_list[:]))
-            else:
-                gated(first, y, first_list, gates[0], all_tokens)
-            next_y, next_banks = make_y(n + 1)
-            second = tile_at("second%d" % n, second_at[n], T)
-            parts = [slice(0, SPLIT_ADD), slice(SPLIT_ADD, T)] if SPLIT_ADD and n not in PE_ADD else [all_tokens]
-            if n in SCALED:
-                nc.vector.tensor_copy(second[:], y[:].indirect(second_list[:]))
-                turned = []
-                for term in (first, second):
-                    for b in range(TOKEN_BLOCKS):
-                        place = len(turned) % (BANK // P)
-                        if place == 0:
-                            bank = bank_on(next_banks[len(turned) // (BANK // P)])
-                        turned.append(token_block(bank, place))
-                        nc.tensor.transpose(turned[-1], token_block(term, b), identity[:])
-            else:
-                for cols in parts:
-                    gated(second, y, second_list, gates[1], cols)
-            terms.append((first, second))
-            banks.append(next_banks)
-            if n not in PE_ADD and n not in SCALED:
-                total = tile_on("total%d" % n, [P, T], F32)
-                for cols in parts:
-                    nc.vector.tensor_tensor(total[:, cols], first[:, cols], second[:, cols], ADD)
-                nc.sync.dma_start(out[n * P : (n + 1) * P, :], total[:])
-            y = next_y
+        def gated(term, y, r, cols):
+            offsets = entries(inverse_lists[r], cols.start, cols.stop)
+            nc.vector.tensor_tensor(term[:, cols], y[:].indirect(offsets), gates[r][:, cols], MULT)
 
-        for n in SCALED:
-            if not SPREAD:
-                gate_banks = [bank_tile(), bank_on(banks[0][-1])]
-                for r, bank in enumerate(gate_banks):
-                    for b in range(TOKEN_BLOCKS):
-                        nc.tensor.transpose(bank[:, 32 * b : 32 * b + P], token_block(gates[r], b), identity[:])
-                    nc.scalar.copy(gate_cols[:, r : 2 * TOKEN_BLOCKS : 2], bank[:, 0 : 32 * TOKEN_BLOCKS : 32])
-            scaled = [tile_on(SCALED_ON[r], [P, T], F32) for r in range(2)]
-            total = tile_on("total%d" % n, [P, T], F32)
-            order = [(b, r) for b in range(TOKEN_BLOCKS) for r in range(2)]
-            if SCALED_ON[0] != SCALED_ON[1][:-1]:
-                order.sort(key=lambda br: br[1])
-            for b, r in order:
-                i = r * TOKEN_BLOCKS + b
-                nc.scalar.activation(token_block(scaled[r], b), turned[i], COPY, scale=gate_cols[:, 2 * b + r : 2 * b + r + 1])
-            for c0 in range(0, T, BANK):
-                c1 = min(c0 + BANK, T)
-                bank = bank_on(banks[1][c0 // BANK])
-                for b in range(c0 // P, c1 // P):
-                    for r in range(2):
-                        nc.tensor.matmul(
-                            token_block(bank, b - c0 // P),
-                            token_block(scaled[r], b),
-                            identity[:],
-                            start=(r == 0),
-                            stop=(r == 1),
-                            is_transpose=True,
-                        )
-                nc.scalar.copy(total[:, c0:c1], bank[:, : c1 - c0])
-                if STORE_SPLIT:
-                    nc.scalar.dma_start(out[n * P : (n + 1) * P, c0:c1], total[:, c0:c1])
-            if not STORE_SPLIT:
-                nc.scalar.dma_start(out[n * P : (n + 1) * P, :], total[:])
+        first = tile_on("first0", [P, T], F32)
+        nc.vector.tensor_copy(first[:], y0[:].indirect(inverse_lists[0][:]))
+        y1, y1_banks = make_y(1, range(E, Y_AFTER[1] + 1))
+        second = tile_at("second0", second_at[0], T)
+        nc.vector.tensor_copy(second[:], y0[:].indirect(inverse_lists[1][:]))
+        turned = []
+        for term in (first, second):
+            for b in range(TOKEN_BLOCKS):
+                n_bank, place = divmod(len(turned), BANK // P)
+                if place == 0:
+                    bank = bank_on(y1_banks[n_bank])
+                turned.append(token_block(bank, place))
+                nc.tensor.transpose(turned[-1], token_block(term, b), identity[:])
 
-        for n in PE_ADD:
-            turned = tile_on("w2_codes2" if n == 0 else "turned", [P, T], F32)
-            total = tile_on("total%d" % n, [P, T], F32)
-            for k, c0 in enumerate(range(0, T, BANK)):
-                c1 = min(c0 + BANK, T)
-                bank = bank_on(banks[0][k]) if n == 0 else bank_tile()
-                for b in range(c0 // P, c1 // P):
-                    for r in range(2):
-                        nc.tensor.matmul(
-                            token_block(bank, b - c0 // P),
-                            token_block(terms[n][r], b),
-                            identity[:],
-                            start=(r == 0),
-                            stop=(r == 1),
-                            is_transpose=True,
-                        )
-                nc.scalar.copy(turned[:, c0:c1], bank[:, : c1 - c0])
-            for k, c0 in enumerate(range(0, T, BANK)):
-                c1 = min(c0 + BANK, T)
-                bank = bank_on(banks[1][k]) if n == 0 else bank_tile()
-                for b in range(c0 // P, c1 // P):
-                    nc.tensor.transpose(token_block(bank, b - c0 // P), token_block(turned, b), identity[:])
-                nc.scalar.copy(total[:, c0:c1], bank[:, : c1 - c0])
-            nc.scalar.dma_start(out[n * P : (n + 1) * P, :], total[:])
+        first = tile_on("first1", [P, T], F32)
+        gated(first, y1, 0, all_tokens)
+        y2, y2_banks = make_y(2, range(Y_AFTER[1] + 1, PIECES))
+        second = tile_at("second1", second_at[1], T)
+        for cols in cuts(MIDDLE_CUTS):
+            gated(second, y1, 1, cols)
+        total = tile_on("total1", [P, T], F32)
+        for cols in cuts(MIDDLE_CUTS):
+            nc.vector.tensor_tensor(total[:, cols], first[:, cols], second[:, cols], ADD)
+        nc.sync.dma_start(out[P : 2 * P, :], total[:])
+
+        gate_banks = [bank_on(tag) for tag in (next_tag("bank", BANKS), y1_banks[-1])]
+        for r, bank in enumerate(gate_banks):
+            for b in range(TOKEN_BLOCKS):
+                nc.tensor.transpose(bank[:, 32 * b : 32 * b + P], token_block(gates[r], b), identity[:])
+            nc.scalar.copy(gate_columns[:, r : 2 * TOKEN_BLOCKS : 2], bank[:, 0 : 32 * TOKEN_BLOCKS : 32])
+        scaled = [tile_on(tag, [P, T], F32) for tag in ("w2_rounded1", "w2_codes2")]
+        total = tile_on("total0", [P, T], F32)
+        for r in range(2):
+            for b in range(TOKEN_BLOCKS):
+                scale = gate_columns[:, 2 * b + r : 2 * b + r + 1]
+                nc.scalar.activation(token_block(scaled[r], b), turned[r * TOKEN_BLOCKS + b], COPY, scale=scale)
+        for tag, cols in zip(y2_banks, cuts((0, BANK, T))):
+            bank = bank_on(tag)
+            for b in range(cols.start // P, cols.stop // P):
+                for r in range(2):
+                    nc.tensor.matmul(
+                        token_block(bank, b - cols.start // P),
+                        token_block(scaled[r], b),
+                        identity[:],
+                        start=(r == 0),
+                        stop=(r == 1),
+                        is_transpose=True,
+                    )
+            nc.scalar.copy(total[:, cols], bank[:, : cols.stop - cols.start])
+            nc.scalar.dma_start(out[0:P, cols], total[:, cols])
 
         first = tile_on("first2", [P, T], F32)
         total = tile_on("total2", [P, T], F32)
         second = tile_on("second2", [P, T], F32)
-        if WHOLE_FIRST:
-            gated(first, y, first_list, gates[0], all_tokens)
-        for cols in [slice(c0, c1) for c0, c1 in zip(CUTS, CUTS[1:])]:
-            if not WHOLE_FIRST:
-                gated(first, y, first_list, gates[0], cols)
-            gated(second, y, second_list, gates[1], cols)
-            add_and_store(2, total, first, second, cols)
+        for cols in cuts(LAST_CUTS):
+            gated(first, y2, 0, cols)
+            gated(second, y2, 1, cols)
+            nc.vector.tensor_tensor(total[:, cols], first[:, cols], second[:, cols], ADD)
+            nc.sync.dma_start(out[2 * P : 3 * P, cols], total[:, cols])

@@ -45,6 +45,7 @@ HIDDEN_BUFS = 2
 
 HEAD_EXPERTS = 2
 SHARED_FROM = 14
+PAIRED = range(PASSES, 3 * CHUNKS)
 SCALAR_EXTRA = 16
 VECTOR_PIECES = (1, E, E + 1, E + 2)
 PAIRS = ((0, 2), (2, 4), (4, 5))
@@ -136,6 +137,16 @@ def tile_moe_pkd_glu_sigmoid_kernel(
             e, c = divmod(chunk, CHUNKS)
             w, o = (w1, w3)[c // PASSES], c % PASSES
             rows = w[e, o * P * PACK : (o + 1) * P * PACK, :].rearrange("(p j) c -> p j c", j=PACK)
+            if chunk in PAIRED:
+                if o == 0:
+                    both = tile_at("both%d" % chunk, chunk % RAW_PLACES * RAW_BYTES, PASSES * RAW)
+                    nc.sync.dma_start(
+                        both[:].rearrange("p (o x) -> p o x", o=PASSES),
+                        w[e].rearrange("(o p j) c -> p o (j c)", o=PASSES, j=PACK),
+                    )
+                    for later in range(PASSES):
+                        raw[chunk + later] = [both[:, later * RAW : (later + 1) * RAW]]
+                return
             width = H // 2 if chunk == LAST_CHUNK else H
             raw[chunk] = []
             for c0 in range(0, H, width):
@@ -146,9 +157,9 @@ def tile_moe_pkd_glu_sigmoid_kernel(
 
         def vector_planes(chunk):
             e, c = divmod(chunk, CHUNKS)
-            if chunk == LAST_CHUNK or c == PASSES:
+            if chunk in (PASSES, LAST_CHUNK):
                 return PACK // 2
-            return PACK if c == 0 and e > 0 else 0
+            return PACK if c % PASSES == 0 and e > 0 else 0
 
         def quantise_chunk(chunk):
             late_expert = HEAD_EXPERTS + chunk

@@ -1,7 +1,6 @@
 from contextlib import ExitStack
 
 import concourse.mybir as mybir
-from concourse.masks import make_identity
 
 K, T, E, C, H, N = 1024, 640, 5, 256, 512, 384
 S = E * C
@@ -47,14 +46,9 @@ HEAD_EXPERTS = 2
 SHARED_FROM = 14
 PAIRED = range(PASSES, 3 * CHUNKS)
 SCALAR_EXTRA = 16
-VECTOR_PIECES = (1, E, E + 1, E + 2)
 PAIRS = ((0, 2), (2, 4), (4, 5))
-GROUPS = (PAIRS, ((0, 1), (1, 3), (3, 4), (4, 5)), PAIRS)
-LISTS_AFTER = VECTOR_PIECES[-1]
-GATES_AFTER = (PIECES - 4, PIECES - 1)
-Y_AFTER = {1: 2 * E, 2: PIECES - 1}
-SECOND_AFTER = {0: 2 * E - 1, 1: PIECES - 1}
-MIDDLE_CUTS = (0, T // 2, T)
+LISTS_AFTER = 4
+GATES_AFTER = (11, PIECES - 1)
 LAST_CUTS = (0, T // 2, T - P, T)
 
 
@@ -77,8 +71,8 @@ def tile_moe_pkd_glu_sigmoid_kernel(
         def tile_on(tag, shape, dtype):
             return rings.tile(shape, dtype, name="tile", tag=tag, align_bytes=ALIGN)
 
-        def tile_at(name, offset, columns):
-            return stream.tile([P, columns], F32, name=name, align_bytes=ALIGN, offset=offset)
+        def tile_at(name, offset, columns, dtype=F32):
+            return stream.tile([P, columns], dtype, name=name, align_bytes=ALIGN, offset=offset)
 
         def bank_on(tag):
             return psum.tile([P, BANK], F32, name="bank", tag=tag)
@@ -109,11 +103,7 @@ def tile_moe_pkd_glu_sigmoid_kernel(
                 token_scales[32 * q : 32 * q + SCALE_ROWS * PASSES, :],
                 x_scales[:, SCALE_ROWS * q : SCALE_ROWS * (q + 1), :].bitcast(I32),
             )
-        identity = keep.tile([P, P], F32, name="identity")
-        make_identity(nc, identity[:])
-
         gates = [keep.tile([P, T], F32, name="gate%d" % r, align_bytes=ALIGN) for r in range(2)]
-        gate_columns = keep.tile([P, 2 * TOKEN_BLOCKS], F32, name="gate_columns")
 
         slot_words, slot_scales = {}, {}
 
@@ -226,9 +216,6 @@ def tile_moe_pkd_glu_sigmoid_kernel(
                 nc.vector.tensor_tensor(by_slot, lin[e][half], sig[e, half], MULT)
 
         inverse_lists = [keep.tile([P, T // LIST_COLUMN], U16, name="inverse_list%d" % r) for r in range(2)]
-        w2_rounded = [tile_on("w2_rounded%d" % n, [P, E * PIECE], BF16) for n in range(N_TILES)]
-        w2_codes = [tile_on("w2_codes%d" % n, [P, E * P], U32) for n in range(N_TILES)]
-        w2_scales = [tile_on("w2_scales%d" % n, [P, E * P], U8) for n in range(N_TILES)]
 
         for e in range(E):
             done = []
@@ -250,26 +237,33 @@ def tile_moe_pkd_glu_sigmoid_kernel(
             lin[e] = [first_layer_product(done[PASSES:], e, half) for half in halves]
         sigmoid_onto(half_values(raw[LAST_CHUNK][-1], 0), E - 1, 0)
 
-        pieces, y_at, second_at = [], {}, {}
-        offset = (LAST_CHUNK + 1) % RAW_PLACES * RAW_BYTES
+        def place(number):
+            return number % RAW_PLACES * RAW_BYTES
+
+        def kept(name, columns, dtype):
+            return keep.tile([P, columns], dtype, name=name, align_bytes=ALIGN)
+
+        raw_groups = {}
+        group_offsets = {
+            (0, 0): place(8),
+            (0, 2): place(8) + 8 * PIECE,
+            (0, 4): place(9),
+            (1, 0): place(9) + 4 * PIECE,
+            (1, 2): place(10),
+            (1, 4): place(10) + 8 * PIECE,
+            (2, 0): place(11),
+            (2, 2): place(11) + 8 * PIECE,
+            (2, 4): place(0),
+        }
         for number in range(PIECES):
-            if offset + 4 * (S + PIECE + T) > RAW_PLACES * RAW_BYTES:
-                offset = 0
-            for n, after in Y_AFTER.items():
-                if after == number:
-                    y_at[n] = offset
-                    offset += 4 * S - ALIGN
             n, e = divmod(number, E)
-            pieces.append(tile_at("piece%d" % number, offset, PIECE)[:])
+            e0, e1 = PAIRS[e // 2]
+            if e == e0:
+                raw_groups[n, e0] = tile_at("pieces%d_%d" % (n, e0), group_offsets[n, e0], (e1 - e0) * PIECE)
             nc.sync.dma_start(
-                pieces[number].rearrange("p (j c) -> p j c", j=PACK),
+                raw_groups[n, e0][:, (e - e0) * PIECE : (e - e0 + 1) * PIECE].rearrange("p (j c) -> p j c", j=PACK),
                 w2[e, :, n * P : (n + 1) * P].rearrange("(p j) c -> p j c", j=PACK),
             )
-            offset += 4 * PIECE
-            for n, after in SECOND_AFTER.items():
-                if after == number:
-                    second_at[n] = offset - ALIGN
-                    offset += 4 * T - ALIGN
             if number == LISTS_AFTER:
                 for list_tile, source in zip(inverse_lists, (pos1, pos2)):
                     nc.sync.dma_start(list_tile[:], source)
@@ -277,122 +271,114 @@ def tile_moe_pkd_glu_sigmoid_kernel(
                 if after == number:
                     nc.sync.dma_start(gates[r][:], gate[r, :P, :])
 
-        def round_piece(number):
-            n, e = divmod(number, E)
-            dst = w2_rounded[n][:, e * PIECE : (e + 1) * PIECE].rearrange("p (c i j) -> p c j i", i=2, j=PACK)
-            src = pieces[number].rearrange("p (j c i) -> p c j i", i=2, j=PACK)
-            copy = nc.vector.tensor_copy if number in VECTOR_PIECES else nc.scalar.copy
-            copy(dst, src)
+        y = [kept("y%d" % n, S, F32) for n in range(N_TILES)]
+        terms, groups, rounded_groups = {}, {}, {}
+        rounded_places = (place(1), place(1) + RAW_BYTES // 2)
 
-        def quantise_pieces(n):
-            for e0, e1 in GROUPS[n]:
-                words = slice(e0 * P, e1 * P)
-                quantise(w2_codes[n][:, words], w2_scales[n][:, words], w2_rounded[n][:, e0 * PIECE : e1 * PIECE])
+        def round_group(n, e0, e1, offset):
+            rounded = tile_at("w2_rounded%d_%d" % (n, e0), offset, (e1 - e0) * PIECE, BF16)
+            dst = rounded[:].rearrange("p (e c i j) -> p e c j i", e=e1 - e0, i=2, j=PACK)
+            src = raw_groups[n, e0][:].rearrange("p (e j c i) -> p e c j i", e=e1 - e0, i=2, j=PACK)
+            if n == 0:
+                for e in range(e0, e1):
+                    copy = nc.vector.tensor_copy if e == 1 else nc.scalar.copy
+                    copy(dst[:, e - e0], src[:, e - e0])
+                    if e == E // 2:
+                        sigmoid_onto(raw_groups[n, e0][:, :PIECE], E - 1, 1)
+            else:
+                nc.vector.tensor_copy(dst, src)
+            rounded_groups[n, e0] = rounded
 
-        def slot_results(n, y, e0, e1, slots):
-            tag = next_tag("bank", BANKS)
-            bank = bank_on(tag)
+        def quantise_group(n, e0, e1):
+            if n > 0 and e1 == E:
+                codes = tile_at("w2_codes%d_%d" % (n, e0), place(2) + (n - 1) * RAW_BYTES // 2, (e1 - e0) * P, U32)
+            else:
+                codes = kept("w2_codes%d_%d" % (n, e0), (e1 - e0) * P, U32)
+            scales = kept("w2_scales%d_%d" % (n, e0), (e1 - e0) * P, U8)
+            quantise(codes[:], scales[:], rounded_groups[n, e0][:])
+            groups[n, e0] = (codes, scales)
+
+        def slot_results(n, e0, e1, slots):
+            bank = bank_on(next_tag("bank", BANKS))
             width = slots.stop - slots.start
             for e in range(e0, e1):
                 nc.tensor.matmul_mx(
                     out=bank[:, (e - e0) * width : (e - e0 + 1) * width],
-                    lhsT=w2_codes[n][:, e * P : (e + 1) * P].bitcast(FP8X4),
-                    lhsT_scale=w2_scales[n][:, e * P : (e + 1) * P],
+                    lhsT=token_block(groups[n, e0][0], e - e0).bitcast(FP8X4),
+                    lhsT_scale=token_block(groups[n, e0][1], e - e0),
                     rhs=h_codes[e][:, slots].bitcast(FP8X4),
                     rhs_scale=h_scales[e][:, slots],
                     start=True,
                     stop=True,
                 )
             first_slot = e0 * C + slots.start
-            nc.scalar.copy(y[:, first_slot : first_slot + (e1 - e0) * width], bank[:, : (e1 - e0) * width])
-            return tag
+            nc.scalar.copy(y[n][:, first_slot : first_slot + (e1 - e0) * width], bank[:, : (e1 - e0) * width])
+
+        def fetched(n, r, cols):
+            offsets = entries(inverse_lists[r], cols.start, cols.stop)
+            nc.scalar.activation(terms[n, r][:, cols], y[n][:].indirect(offsets), COPY)
+
+        def gated(n, r, cols, product=None):
+            fetched_term = terms[n, r]
+            if product is not None:
+                terms[n, r] = product
+            nc.vector.tensor_tensor(terms[n, r][:, cols], fetched_term[:, cols], gates[r][:, cols], MULT)
+
+        def fetched_gated(n, r, cols):
+            offsets = entries(inverse_lists[r], cols.start, cols.stop)
+            nc.vector.tensor_tensor(terms[n, r][:, cols], y[n][:].indirect(offsets), gates[r][:, cols], MULT)
+
+        def stored(n, cols):
+            first, second = terms[n, 0], terms[n, 1]
+            nc.vector.tensor_tensor(first[:, cols], first[:, cols], second[:, cols], ADD)
+            nc.sync.dma_start(out[n * P : (n + 1) * P, cols], first[:, cols])
 
         all_slots = slice(0, C)
-        all_tokens = slice(0, T)
-
-        for number in range(E):
-            round_piece(number)
-            if number == E // 2:
-                sigmoid_onto(pieces[number], E - 1, 1)
-        h_values = keep.tile([P, C * PACK], BF16, name="h_last", align_bytes=ALIGN)
+        tokens = slice(0, T)
+        last_parts = cuts(LAST_CUTS)
+        for number, (e0, e1) in enumerate(PAIRS):
+            round_group(0, e0, e1, place(5) + number * 4 * PIECE)
+        h_values = tile_at("h_last", rounded_places[1], C * PACK, BF16)
         hidden(h_values, E - 1)
         for half in halves:
             slots = half_slots(half)
             quantise(h_codes[E - 1][:, slots], h_scales[E - 1][:, slots], half_values(h_values, half))
-        quantise_pieces(0)
-        y0 = tile_on("y0", [P, S], F32)
-        for e0, e1 in GROUPS[0][:-1]:
-            slot_results(0, y0, e0, e1, all_slots)
+        for e0, e1 in PAIRS:
+            quantise_group(0, e0, e1)
+        for e0, e1 in PAIRS[:-1]:
+            slot_results(0, e0, e1, all_slots)
         for half in halves:
-            slot_results(0, y0, E - 1, E, half_slots(half))
-
-        def make_y(n, numbers):
-            for number in numbers:
-                round_piece(number)
-            quantise_pieces(n)
-            y = tile_at("y%d" % n, y_at[n], S)
-            return y, [slot_results(n, y, e0, e1, all_slots) for e0, e1 in GROUPS[n]]
-
-        def gated(term, y, r, cols):
-            offsets = entries(inverse_lists[r], cols.start, cols.stop)
-            nc.vector.tensor_tensor(term[:, cols], y[:].indirect(offsets), gates[r][:, cols], MULT)
-
-        first = tile_on("first0", [P, T], F32)
-        nc.vector.tensor_copy(first[:], y0[:].indirect(inverse_lists[0][:]))
-        y1, y1_banks = make_y(1, range(E, Y_AFTER[1] + 1))
-        second = tile_at("second0", second_at[0], T)
-        nc.vector.tensor_copy(second[:], y0[:].indirect(inverse_lists[1][:]))
-        turned = []
-        for term in (first, second):
-            for b in range(TOKEN_BLOCKS):
-                n_bank, place = divmod(len(turned), BANK // P)
-                if place == 0:
-                    bank = bank_on(y1_banks[n_bank])
-                turned.append(token_block(bank, place))
-                nc.tensor.transpose(turned[-1], token_block(term, b), identity[:])
-
-        first = tile_on("first1", [P, T], F32)
-        gated(first, y1, 0, all_tokens)
-        y2, y2_banks = make_y(2, range(Y_AFTER[1] + 1, PIECES))
-        second = tile_at("second1", second_at[1], T)
-        for cols in cuts(MIDDLE_CUTS):
-            gated(second, y1, 1, cols)
-        total = tile_on("total1", [P, T], F32)
-        for cols in cuts(MIDDLE_CUTS):
-            nc.vector.tensor_tensor(total[:, cols], first[:, cols], second[:, cols], ADD)
-        nc.sync.dma_start(out[P : 2 * P, :], total[:])
-
-        gate_banks = [bank_on(tag) for tag in (next_tag("bank", BANKS), y1_banks[-1])]
-        for r, bank in enumerate(gate_banks):
-            for b in range(TOKEN_BLOCKS):
-                nc.tensor.transpose(bank[:, 32 * b : 32 * b + P], token_block(gates[r], b), identity[:])
-            nc.scalar.copy(gate_columns[:, r : 2 * TOKEN_BLOCKS : 2], bank[:, 0 : 32 * TOKEN_BLOCKS : 32])
-        scaled = [tile_on(tag, [P, T], F32) for tag in ("w2_rounded1", "w2_codes2")]
-        total = tile_on("total0", [P, T], F32)
-        for r in range(2):
-            for b in range(TOKEN_BLOCKS):
-                scale = gate_columns[:, 2 * b + r : 2 * b + r + 1]
-                nc.scalar.activation(token_block(scaled[r], b), turned[r * TOKEN_BLOCKS + b], COPY, scale=scale)
-        for tag, cols in zip(y2_banks, cuts((0, BANK, T))):
-            bank = bank_on(tag)
-            for b in range(cols.start // P, cols.stop // P):
-                for r in range(2):
-                    nc.tensor.matmul(
-                        token_block(bank, b - cols.start // P),
-                        token_block(scaled[r], b),
-                        identity[:],
-                        start=(r == 0),
-                        stop=(r == 1),
-                        is_transpose=True,
-                    )
-            nc.scalar.copy(total[:, cols], bank[:, : cols.stop - cols.start])
-            nc.scalar.dma_start(out[0:P, cols], total[:, cols])
-
-        first = tile_on("first2", [P, T], F32)
-        total = tile_on("total2", [P, T], F32)
-        second = tile_on("second2", [P, T], F32)
-        for cols in cuts(LAST_CUTS):
-            gated(first, y2, 0, cols)
-            gated(second, y2, 1, cols)
-            nc.vector.tensor_tensor(total[:, cols], first[:, cols], second[:, cols], ADD)
-            nc.sync.dma_start(out[2 * P : 3 * P, cols], total[:, cols])
+            slot_results(0, E - 1, E, half_slots(half))
+        for key in ((0, 0), (2, 0), (2, 1)):
+            terms[key] = kept("term%d_%d" % key, T, F32)
+        fetched(0, 0, tokens)
+        turn = 1
+        for n in (1, 2):
+            for e0, e1 in PAIRS:
+                round_group(n, e0, e1, rounded_places[turn % 2])
+                turn = turn + 1
+                quantise_group(n, e0, e1)
+                slot_results(n, e0, e1, all_slots)
+                if (n, e0) == (2, 0):
+                    gated(0, 0, tokens, tile_at("product0_0", group_offsets[2, 0], T))
+            if n == 1:
+                terms[0, 1] = tile_at("term0_1", place(2) + ALIGN, T)
+                fetched(0, 1, tokens)
+        terms[1, 0] = tile_at("term1_0", place(2) + RAW_BYTES // 2 + ALIGN, T)
+        terms[1, 1] = tile_at("term1_1", rounded_places[0] - 4 * T + PIECE, T)
+        fetched(1, 0, tokens)
+        for cols in last_parts:
+            fetched(2, 0, cols)
+            if cols.start > 0:
+                fetched(2, 1, cols)
+        fetched_gated(1, 1, tokens)
+        gated(0, 1, tokens, tile_at("product0_1", rounded_places[0] + PIECE, T))
+        stored(0, tokens)
+        fetched_gated(2, 1, last_parts[0])
+        gated(1, 0, tokens)
+        stored(1, tokens)
+        for cols in last_parts:
+            gated(2, 0, cols)
+            if cols.start > 0:
+                gated(2, 1, cols)
+            stored(2, cols)

@@ -1,6 +1,7 @@
 from contextlib import ExitStack
 
 import concourse.mybir as mybir
+from concourse.masks import make_identity
 
 K, T, E, C, H, N = 1024, 640, 5, 256, 512, 384
 S = E * C
@@ -44,11 +45,10 @@ HIDDEN_BUFS = 2
 
 HEAD_EXPERTS = 2
 SHARED_FROM = 14
-PAIRED = range(PASSES, 3 * CHUNKS)
+PAIRED = range(3 * CHUNKS)
 SCALAR_EXTRA = 16
 PAIRS = ((0, 2), (2, 4), (4, 5))
 LISTS_AFTER = 4
-GATES_AFTER = (11, PIECES - 1)
 LAST_CUTS = (0, T // 2, T - P, T)
 
 
@@ -90,20 +90,40 @@ def tile_moe_pkd_glu_sigmoid_kernel(
             nc.vector.quantize_mx(out=codes.bitcast(FP8X4), scales=scales, in_=values)
 
         slot_list = keep.tile([P, S // LIST_COLUMN], U16, name="slot_list")
-        nc.sync.dma_start(slot_list[:], offs)
         token_scales = keep.tile([P, T // 4], I32, name="token_scales", align_bytes=ALIGN)
         nc.vector.memset(token_scales[:], 0)
+        gate_rows = keep.tile([P, T], F32, name="gate_rows", align_bytes=ALIGN)
+        nc.vector.memset(gate_rows[:], 0.0)
         token_words = keep.tile([P, PASSES * T], I32, name="token_words", align_bytes=ALIGN)
         nc.sync.dma_start(
             token_words[:].rearrange("p (o t) -> p o t", o=PASSES),
             x_words.rearrange("o p t r -> p o (t r)").bitcast(I32),
         )
+        nc.sync.dma_start(slot_list[:], offs)
         for q in range(P // 32):
             nc.sync.dma_start(
                 token_scales[32 * q : 32 * q + SCALE_ROWS * PASSES, :],
                 x_scales[:, SCALE_ROWS * q : SCALE_ROWS * (q + 1), :].bitcast(I32),
             )
+        nc.sync.dma_start(gate_rows[0:2, :], gate[:, 0, :])
+        identity = keep.tile([P, P], F32, name="identity")
+        make_identity(nc, identity[:])
+
         gates = [keep.tile([P, T], F32, name="gate%d" % r, align_bytes=ALIGN) for r in range(2)]
+        columns = keep.tile([P, TOKEN_BLOCKS, 2], F32, name="gate_columns")
+        bank = bank_on(next_tag("bank", BANKS))
+        for b in range(TOKEN_BLOCKS):
+            nc.tensor.transpose(bank[:, 32 * b : 32 * b + P], token_block(gate_rows, b), identity[:])
+        nc.scalar.copy(columns[:], bank[:, : 32 * TOKEN_BLOCKS].rearrange("p (b c) -> p b c", c=32)[:, :, 0:2])
+        rest = bank_on(next_tag("bank", BANKS))
+        for r in range(2):
+            bank = bank_on(next_tag("bank", BANKS))
+            for b in range(TOKEN_BLOCKS):
+                spot = token_block(bank, b) if b < BANK // P else token_block(rest, r)
+                nc.tensor.transpose(spot, columns[:, b, r : r + 1].to_broadcast([P, P]), identity[:])
+            nc.scalar.copy(gates[r][:, :BANK], bank[:])
+        for r in range(2):
+            nc.scalar.copy(gates[r][:, BANK:], token_block(rest, r))
 
         slot_words, slot_scales = {}, {}
 
@@ -149,7 +169,7 @@ def tile_moe_pkd_glu_sigmoid_kernel(
             e, c = divmod(chunk, CHUNKS)
             if chunk in (PASSES, LAST_CHUNK):
                 return PACK // 2
-            return PACK if c % PASSES == 0 and e > 0 else 0
+            return PACK if c % PASSES == 0 else 0
 
         def quantise_chunk(chunk):
             late_expert = HEAD_EXPERTS + chunk
@@ -267,9 +287,6 @@ def tile_moe_pkd_glu_sigmoid_kernel(
             if number == LISTS_AFTER:
                 for list_tile, source in zip(inverse_lists, (pos1, pos2)):
                     nc.sync.dma_start(list_tile[:], source)
-            for r, after in enumerate(GATES_AFTER):
-                if after == number:
-                    nc.sync.dma_start(gates[r][:], gate[r, :P, :])
 
         y = [kept("y%d" % n, S, F32) for n in range(N_TILES)]
         terms, groups, rounded_groups = {}, {}, {}

@@ -31,7 +31,7 @@ N_TILES = N // P
 PIECES = N_TILES * E
 HALF = C // 2
 BANK = 512
-BANKS = 8
+BANKS = 5
 TOKEN_BLOCKS = T // P
 LIST_COLUMN = 16
 SCALE_ROWS = 4
@@ -109,21 +109,27 @@ def tile_moe_pkd_glu_sigmoid_kernel(
         identity = keep.tile([P, P], F32, name="identity")
         make_identity(nc, identity[:])
 
-        gates = [keep.tile([P, T], F32, name="gate%d" % r, align_bytes=ALIGN) for r in range(2)]
+        second_gate = tile_at("second_gate", RAW_PLACES * RAW_BYTES, T)
         columns = keep.tile([P, TOKEN_BLOCKS, 2], F32, name="gate_columns")
         bank = bank_on(next_tag("bank", BANKS))
         for b in range(TOKEN_BLOCKS):
             nc.tensor.transpose(bank[:, 32 * b : 32 * b + P], token_block(gate_rows, b), identity[:])
         nc.scalar.copy(columns[:], bank[:, : 32 * TOKEN_BLOCKS].rearrange("p (b c) -> p b c", c=32)[:, :, 0:2])
-        rest = bank_on(next_tag("bank", BANKS))
-        for r in range(2):
-            bank = bank_on(next_tag("bank", BANKS))
-            for b in range(TOKEN_BLOCKS):
-                spot = token_block(bank, b) if b < BANK // P else token_block(rest, r)
-                nc.tensor.transpose(spot, columns[:, b, r : r + 1].to_broadcast([P, P]), identity[:])
-            nc.scalar.copy(gates[r][:, :BANK], bank[:])
-        for r in range(2):
-            nc.scalar.copy(gates[r][:, BANK:], token_block(rest, r))
+
+        def spread(tags):
+            rest = bank_on(tags[2])
+            spans = []
+            for r in range(2):
+                bank = bank_on(tags[r])
+                for b in range(TOKEN_BLOCKS):
+                    spot = token_block(bank, b) if b < BANK // P else token_block(rest, r)
+                    nc.tensor.transpose(spot, columns[:, b, r : r + 1].to_broadcast([P, P]), identity[:])
+                spans.append((bank, rest[:, r * P : (r + 1) * P]))
+            return spans
+
+        psum_gates = spread(["gate_bank%d" % turn for turn in range(3)])
+        nc.scalar.copy(second_gate[:, :BANK], psum_gates[1][0][:])
+        nc.scalar.copy(second_gate[:, BANK:], psum_gates[1][1])
 
         slot_words, slot_scales = {}, {}
 
@@ -293,8 +299,9 @@ def tile_moe_pkd_glu_sigmoid_kernel(
         rounded_places = (place(1), place(1) + RAW_BYTES // 2)
 
         def round_group(n, e0, e1, offset):
-            rounded = tile_at("w2_rounded%d_%d" % (n, e0), offset, (e1 - e0) * PIECE, BF16)
-            dst = rounded[:].rearrange("p (e c i j) -> p e c j i", e=e1 - e0, i=2, j=PACK)
+            room = 3 * PIECE if (n, e0) == (2, 4) else (e1 - e0) * PIECE
+            rounded = tile_at("w2_rounded%d_%d" % (n, e0), offset, room, BF16)[:, : (e1 - e0) * PIECE]
+            dst = rounded.rearrange("p (e c i j) -> p e c j i", e=e1 - e0, i=2, j=PACK)
             src = raw_groups[n, e0][:].rearrange("p (e j c i) -> p e c j i", e=e1 - e0, i=2, j=PACK)
             if n == 0:
                 for e in range(e0, e1):
@@ -312,7 +319,7 @@ def tile_moe_pkd_glu_sigmoid_kernel(
             else:
                 codes = kept("w2_codes%d_%d" % (n, e0), (e1 - e0) * P, U32)
             scales = kept("w2_scales%d_%d" % (n, e0), (e1 - e0) * P, U8)
-            quantise(codes[:], scales[:], rounded_groups[n, e0][:])
+            quantise(codes[:], scales[:], rounded_groups[n, e0])
             groups[n, e0] = (codes, scales)
 
         def slot_results(n, e0, e1, slots):
@@ -335,15 +342,19 @@ def tile_moe_pkd_glu_sigmoid_kernel(
             offsets = entries(inverse_lists[r], cols.start, cols.stop)
             nc.scalar.activation(terms[n, r][:, cols], y[n][:].indirect(offsets), COPY)
 
-        def gated(n, r, cols, product=None):
+        def gated_from_psum(n, r, cols, product=None):
             fetched_term = terms[n, r]
             if product is not None:
                 terms[n, r] = product
-            nc.vector.tensor_tensor(terms[n, r][:, cols], fetched_term[:, cols], gates[r][:, cols], MULT)
+            if cols.start < BANK:
+                low = slice(cols.start, min(cols.stop, BANK))
+                nc.vector.tensor_tensor(terms[n, r][:, low], psum_gates[r][0][:, low], fetched_term[:, low], MULT)
+            if cols.stop > BANK:
+                nc.vector.tensor_tensor(terms[n, r][:, BANK:], psum_gates[r][1], fetched_term[:, BANK:], MULT)
 
         def fetched_gated(n, r, cols):
             offsets = entries(inverse_lists[r], cols.start, cols.stop)
-            nc.vector.tensor_tensor(terms[n, r][:, cols], y[n][:].indirect(offsets), gates[r][:, cols], MULT)
+            nc.vector.tensor_tensor(terms[n, r][:, cols], y[n][:].indirect(offsets), second_gate[:, cols], MULT)
 
         def stored(n, cols):
             first, second = terms[n, 0], terms[n, 1]
@@ -366,7 +377,7 @@ def tile_moe_pkd_glu_sigmoid_kernel(
             slot_results(0, e0, e1, all_slots)
         for half in halves:
             slot_results(0, E - 1, E, half_slots(half))
-        for key in ((0, 0), (2, 0), (2, 1)):
+        for key in ((0, 0), (1, 1), (2, 0), (2, 1)):
             terms[key] = kept("term%d_%d" % key, T, F32)
         fetched(0, 0, tokens)
         turn = 1
@@ -377,25 +388,33 @@ def tile_moe_pkd_glu_sigmoid_kernel(
                 quantise_group(n, e0, e1)
                 slot_results(n, e0, e1, all_slots)
                 if (n, e0) == (2, 0):
-                    gated(0, 0, tokens, tile_at("product0_0", group_offsets[2, 0], T))
+                    gated_from_psum(0, 0, tokens, tile_at("product0_0", group_offsets[2, 0], T))
             if n == 1:
-                terms[0, 1] = tile_at("term0_1", place(2) + ALIGN, T)
-                fetched(0, 1, tokens)
-        terms[1, 0] = tile_at("term1_0", place(2) + RAW_BYTES // 2 + ALIGN, T)
-        terms[1, 1] = tile_at("term1_1", rounded_places[0] - 4 * T + PIECE, T)
-        fetched(1, 0, tokens)
+                terms[1, 0] = kept("term1_0", T, F32)
+                fetched(1, 0, tokens)
+        first_half, second_half = cuts((0, BANK, T))
+        late = tile_at("term1_1_late", place(2) + RAW_BYTES // 2 + ALIGN, T)
+        offsets = entries(inverse_lists[1], second_half.start, second_half.stop)
+        nc.scalar.activation(late[:, second_half], y[1][:].indirect(offsets), COPY)
         for cols in last_parts:
             fetched(2, 0, cols)
-            if cols.start > 0:
-                fetched(2, 1, cols)
-        fetched_gated(1, 1, tokens)
-        gated(0, 1, tokens, tile_at("product0_1", rounded_places[0] + PIECE, T))
-        stored(0, tokens)
-        fetched_gated(2, 1, last_parts[0])
-        gated(1, 0, tokens)
+            fetched(2, 1, cols)
+        terms[0, 1] = tile_at("term0_1", rounded_places[0] - 4 * T + ALIGN, T)
+        terms[1, 1] = tile_at("term1_1", rounded_places[0] + ALIGN, T)
+        fetched_gated(0, 1, tokens)
+        fetched_gated(1, 1, first_half)
+        total = tile_at("total0", RAW_PLACES * RAW_BYTES, T)
+        nc.gpsimd.tensor_tensor(total[:], terms[0, 0][:], terms[0, 1][:], ADD)
+        nc.sync.dma_start(out[0:P, :], total[:])
+        gated_from_psum(1, 0, tokens, tile_at("product1_0", rounded_places[0] + ALIGN + 4 * T, T))
+        product = terms[1, 1]
+        terms[1, 1] = late
+        gated_from_psum(1, 1, second_half, product)
+        for r in range(2):
+            gated_from_psum(2, r, last_parts[0])
         stored(1, tokens)
         for cols in last_parts:
-            gated(2, 0, cols)
             if cols.start > 0:
-                gated(2, 1, cols)
+                for r in range(2):
+                    gated_from_psum(2, r, cols)
             stored(2, cols)

@@ -305,7 +305,7 @@ def tile_moe_pkd_glu_sigmoid_kernel(
             src = raw_groups[n, e0][:].rearrange("p (e j c i) -> p e c j i", e=e1 - e0, i=2, j=PACK)
             if n == 0:
                 for e in range(e0, e1):
-                    copy = nc.vector.tensor_copy if e == 1 else nc.scalar.copy
+                    copy = nc.vector.tensor_copy if e < 2 else nc.scalar.copy
                     copy(dst[:, e - e0], src[:, e - e0])
                     if e == E // 2:
                         sigmoid_onto(raw_groups[n, e0][:, :PIECE], E - 1, 1)

@@ -228,6 +228,20 @@ def tile_moe_pkd_glu_sigmoid_kernel(
                     )
             return bank[:].rearrange("p (t s) -> p s t", t=PACK)
 
+        def one_pass(banks, codes, scales, e, o):
+            for half in halves:
+                for t in range(PACK):
+                    plane = slice(t * P, (t + 1) * P)
+                    nc.tensor.matmul_mx(
+                        out=banks[half][:, t * HALF : (t + 1) * HALF],
+                        lhsT=codes[:, plane].bitcast(FP8X4),
+                        lhsT_scale=scales[:, plane],
+                        rhs=slot_words[e][:, o * C + half * HALF : o * C + (half + 1) * HALF].bitcast(FP8X4),
+                        rhs_scale=slot_scales[e][SCALE_ROWS * o :, half_slots(half)],
+                        start=(o == 0 and t == 0),
+                        stop=(o == PASSES - 1 and t == PACK - 1),
+                    )
+
         h_codes = [keep.tile([P, C], U32, name="h_codes%d" % e, align_bytes=ALIGN) for e in range(E)]
         h_scales = [keep.tile([P, C], U8, name="h_scales%d" % e, align_bytes=ALIGN) for e in range(E)]
         pre, lin, sig = {}, {}, {}
@@ -249,7 +263,12 @@ def tile_moe_pkd_glu_sigmoid_kernel(
                 chunk = e * CHUNKS + c
                 load_chunk(chunk)
                 done.append(quantise_chunk(chunk))
-                if c == PASSES - 1:
+                if e == E - 1:
+                    if c % PASSES == 0:
+                        last_banks = [bank_on(next_tag("bank", BANKS)) for half in halves]
+                        (pre, lin)[c // PASSES][e] = [bank[:].rearrange("p (t s) -> p s t", t=PACK) for bank in last_banks]
+                    one_pass(last_banks, *done[-1], e, c % PASSES)
+                elif c == PASSES - 1:
                     pre[e] = [first_layer_product(done, e, half) for half in halves]
                 if c == CHUNKS - 1 and e < E - 1:
                     for half in halves if chunk < SHARED_FROM else halves[:1]:
@@ -260,7 +279,8 @@ def tile_moe_pkd_glu_sigmoid_kernel(
                     h_values = tile_on(next_tag("h_values", HIDDEN_BUFS), [P, C * PACK], BF16)[:]
                     hidden(h_values, e - 1)
                     quantise(h_codes[e - 1][:], h_scales[e - 1][:], h_values)
-            lin[e] = [first_layer_product(done[PASSES:], e, half) for half in halves]
+            if e < E - 1:
+                lin[e] = [first_layer_product(done[PASSES:], e, half) for half in halves]
         sigmoid_onto(half_values(raw[LAST_CHUNK][-1], 0), E - 1, 0)
 
         def place(number):

from contextlib import ExitStack

import concourse.mybir as mybir
from concourse.masks import make_identity

K, T, E, C, H, N = 1024, 640, 5, 256, 512, 384
S = E * C
FLOPS = 2 * S * (2 * K * H + H * N)
BYTES = 4 * (2 * E * K * H + E * H * N + 2 * 128 * T + N * T) + K * T + K * T // 32 + 2 * 128 * (S + 2 * T) // 16

F32 = mybir.dt.float32
BF16 = mybir.dt.bfloat16
I32 = mybir.dt.int32
U32 = mybir.dt.uint32
U16 = mybir.dt.uint16
U8 = mybir.dt.uint8
FP8X4 = mybir.dt.float8_e4m3fn_x4
MULT = mybir.AluOpType.mult
ADD = mybir.AluOpType.add
SIGMOID = mybir.ActivationFunctionType.Sigmoid
COPY = mybir.ActivationFunctionType.Copy

P = 128
PACK = 4
PASSES = K // (P * PACK)
CHUNKS = 2 * PASSES
LAST_CHUNK = E * CHUNKS - 1
RAW = PACK * H
PIECE = PACK * P
N_TILES = N // P
PIECES = N_TILES * E
HALF = C // 2
BANK = 512
BANKS = 5
TOKEN_BLOCKS = T // P
LIST_COLUMN = 16
SCALE_ROWS = 4
ALIGN = 256

RAW_PLACES = 12
RAW_BYTES = 4 * RAW
ROUNDED_BUFS = 4
CODE_BUFS = 5
HIDDEN_BUFS = 2

HEAD_EXPERTS = 2
SHARED_FROM = 14
PAIRED = range(3 * CHUNKS)
SCALAR_EXTRA = 16
PAIRS = ((0, 2), (2, 4), (4, 5))
LISTS_AFTER = 4
LAST_CUTS = (0, T // 2, T - P, T)


def tile_moe_pkd_glu_sigmoid_kernel(
    tc, x_words, x_scales, w1, w3, w2, gate, offs, pos1, pos2, out
):
    nc = tc.nc
    with ExitStack() as ctx:
        keep = ctx.enter_context(tc.tile_pool(name="keep", bufs=1))
        rings = ctx.enter_context(tc.tile_pool(name="rings", bufs=1))
        stream = ctx.enter_context(tc.tile_pool(name="stream", bufs=1))
        psum = ctx.enter_context(tc.psum_pool(name="psum", bufs=1))
        turns = {}

        def next_tag(ring, depth):
            turn = turns.get(ring, 0)
            turns[ring] = turn + 1
            return "%s%d" % (ring, turn % depth)

        def tile_on(tag, shape, dtype):
            return rings.tile(shape, dtype, name="tile", tag=tag, align_bytes=ALIGN)

        def tile_at(name, offset, columns, dtype=F32):
            return stream.tile([P, columns], dtype, name=name, align_bytes=ALIGN, offset=offset)

        def bank_on(tag):
            return psum.tile([P, BANK], F32, name="bank", tag=tag)

        def token_block(tile, b):
            return tile[:, b * P : (b + 1) * P]

        def entries(list_tile, start, stop):
            return list_tile[:, start // LIST_COLUMN : stop // LIST_COLUMN]

        def cuts(edges):
            return [slice(c0, c1) for c0, c1 in zip(edges, edges[1:])]

        def quantise(codes, scales, values):
            nc.vector.quantize_mx(out=codes.bitcast(FP8X4), scales=scales, in_=values)

        slot_list = keep.tile([P, S // LIST_COLUMN], U16, name="slot_list")
        token_scales = keep.tile([P, T // 4], I32, name="token_scales", align_bytes=ALIGN)
        nc.vector.memset(token_scales[:], 0)
        gate_rows = keep.tile([P, T], F32, name="gate_rows", align_bytes=ALIGN)
        nc.vector.memset(gate_rows[:], 0.0)
        token_words = keep.tile([P, PASSES * T], I32, name="token_words", align_bytes=ALIGN)
        nc.sync.dma_start(
            token_words[:].rearrange("p (o t) -> p o t", o=PASSES),
            x_words.rearrange("o p t r -> p o (t r)").bitcast(I32),
        )
        nc.sync.dma_start(slot_list[:], offs)
        for q in range(P // 32):
            nc.sync.dma_start(
                token_scales[32 * q : 32 * q + SCALE_ROWS * PASSES, :],
                x_scales[:, SCALE_ROWS * q : SCALE_ROWS * (q + 1), :].bitcast(I32),
            )
        nc.sync.dma_start(gate_rows[0:2, :], gate[:, 0, :])
        identity = keep.tile([P, P], F32, name="identity")
        make_identity(nc, identity[:])

        second_gate = tile_at("second_gate", RAW_PLACES * RAW_BYTES, T)
        columns = keep.tile([P, TOKEN_BLOCKS, 2], F32, name="gate_columns")
        bank = bank_on(next_tag("bank", BANKS))
        for b in range(TOKEN_BLOCKS):
            nc.tensor.transpose(bank[:, 32 * b : 32 * b + P], token_block(gate_rows, b), identity[:])
        nc.scalar.copy(columns[:], bank[:, : 32 * TOKEN_BLOCKS].rearrange("p (b c) -> p b c", c=32)[:, :, 0:2])

        def spread(tags):
            rest = bank_on(tags[2])
            spans = []
            for r in range(2):
                bank = bank_on(tags[r])
                for b in range(TOKEN_BLOCKS):
                    spot = token_block(bank, b) if b < BANK // P else token_block(rest, r)
                    nc.tensor.transpose(spot, columns[:, b, r : r + 1].to_broadcast([P, P]), identity[:])
                spans.append((bank, rest[:, r * P : (r + 1) * P]))
            return spans

        psum_gates = spread(["gate_bank%d" % turn for turn in range(3)])
        nc.scalar.copy(second_gate[:, :BANK], psum_gates[1][0][:])
        nc.scalar.copy(second_gate[:, BANK:], psum_gates[1][1])

        slot_words, slot_scales = {}, {}

        def gather_words(e):
            slot_words[e] = tile_on("words%d" % e, [P, PASSES * C], U32)
            for o in range(PASSES):
                window = token_words[:, o * T : (o + 1) * T].bitcast(U32)
                offsets = entries(slot_list, e * C, (e + 1) * C)
                nc.vector.tensor_copy(slot_words[e][:, o * C : (o + 1) * C], window.indirect(offsets))

        for e in range(HEAD_EXPERTS):
            gather_words(e)
        for e in range(E):
            slot_scales[e] = keep.tile([P, C], U8, name="slot_scales%d" % e, align_bytes=ALIGN)
            offsets = entries(slot_list, e * C, (e + 1) * C)
            nc.vector.tensor_copy(slot_scales[e][:], token_scales[:].bitcast(U8).indirect(offsets))

        raw = {}

        def load_chunk(chunk):
            e, c = divmod(chunk, CHUNKS)
            w, o = (w1, w3)[c // PASSES], c % PASSES
            rows = w[e, o * P * PACK : (o + 1) * P * PACK, :].rearrange("(p j) c -> p j c", j=PACK)
            if chunk in PAIRED:
                if o == 0:
                    both = tile_at("both%d" % chunk, chunk % RAW_PLACES * RAW_BYTES, PASSES * RAW)
                    nc.sync.dma_start(
                        both[:].rearrange("p (o x) -> p o x", o=PASSES),
                        w[e].rearrange("(o p j) c -> p o (j c)", o=PASSES, j=PACK),
                    )
                    for later in range(PASSES):
                        raw[chunk + later] = [both[:, later * RAW : (later + 1) * RAW]]
                return
            width = H // 2 if chunk == LAST_CHUNK else H
            raw[chunk] = []
            for c0 in range(0, H, width):
                offset = chunk % RAW_PLACES * RAW_BYTES + 4 * PACK * c0
                part = tile_at("part%d_%d" % (chunk, c0), offset, PACK * width)[:]
                nc.sync.dma_start(part.rearrange("p (j c) -> p j c", j=PACK), rows[:, :, c0 : c0 + width])
                raw[chunk].append(part)

        def vector_planes(chunk):
            e, c = divmod(chunk, CHUNKS)
            if chunk in (PASSES, LAST_CHUNK):
                return PACK // 2
            return PACK if c % PASSES == 0 else 0

        def quantise_chunk(chunk):
            late_expert = HEAD_EXPERTS + chunk
            tag = "words%d" % late_expert if late_expert < E else next_tag("rounded", ROUNDED_BUFS)
            rounded = tile_on(tag, [P, RAW], BF16)
            parts = raw[chunk]
            dst = rounded[:].rearrange("p (t m j) -> p m j t", t=PACK, j=PACK)
            for n_part, part in enumerate(parts):
                src = part.rearrange("p (j m t) -> p m j t", j=PACK, t=PACK)
                if SHARED_FROM <= chunk < LAST_CHUNK:
                    cut = P - SCALAR_EXTRA
                    nc.vector.tensor_copy(dst[:, :cut, :, 0:2], src[:, :cut, :, 0:2])
                    nc.scalar.copy(dst[:, :, :, 2:4], src[:, :, :, 2:4])
                    nc.scalar.copy(dst[:, cut:, :, 0:2], src[:, cut:, :, 0:2])
                else:
                    words = slice(n_part * P // len(parts), (n_part + 1) * P // len(parts))
                    for t0 in range(0, PACK, 2):
                        copy = nc.vector.tensor_copy if t0 < vector_planes(chunk) else nc.scalar.copy
                        copy(dst[:, words, :, t0 : t0 + 2], src[:, :, :, t0 : t0 + 2])
            codes = tile_on(next_tag("codes", CODE_BUFS), [P, H], U32)
            scales = tile_on(next_tag("scales", CODE_BUFS), [P, H], U8)
            step = H // len(parts)
            for w0 in range(0, H, step):
                quantise(codes[:, w0 : w0 + step], scales[:, w0 : w0 + step], rounded[:, w0 * PACK : (w0 + step) * PACK])
            if late_expert < E:
                gather_words(late_expert)
            return codes, scales

        halves = range(C // HALF)

        def half_slots(half):
            return slice(half * HALF, (half + 1) * HALF)

        def half_values(tile, half):
            return tile[:, half * BANK : (half + 1) * BANK]

        def first_layer_product(passes, e, half):
            bank = bank_on(next_tag("bank", BANKS))
            for t in range(PACK):
                plane = slice(t * P, (t + 1) * P)
                for o, (codes, scales) in enumerate(passes):
                    nc.tensor.matmul_mx(
                        out=bank[:, t * HALF : (t + 1) * HALF],
                        lhsT=codes[:, plane].bitcast(FP8X4),
                        lhsT_scale=scales[:, plane],
                        rhs=slot_words[e][:, o * C + half * HALF : o * C + (half + 1) * HALF].bitcast(FP8X4),
                        rhs_scale=slot_scales[e][SCALE_ROWS * o :, half_slots(half)],
                        start=(o == 0),
                        stop=(o == PASSES - 1),
                    )
            return bank[:].rearrange("p (t s) -> p s t", t=PACK)

        def one_pass(banks, codes, scales, e, o):
            for half in halves:
                for t in range(PACK):
                    plane = slice(t * P, (t + 1) * P)
                    nc.tensor.matmul_mx(
                        out=banks[half][:, t * HALF : (t + 1) * HALF],
                        lhsT=codes[:, plane].bitcast(FP8X4),
                        lhsT_scale=scales[:, plane],
                        rhs=slot_words[e][:, o * C + half * HALF : o * C + (half + 1) * HALF].bitcast(FP8X4),
                        rhs_scale=slot_scales[e][SCALE_ROWS * o :, half_slots(half)],
                        start=(o == 0 and t == 0),
                        stop=(o == PASSES - 1 and t == PACK - 1),
                    )

        h_codes = [keep.tile([P, C], U32, name="h_codes%d" % e, align_bytes=ALIGN) for e in range(E)]
        h_scales = [keep.tile([P, C], U8, name="h_scales%d" % e, align_bytes=ALIGN) for e in range(E)]
        pre, lin, sig = {}, {}, {}

        def sigmoid_onto(spent, e, half):
            sig[e, half] = spent.rearrange("p (s t) -> p s t", t=PACK)
            nc.scalar.activation(sig[e, half], pre[e][half], SIGMOID)

        def hidden(h_values, e):
            for half in halves:
                by_slot = half_values(h_values, half).rearrange("p (s t) -> p s t", t=PACK)
                nc.vector.tensor_tensor(by_slot, lin[e][half], sig[e, half], MULT)

        inverse_lists = [keep.tile([P, T // LIST_COLUMN], U16, name="inverse_list%d" % r) for r in range(2)]

        for e in range(E):
            done = []
            for c in range(CHUNKS):
                chunk = e * CHUNKS + c
                load_chunk(chunk)
                done.append(quantise_chunk(chunk))
                if e == E - 1:
                    if c % PASSES == 0:
                        last_banks = [bank_on(next_tag("bank", BANKS)) for half in halves]
                        (pre, lin)[c // PASSES][e] = [bank[:].rearrange("p (t s) -> p s t", t=PACK) for bank in last_banks]
                    one_pass(last_banks, *done[-1], e, c % PASSES)
                elif c == PASSES - 1:
                    pre[e] = [first_layer_product(done, e, half) for half in halves]
                if c == CHUNKS - 1 and e < E - 1:
                    for half in halves if chunk < SHARED_FROM else halves[:1]:
                        sigmoid_onto(half_values(raw[chunk][0], half), e, half)
                if c == 0 and e > 0:
                    if chunk > SHARED_FROM:
                        sigmoid_onto(half_values(raw[chunk][0], 1), e - 1, 1)
                    h_values = tile_on(next_tag("h_values", HIDDEN_BUFS), [P, C * PACK], BF16)[:]
                    hidden(h_values, e - 1)
                    quantise(h_codes[e - 1][:], h_scales[e - 1][:], h_values)
            if e < E - 1:
                lin[e] = [first_layer_product(done[PASSES:], e, half) for half in halves]
        sigmoid_onto(half_values(raw[LAST_CHUNK][-1], 0), E - 1, 0)

        def place(number):
            return number % RAW_PLACES * RAW_BYTES

        def kept(name, columns, dtype):
            return keep.tile([P, columns], dtype, name=name, align_bytes=ALIGN)

        raw_groups = {}
        group_offsets = {
            (0, 0): place(8),
            (0, 2): place(8) + 8 * PIECE,
            (0, 4): place(9),
            (1, 0): place(9) + 4 * PIECE,
            (1, 2): place(10),
            (1, 4): place(10) + 8 * PIECE,
            (2, 0): place(11),
            (2, 2): place(11) + 8 * PIECE,
            (2, 4): place(0),
        }
        for number in range(PIECES):
            n, e = divmod(number, E)
            e0, e1 = PAIRS[e // 2]
            if e == e0:
                raw_groups[n, e0] = tile_at("pieces%d_%d" % (n, e0), group_offsets[n, e0], (e1 - e0) * PIECE)
            nc.sync.dma_start(
                raw_groups[n, e0][:, (e - e0) * PIECE : (e - e0 + 1) * PIECE].rearrange("p (j c) -> p j c", j=PACK),
                w2[e, :, n * P : (n + 1) * P].rearrange("(p j) c -> p j c", j=PACK),
            )
            if number == LISTS_AFTER:
                for list_tile, source in zip(inverse_lists, (pos1, pos2)):
                    nc.sync.dma_start(list_tile[:], source)

        y = [kept("y%d" % n, S, F32) for n in range(N_TILES)]
        terms, groups, rounded_groups = {}, {}, {}
        rounded_places = (place(1), place(1) + RAW_BYTES // 2)

        def round_group(n, e0, e1, offset):
            room = 3 * PIECE if (n, e0) == (2, 4) else (e1 - e0) * PIECE
            rounded = tile_at("w2_rounded%d_%d" % (n, e0), offset, room, BF16)[:, : (e1 - e0) * PIECE]
            dst = rounded.rearrange("p (e c i j) -> p e c j i", e=e1 - e0, i=2, j=PACK)
            src = raw_groups[n, e0][:].rearrange("p (e j c i) -> p e c j i", e=e1 - e0, i=2, j=PACK)
            if n == 0:
                for e in range(e0, e1):
                    copy = nc.vector.tensor_copy if e < 2 else nc.scalar.copy
                    copy(dst[:, e - e0], src[:, e - e0])
                    if e == E // 2:
                        sigmoid_onto(raw_groups[n, e0][:, :PIECE], E - 1, 1)
            else:
                nc.vector.tensor_copy(dst, src)
            rounded_groups[n, e0] = rounded

        def quantise_group(n, e0, e1):
            if n > 0 and e1 == E:
                codes = tile_at("w2_codes%d_%d" % (n, e0), place(2) + (n - 1) * RAW_BYTES // 2, (e1 - e0) * P, U32)
            else:
                codes = kept("w2_codes%d_%d" % (n, e0), (e1 - e0) * P, U32)
            scales = kept("w2_scales%d_%d" % (n, e0), (e1 - e0) * P, U8)
            quantise(codes[:], scales[:], rounded_groups[n, e0])
            groups[n, e0] = (codes, scales)

        def slot_results(n, e0, e1, slots):
            bank = bank_on(next_tag("bank", BANKS))
            width = slots.stop - slots.start
            for e in range(e0, e1):
                nc.tensor.matmul_mx(
                    out=bank[:, (e - e0) * width : (e - e0 + 1) * width],
                    lhsT=token_block(groups[n, e0][0], e - e0).bitcast(FP8X4),
                    lhsT_scale=token_block(groups[n, e0][1], e - e0),
                    rhs=h_codes[e][:, slots].bitcast(FP8X4),
                    rhs_scale=h_scales[e][:, slots],
                    start=True,
                    stop=True,
                )
            first_slot = e0 * C + slots.start
            nc.scalar.copy(y[n][:, first_slot : first_slot + (e1 - e0) * width], bank[:, : (e1 - e0) * width])

        def fetched(n, r, cols):
            offsets = entries(inverse_lists[r], cols.start, cols.stop)
            nc.scalar.activation(terms[n, r][:, cols], y[n][:].indirect(offsets), COPY)

        def gated_from_psum(n, r, cols, product=None):
            fetched_term = terms[n, r]
            if product is not None:
                terms[n, r] = product
            if cols.start < BANK:
                low = slice(cols.start, min(cols.stop, BANK))
                nc.vector.tensor_tensor(terms[n, r][:, low], psum_gates[r][0][:, low], fetched_term[:, low], MULT)
            if cols.stop > BANK:
                nc.vector.tensor_tensor(terms[n, r][:, BANK:], psum_gates[r][1], fetched_term[:, BANK:], MULT)

        def fetched_gated(n, r, cols):
            offsets = entries(inverse_lists[r], cols.start, cols.stop)
            nc.vector.tensor_tensor(terms[n, r][:, cols], y[n][:].indirect(offsets), second_gate[:, cols], MULT)

        def stored(n, cols):
            first, second = terms[n, 0], terms[n, 1]
            nc.vector.tensor_tensor(first[:, cols], first[:, cols], second[:, cols], ADD)
            nc.sync.dma_start(out[n * P : (n + 1) * P, cols], first[:, cols])

        all_slots = slice(0, C)
        tokens = slice(0, T)
        last_parts = cuts(LAST_CUTS)
        for number, (e0, e1) in enumerate(PAIRS):
            round_group(0, e0, e1, place(5) + number * 4 * PIECE)
        h_values = tile_at("h_last", rounded_places[1], C * PACK, BF16)
        hidden(h_values, E - 1)
        for half in halves:
            slots = half_slots(half)
            quantise(h_codes[E - 1][:, slots], h_scales[E - 1][:, slots], half_values(h_values, half))
        for e0, e1 in PAIRS:
            quantise_group(0, e0, e1)
        for e0, e1 in PAIRS[:-1]:
            slot_results(0, e0, e1, all_slots)
        for half in halves:
            slot_results(0, E - 1, E, half_slots(half))
        for key in ((0, 0), (1, 1), (2, 0), (2, 1)):
            terms[key] = kept("term%d_%d" % key, T, F32)
        fetched(0, 0, tokens)
        turn = 1
        for n in (1, 2):
            for e0, e1 in PAIRS:
                round_group(n, e0, e1, rounded_places[turn % 2])
                turn = turn + 1
                quantise_group(n, e0, e1)
                slot_results(n, e0, e1, all_slots)
                if (n, e0) == (2, 0):
                    gated_from_psum(0, 0, tokens, tile_at("product0_0", group_offsets[2, 0], T))
            if n == 1:
                terms[1, 0] = kept("term1_0", T, F32)
                fetched(1, 0, tokens)
        first_half, second_half = cuts((0, BANK, T))
        late = tile_at("term1_1_late", place(2) + RAW_BYTES // 2 + ALIGN, T)
        offsets = entries(inverse_lists[1], second_half.start, second_half.stop)
        nc.scalar.activation(late[:, second_half], y[1][:].indirect(offsets), COPY)
        for cols in last_parts:
            fetched(2, 0, cols)
            fetched(2, 1, cols)
        terms[0, 1] = tile_at("term0_1", rounded_places[0] - 4 * T + ALIGN, T)
        terms[1, 1] = tile_at("term1_1", rounded_places[0] + ALIGN, T)
        fetched_gated(0, 1, tokens)
        fetched_gated(1, 1, first_half)
        total = tile_at("total0", RAW_PLACES * RAW_BYTES, T)
        nc.gpsimd.tensor_tensor(total[:], terms[0, 0][:], terms[0, 1][:], ADD)
        nc.sync.dma_start(out[0:P, :], total[:])
        gated_from_psum(1, 0, tokens, tile_at("product1_0", rounded_places[0] + ALIGN + 4 * T, T))
        product = terms[1, 1]
        terms[1, 1] = late
        gated_from_psum(1, 1, second_half, product)
        for r in range(2):
            gated_from_psum(2, r, last_parts[0])
        stored(1, tokens)
        for cols in last_parts:
            if cols.start > 0:
                for r in range(2):
                    gated_from_psum(2, r, cols)
            stored(2, cols)
